import numpy as np
import ml_dtypes


def mxq(x, axis, fmt="e4m3"):
    dtype, down = {"e4m3": (ml_dtypes.float8_e4m3fn, 7), "e5m2": (ml_dtypes.float8_e5m2, 14)}[fmt]
    v = np.moveaxis(np.asarray(x, np.float32).astype(ml_dtypes.bfloat16).astype(np.float64), axis, -1)
    blocks = v.reshape(v.shape[:-1] + (-1, 32))
    amax = np.abs(blocks).max(-1, keepdims=True)
    byte = np.maximum(np.where(amax > 0, np.frexp(amax)[1] - 1 + 127, 0) - down, 1)
    scale = np.exp2(byte - 127.0)
    codes = (blocks / scale).astype(np.float32).astype(dtype).astype(np.float64)
    return np.moveaxis((codes * scale).reshape(v.shape), -1, axis)


WIDE = False


def mx_kscale(k):
    if not WIDE:
        return np.ones(k)
    levels = np.array([10, -10, 5, -5, 0])
    if k % 512:
        return np.exp2(np.random.permutation(np.resize(levels, k // 32))).repeat(32)
    a = np.empty((k // 512, 16))
    for p in range(k // 512):
        a[p, :8] = np.random.permutation(np.resize(levels, 8))
        for g in range(8):
            far = levels[np.abs(levels - a[p, g]) >= 10]
            a[p, g + 8] = far[np.random.randint(len(far))]
    return np.exp2(a.ravel()).repeat(32)


def f64(x):
    return np.asarray(x).astype(np.float64)


def striped(idx):
    return np.tile(idx.reshape(-1, 16).T, (8, 1)).astype(np.uint16)


def unstriped(offs):
    return offs[:16].T.reshape(-1).astype(np.int64)


E2M1 = np.array([0.0, 0.5, 1.0, 1.5, 2.0, 3.0, 4.0, 6.0, -0.0, -0.5, -1.0, -1.5, -2.0, -3.0, -4.0, -6.0])


def pack_weight(w, fmt):
    k, n = w.shape
    w = f64(np.asarray(w, np.float32).astype(ml_dtypes.bfloat16)).reshape(k // 32, 32, n)
    amax = np.abs(w).max(1)
    if fmt == "e4m3":
        byte = np.frexp(amax)[1] - 1 + 127 - 7
    else:
        mant, ex = np.frexp(amax / 6.0)
        byte = np.where(mant > 0.5, ex, ex - 1) + 127
    byte = np.clip(np.where(amax > 0, byte, 1), 1, 254)
    scaled = (w * np.exp2(127.0 - byte)[:, None, :]).reshape(k, n).astype(np.float32)
    by_word = np.ascontiguousarray(scaled.reshape(k // 512, 128, 4, n).transpose(0, 1, 3, 2))
    if fmt == "e4m3":
        words = by_word.astype(ml_dtypes.float8_e4m3fn).view(np.uint8)
    else:
        c = by_word.astype(ml_dtypes.float4_e2m1fn).view(np.uint8) & 0xF
        words = (c[..., 0::2] | (c[..., 1::2] << 4)).reshape(k // 512, 128, 2 * n)
    return np.ascontiguousarray(words), np.ascontiguousarray(byte.astype(np.uint8).reshape(k // 512, 16, n))


def unpack_weight(words, scales, fmt):
    g, _, n = scales.shape
    words = np.ascontiguousarray(words).reshape(g, 128, n, -1)
    if fmt == "e4m3":
        vals = words.view(ml_dtypes.float8_e4m3fn).astype(np.float64)
    else:
        nib = np.empty((g, 128, n, 4), np.uint8)
        nib[..., 0::2] = words & 0xF
        nib[..., 1::2] = words >> 4
        vals = E2M1[nib]
    vals = vals * np.repeat(np.exp2(scales.astype(np.float64) - 127.0), 8, axis=1)[..., None]
    return vals.transpose(0, 1, 3, 2).reshape(g * 512, n)


def relu2(v):
    return np.maximum(v, 0.0) ** 2


K, T, E, C, H, N = 2048, 512, 4, 256, 512, 384


def by_expert(wq, xq):
    return np.concatenate([wq[e].T @ xq[:, e * C:(e + 1) * C] for e in range(E)], axis=1)


def setup_inputs():
    n = np.random.standard_normal
    s = mx_kscale(K)[:, None]
    u = mx_kscale(H)
    first = np.random.permutation(np.repeat(np.arange(E), T // E))
    second = (first + 1 + np.random.permutation(np.repeat(np.arange(E - 1), -(-T // (E - 1)))[:T])) % E
    while np.bincount(second, minlength=E).max() != T // E:
        load = np.bincount(second, minlength=E); hi, lo = int(load.argmax()), int(load.argmin())
        t = np.flatnonzero((second == hi) & (first != lo))[0]; second[t] = lo
    slot_token = np.empty(E * C, np.int64); pos = np.empty((2, T), np.int64); fill = np.zeros(E, np.int64)
    place = np.stack([np.random.permutation(C) for _ in range(E)])
    for r, deal in enumerate((first, second)):
        for t in np.random.permutation(T):
            e = deal[t]; j = e * C + place[e, fill[e]]; fill[e] += 1; slot_token[j] = t; pos[r, t] = j
    g = np.random.uniform(0.2, 0.8, T)
    w1 = [pack_weight(m, "e2m1") for m in n((E, K, H)) / np.sqrt(K) / s[None] * u[None, None, :]]
    w2 = [pack_weight(m, "e2m1") for m in n((E, H, N)) / np.sqrt(H) / u[None, :, None] ** 2]
    return {
        "xT": (n((K, T)) * s).astype(np.float32),
        "w1_words": np.stack([m[0] for m in w1]),
        "w1_scales": np.stack([m[1] for m in w1]),
        "w2_words": np.stack([m[0] for m in w2]),
        "w2_scales": np.stack([m[1] for m in w2]),
        "gate": np.stack([np.tile(g, (N, 1)), np.tile(1.0 - g, (N, 1))]).astype(np.float32),
        "offs": striped(slot_token),
        "pos1": striped(pos[0]),
        "pos2": striped(pos[1]),
    }


def reference(xT, w1_words, w1_scales, w2_words, w2_scales, gate, offs, pos1, pos2):
    idx = unstriped(offs)
    w1 = np.stack([unpack_weight(w1_words[e], w1_scales[e], "e2m1") for e in range(E)])
    w2 = np.stack([unpack_weight(w2_words[e], w2_scales[e], "e2m1") for e in range(E)])
    xq = mxq(f64(xT)[:, idx], 0, "e4m3")
    h = relu2(by_expert(w1, xq))
    y = by_expert(w2, mxq(h, 0, "e4m3"))
    return f64(gate[0]) * y[:, unstriped(pos1)] + f64(gate[1]) * y[:, unstriped(pos2)]

@@ -1,0 +1,288 @@
+from contextlib import ExitStack
+
+import concourse.mybir as mybir
+from concourse.masks import make_identity
+
+K, T, E, C, H, N = 2048, 512, 4, 256, 512, 384
+P = 128
+PASSES = K // 512
+SLOTS = E * C
+FLOPS = 2 * SLOTS * (K * H + H * N)
+
+F32 = mybir.dt.float32
+BF16 = mybir.dt.bfloat16
+I32 = mybir.dt.int32
+U32 = mybir.dt.uint32
+U16 = mybir.dt.uint16
+U8 = mybir.dt.uint8
+FP8X4 = mybir.dt.float8_e4m3fn_x4
+FP4X4 = mybir.dt.float4_e2m1fn_x4
+RELU = mybir.ActivationFunctionType.Relu
+SQUARE = mybir.ActivationFunctionType.Square
+MULT = mybir.AluOpType.mult
+ADD = mybir.AluOpType.add
+
+
+def tile_moe_pln_mlp_relu2_kernel(
+    tc, xT, w1_words, w1_scales, w2_words, w2_scales, gate, offs, pos1, pos2, out
+):
+    nc = tc.nc
+    with ExitStack() as ctx:
+        lists = ctx.enter_context(tc.tile_pool(name="lists", bufs=1))
+        keep = ctx.enter_context(tc.tile_pool(name="keep", bufs=1))
+        work = ctx.enter_context(tc.tile_pool(name="work", bufs=4))
+        psum = ctx.enter_context(tc.psum_pool(name="psum", bufs=4))
+        aux = ctx.enter_context(tc.psum_pool(name="aux", bufs=4))
+
+        def hold(shape, dtype, name, tag=None):
+            return keep.tile(shape, dtype, name=name, tag=tag or name, align_bytes=64)
+
+        offs_t = lists.tile([P, SLOTS // 16], U16, name="offs_t")
+        pos1_t = lists.tile([P, T // 16], U16, name="pos1_t")
+        pos2_t = lists.tile([P, T // 16], U16, name="pos2_t")
+
+        xT_v = xT.rearrange("(s p j) t -> s p j t", p=P, j=4)
+        w1w_v = w1_words.bitcast(I32)
+        w1s_v = w1_scales.bitcast(I32)
+        w2w_v = w2_words.bitcast(I32)
+        w2s_v = w2_scales.bitcast(I32)
+
+        half = T // 2
+        raw = {}
+        for i in range(2):
+            raw[0, i] = hold([P, 4, half], F32, "raw0%d" % i)
+        for s in range(1, PASSES):
+            raw[s, 0] = hold([P, 4, T], F32, "raw%d" % s)
+        xb = [hold([P, T, 4], BF16, "xb%d" % s) for s in range(PASSES)]
+        xw = hold([P, PASSES * T], U32, "xw")
+        xs = hold([P, 2 * T], U8, "xs")
+        gw = {}
+        gs = [hold([P, SLOTS], U8, "gs%d" % h) for h in range(2)]
+        gp = [hold([P, SLOTS], U8, "gp%d" % h) for h in range(2)]
+        w1s = hold([P, E * PASSES * H], U8, "w1s")
+        w1w = {}
+        hw = hold([P, SLOTS], U32, "hw")
+        hs = hold([P, SLOTS], U8, "hs")
+        y = [hold([P, SLOTS], F32, "y%d" % j) for j in range(N // P)]
+        ident = hold([P, P], F32, "ident")
+
+        def load_x(s, i=0):
+            lo = i * half
+            n = half if s == 0 else T
+            nc.sync.dma_start(out=raw[s, i][:], in_=xT_v[s][:, :, lo : lo + n])
+
+        def load_w1(e, tag=None):
+            w1w[e] = hold([P, PASSES * 2 * H], U8, "w1w%d" % e, tag)
+            nc.sync.dma_start(
+                out=w1w[e][:].bitcast(I32).rearrange("p (s b) -> p s b", s=PASSES),
+                in_=w1w_v[e].rearrange("s p b -> p s b"),
+            )
+
+        def load_w1_scales():
+            for q in range(4):
+                nc.gpsimd.dma_start(
+                    out=w1s[32 * q : 32 * q + 4, :].bitcast(I32).rearrange("p (a b) -> p a b", b=H // 4),
+                    in_=w1s_v[:, :, 4 * q : 4 * q + 4, :].rearrange("e s r b -> r (e s) b"),
+                )
+
+        nc.sync.dma_start(offs_t[:], offs)
+        nc.vector.memset(w1s[:].bitcast(I32), 0)
+
+        nc.gpsimd.memset(xs[:], 0)
+        for h in range(2):
+            nc.gpsimd.memset(gp[h][:].bitcast(I32), 0)
+        make_identity(nc, ident[:])
+        load_x(0, 0)
+        load_x(0, 1)
+        load_w1_scales()
+        w2s = hold([P, E * N], U8, "w2s")
+        nc.vector.memset(w2s[:].bitcast(I32), 0)
+        for q in range(4):
+            nc.gpsimd.dma_start(
+                out=w2s[32 * q : 32 * q + 4, :].bitcast(I32).rearrange("p (a b) -> p a b", b=N // 4),
+                in_=w2s_v[:, 0, 4 * q : 4 * q + 4, :].rearrange("e r b -> r e b"),
+            )
+        load_x(1)
+        load_x(2)
+        load_x(3)
+        load_w1(0)
+
+        def cast(s, lo, hi, engine):
+            if hi > lo:
+                i, base = (lo // half, lo // half * half) if s == 0 else (0, 0)
+                dst = xb[s][:, lo:hi, :].rearrange("p (c i) t -> p c t i", i=4)
+                src = raw[s, i][:, :, lo - base : hi - base].rearrange("p t (c i) -> p c t i", i=4)
+                if engine == "v":
+                    nc.vector.tensor_copy(dst, src)
+                else:
+                    nc.scalar.copy(dst, src)
+
+        def quantise(s, lo, hi):
+            nc.vector.quantize_mx(
+                out=xw[:, s * T + lo : s * T + hi].bitcast(FP8X4),
+                scales=xs[4 * (s % 2) : P, s // 2 * T + lo : s // 2 * T + hi],
+                in_=xb[s][:, lo:hi, :].rearrange("p c t -> p (c t)"),
+            )
+
+        def words(s, experts, reach=1, tag=None):
+            n = len(experts) * C
+            lo = experts[0] * C // 16
+            codes = hold([P, n], U32, "gw%d%d" % (s, experts[0]), tag)
+            nc.vector.tensor_copy(codes[:], xw[:, s * T : (s + reach) * T].indirect(offs_t[:, lo : lo + n // 16]))
+            for i, e in enumerate(experts):
+                gw[s, e] = codes[:, i * C : (i + 1) * C]
+
+        def scales(h, experts, reach=1):
+            n = len(experts) * C
+            lo = experts[0] * C
+            nc.vector.tensor_copy(
+                gs[h][:, lo : lo + n], xs[:, h * T : (h + reach) * T].indirect(offs_t[:, lo // 16 : (lo + n) // 16])
+            )
+
+        def unpack(h, experts):
+            cols = slice(experts[0] * C, (experts[-1] + 1) * C)
+            for q in range(4):
+                nc.sync.dma_start(
+                    out=gp[h][32 * q : 32 * q + 4, cols].bitcast(I32),
+                    in_=gs[h][32 * q + 4 : 32 * q + 8, cols].bitcast(I32),
+                )
+
+        acc = {}
+
+        def first(s, b):
+            e = b // 2
+            if s == 0:
+                acc[b] = psum.tile([P, H], F32, name="bank")
+            lo = b % 2 * P
+            nc.tensor.matmul_mx(
+                out=acc[b][:],
+                lhsT=gw[s, e][:, lo : lo + P].bitcast(FP8X4),
+                lhsT_scale=(gs, gp)[s % 2][s // 2][:, b * P : (b + 1) * P],
+                rhs=w1w[e][:, s * 2 * H : (s + 1) * 2 * H].bitcast(FP4X4),
+                rhs_scale=w1s[:, (e * PASSES + s) * H : (e * PASSES + s + 1) * H],
+                start=(s == 0),
+                stop=(s == PASSES - 1),
+            )
+
+        def hidden(b, engine):
+            r = work.tile([P, 4, P], F32, name="r", align_bytes=64)
+            lanes = acc[b][:].rearrange("p (m t) -> p t m", t=4)
+            if engine == "v":
+                nc.vector.tensor_scalar_max(r[:], lanes, 0.0)
+            else:
+                nc.scalar.activation(r[:], lanes, RELU)
+            turned = aux.tile([P, 4, P], F32, name="aux")
+            for t in range(4):
+                nc.tensor.transpose(turned[:, t, :], r[:, t, :], ident[:])
+            hb = hold([P, P, 4], BF16, "hb%d" % b)
+            nc.scalar.activation(hb[:], turned[:].rearrange("p t n -> p n t"), SQUARE)
+            nc.vector.quantize_mx(
+                out=hw[:, b * P : (b + 1) * P].bitcast(FP8X4),
+                scales=hs[:, b * P : (b + 1) * P],
+                in_=hb[:].rearrange("p n t -> p (n t)"),
+            )
+
+        def result(experts, j, engine):
+            n = len(experts) * C
+            bank = aux.tile([P, H], F32, name="aux")
+            for i, e in enumerate(experts):
+                w = e * N + j * P
+                nc.tensor.matmul_mx(
+                    out=bank[:, i * C : (i + 1) * C],
+                    lhsT=w2w[:, 2 * w : 2 * (w + P)].bitcast(FP4X4),
+                    lhsT_scale=w2s[:, w : w + P],
+                    rhs=hw[:, e * C : (e + 1) * C].bitcast(FP8X4),
+                    rhs_scale=hs[:, e * C : (e + 1) * C],
+                    start=True,
+                    stop=True,
+                )
+            lo = experts[0] * C
+            if engine == "v":
+                nc.vector.tensor_copy(y[j][:, lo : lo + n], bank[:, 0:n])
+            else:
+                nc.scalar.copy(y[j][:, lo : lo + n], bank[:, 0:n])
+
+        for i, v in enumerate((128, 64)):
+            cast(0, i * half, i * half + v, "v")
+            cast(0, i * half + v, (i + 1) * half, "s")
+            quantise(0, i * half, (i + 1) * half)
+        for e in range(4):
+            words(0, (e,))
+        cast(1, 0, 128, "v")
+        cast(1, 128, T, "s")
+        quantise(1, 0, T)
+        load_w1(1, "raw1")
+        for e in (0, 1):
+            scales(0, (e,))
+            pass
+        unpack(0, (0, 1))
+        for e in (0, 1):
+            words(1, (e,))
+            for b in (2 * e, 2 * e + 1):
+                first(0, b)
+                first(1, b)
+        cast(2, 0, 0, "v")
+        cast(2, 0, T, "s")
+        quantise(2, 0, T)
+        for e in (0, 1):
+            words(2, (e,), 1)
+        load_w1(2, "raw2")
+        cast(3, 0, 192, "v")
+        cast(3, 192, T, "s")
+        quantise(3, 0, T)
+        for e in (0, 1):
+            scales(1, (e,))
+            unpack(1, (e,))
+            words(3, (e,))
+            for b in (2 * e, 2 * e + 1):
+                first(2, b)
+        load_w1(3, "raw3")
+        scales(0, (2, 3), 2)
+        unpack(0, (2, 3))
+        scales(1, (2,))
+        scales(1, (3,))
+        unpack(1, (2, 3))
+        for e in (2, 3):
+            for s in range(1, PASSES):
+                words(s, (e,), PASSES - s)
+        g = hold([P, N // P, 2, T], F32, "g", "xs")
+        for j in range(N // P):
+            nc.sync.dma_start(out=g[:, j], in_=gate[:, j * P : (j + 1) * P, :].rearrange("g p t -> p g t"))
+        for b in range(4):
+            first(3, b)
+            hidden(b, "ssssssss"[b])
+        w2w = hold([P, E * 2 * N], U8, "w2w", "xb3")
+        nc.sync.dma_start(
+            out=w2w[:].bitcast(I32).rearrange("p (e b) -> p e b", e=E),
+            in_=w2w_v[:, 0].rearrange("e p b -> p e b"),
+        )
+        nc.sync.dma_start(pos1_t[:], pos1)
+        nc.sync.dma_start(pos2_t[:], pos2)
+        for b in (4, 5):
+            for s in range(PASSES):
+                first(s, b)
+            hidden(b, "ssssssss"[b])
+        for b in (6, 7):
+            for s in range(PASSES):
+                first(s, b)
+        for j in range(N // P):
+            result((0, 1), j, "vvv"[j])
+        for b in (6, 7):
+            hidden(b, "ssssssss"[b])
+
+        for j in range(N // P):
+            result((2,), j, "sss"[j])
+        for j in range(N // P):
+            result((3,), j, "vss"[j])
+
+        for j in range(N // P):
+            for lo, hi in ((0, T),) if j < 2 else ((0, T // 2), (T // 2, T)):
+                a = work.tile([P, T], F32, name="a")
+                b = work.tile([P, T], F32, name="b")
+                o = work.tile([P, T], F32, name="o")
+                n = slice(0, hi - lo)
+                cols = slice(lo // 16, hi // 16)
+                nc.vector.tensor_tensor(a[:, n], y[j][:].indirect(pos1_t[:, cols]), g[:, j, 0, lo:hi], MULT)
+                nc.vector.tensor_tensor(b[:, n], y[j][:].indirect(pos2_t[:, cols]), g[:, j, 1, lo:hi], MULT)
+                nc.vector.tensor_tensor(o[:, n], a[:, n], b[:, n], ADD)
+                nc.sync.dma_start(out=out[j * P : (j + 1) * P, lo:hi], in_=o[:, n])

@@ -7,6 +7,7 @@ K, T, E, C, H, N = 2048, 512, 4, 256, 512, 384
 P = 128
 PASSES = K // 512
 SLOTS = E * C
+LIFT = (0, 4, 4, 0)
 FLOPS = 2 * SLOTS * (K * H + H * N)
 
 F32 = mybir.dt.float32
@@ -31,11 +32,13 @@ def tile_moe_pln_mlp_relu2_kernel(
         lists = ctx.enter_context(tc.tile_pool(name="lists", bufs=1))
         keep = ctx.enter_context(tc.tile_pool(name="keep", bufs=1))
         work = ctx.enter_context(tc.tile_pool(name="work", bufs=4))
-        psum = ctx.enter_context(tc.psum_pool(name="psum", bufs=4))
-        aux = ctx.enter_context(tc.psum_pool(name="aux", bufs=4))
+        psum = ctx.enter_context(tc.psum_pool(name="psum", bufs=1))
 
         def hold(shape, dtype, name, tag=None):
             return keep.tile(shape, dtype, name=name, tag=tag or name, align_bytes=64)
+
+        def bank(b):
+            return psum.tile([P, H], F32, name="bank%d" % b)
 
         offs_t = lists.tile([P, SLOTS // 16], U16, name="offs_t")
         pos1_t = lists.tile([P, T // 16], U16, name="pos1_t")
@@ -59,7 +62,7 @@ def tile_moe_pln_mlp_relu2_kernel(
         gw = {}
         gs = [hold([P, SLOTS], U8, "gs%d" % h) for h in range(2)]
         gp = [hold([P, SLOTS], U8, "gp%d" % h) for h in range(2)]
-        w1s = hold([P, E * PASSES * H], U8, "w1s")
+        w1s = [hold([P, 2 * PASSES * H], U8, "w1s%d" % i) for i in range(2)]
         w1w = {}
         hw = hold([P, SLOTS], U32, "hw")
         hs = hold([P, SLOTS], U8, "hs")
@@ -78,49 +81,33 @@ def tile_moe_pln_mlp_relu2_kernel(
                 in_=w1w_v[e].rearrange("s p b -> p s b"),
             )
 
-        def load_w1_scales():
-            for q in range(4):
-                nc.gpsimd.dma_start(
-                    out=w1s[32 * q : 32 * q + 4, :].bitcast(I32).rearrange("p (a b) -> p a b", b=H // 4),
-                    in_=w1s_v[:, :, 4 * q : 4 * q + 4, :].rearrange("e s r b -> r (e s) b"),
+        def load_w1_scales(i, queue):
+            for r in range(4):
+                queue.dma_start(
+                    out=w1s[i][r:P:32, :].bitcast(I32).rearrange("p (a b) -> p a b", b=H // 4),
+                    in_=w1s_v[2 * i : 2 * i + 2, :, r:16:4, :].rearrange("e s q b -> q (e s) b"),
                 )
 
-        nc.sync.dma_start(offs_t[:], offs)
-        nc.vector.memset(w1s[:].bitcast(I32), 0)
-
-        nc.gpsimd.memset(xs[:], 0)
-        for h in range(2):
-            nc.gpsimd.memset(gp[h][:].bitcast(I32), 0)
-        make_identity(nc, ident[:])
-        load_x(0, 0)
-        load_x(0, 1)
-        load_w1_scales()
-        w2s = hold([P, E * N], U8, "w2s")
-        nc.vector.memset(w2s[:].bitcast(I32), 0)
-        for q in range(4):
-            nc.gpsimd.dma_start(
-                out=w2s[32 * q : 32 * q + 4, :].bitcast(I32).rearrange("p (a b) -> p a b", b=N // 4),
-                in_=w2s_v[:, 0, 4 * q : 4 * q + 4, :].rearrange("e r b -> r e b"),
-            )
-        load_x(1)
-        load_x(2)
-        load_x(3)
-        load_w1(0)
+        def load_w2_scales(queue):
+            for r in range(4):
+                queue.dma_start(
+                    out=w2s[r:P:32, :].bitcast(I32).rearrange("p (a b) -> p a b", b=N // 4),
+                    in_=w2s_v[:, 0, r:16:4, :].rearrange("e q b -> q e b"),
+                )
 
         def cast(s, lo, hi, engine):
-            if hi > lo:
-                i, base = (lo // half, lo // half * half) if s == 0 else (0, 0)
-                dst = xb[s][:, lo:hi, :].rearrange("p (c i) t -> p c t i", i=4)
-                src = raw[s, i][:, :, lo - base : hi - base].rearrange("p t (c i) -> p c t i", i=4)
-                if engine == "v":
-                    nc.vector.tensor_copy(dst, src)
-                else:
-                    nc.scalar.copy(dst, src)
+            i, base = (lo // half, lo // half * half) if s == 0 else (0, 0)
+            dst = xb[s][:, lo:hi, :].rearrange("p (c i) t -> p c t i", i=4)
+            src = raw[s, i][:, :, lo - base : hi - base].rearrange("p t (c i) -> p c t i", i=4)
+            if engine == "v":
+                nc.vector.tensor_copy(dst, src)
+            else:
+                nc.scalar.copy(dst, src)
 
         def quantise(s, lo, hi):
             nc.vector.quantize_mx(
                 out=xw[:, s * T + lo : s * T + hi].bitcast(FP8X4),
-                scales=xs[4 * (s % 2) : P, s // 2 * T + lo : s // 2 * T + hi],
+                scales=xs[LIFT[s] : P, s // 2 * T + lo : s // 2 * T + hi],
                 in_=xb[s][:, lo:hi, :].rearrange("p c t -> p (c t)"),
             )
 
@@ -139,56 +126,71 @@ def tile_moe_pln_mlp_relu2_kernel(
                 gs[h][:, lo : lo + n], xs[:, h * T : (h + reach) * T].indirect(offs_t[:, lo // 16 : (lo + n) // 16])
             )
 
-        def unpack(h, experts):
+        def unpack(h, experts, queue):
             cols = slice(experts[0] * C, (experts[-1] + 1) * C)
-            for q in range(4):
-                nc.sync.dma_start(
-                    out=gp[h][32 * q : 32 * q + 4, cols].bitcast(I32),
-                    in_=gs[h][32 * q + 4 : 32 * q + 8, cols].bitcast(I32),
-                )
+            queue.dma_start(out=gp[h][0:112, cols].bitcast(I32), in_=gs[h][4:116, cols].bitcast(I32))
+
+        def unpack4(h, experts, queue):
+            cols = slice(experts[0] * C, (experts[-1] + 1) * C)
+            for r in range(4):
+                queue.dma_start(out=gp[h][r:P:32, cols].bitcast(I32), in_=gs[h][4 + r : P : 32, cols].bitcast(I32))
 
         acc = {}
+        relu = {}
+        done = {}
 
         def first(s, b):
             e = b // 2
-            if s == 0:
-                acc[b] = psum.tile([P, H], F32, name="bank")
+            done[b] = done.get(b, 0) + 1
+            if done[b] == 1:
+                acc[b] = bank((0, 1, 2, 3, 6, 7, 0, 1)[b])
             lo = b % 2 * P
+            w = (e % 2 * PASSES + s) * H
             nc.tensor.matmul_mx(
                 out=acc[b][:],
                 lhsT=gw[s, e][:, lo : lo + P].bitcast(FP8X4),
-                lhsT_scale=(gs, gp)[s % 2][s // 2][:, b * P : (b + 1) * P],
+                lhsT_scale=(gp if LIFT[s] else gs)[s // 2][:, b * P : (b + 1) * P],
                 rhs=w1w[e][:, s * 2 * H : (s + 1) * 2 * H].bitcast(FP4X4),
-                rhs_scale=w1s[:, (e * PASSES + s) * H : (e * PASSES + s + 1) * H],
-                start=(s == 0),
-                stop=(s == PASSES - 1),
+                rhs_scale=w1s[e // 2][:, w : w + H],
+                start=(done[b] == 1),
+                stop=(done[b] == PASSES),
             )
 
-        def hidden(b, engine):
-            r = work.tile([P, 4, P], F32, name="r", align_bytes=64)
+        def rectify(b, engine):
+            relu[b] = hold([P, 4, P], F32, "r%d" % b)
             lanes = acc[b][:].rearrange("p (m t) -> p t m", t=4)
             if engine == "v":
-                nc.vector.tensor_scalar_max(r[:], lanes, 0.0)
+                nc.vector.tensor_scalar_max(relu[b][:], lanes, 0.0)
             else:
-                nc.scalar.activation(r[:], lanes, RELU)
-            turned = aux.tile([P, 4, P], F32, name="aux")
+                nc.scalar.activation(relu[b][:], lanes, RELU)
+
+        turned = {}
+
+        def turn(b):
+            turned[b] = bank((4, 5, 2, 3)[b % 4])
             for t in range(4):
-                nc.tensor.transpose(turned[:, t, :], r[:, t, :], ident[:])
-            hb = hold([P, P, 4], BF16, "hb%d" % b)
-            nc.scalar.activation(hb[:], turned[:].rearrange("p t n -> p n t"), SQUARE)
+                nc.tensor.transpose(turned[b][:, t * P : (t + 1) * P], relu[b][:, t, :], ident[:])
+
+        hb = {}
+
+        def square(b):
+            hb[b] = hold([P, P, 4], BF16, "hb%d" % b)
+            nc.scalar.activation(hb[b][:], turned[b][:].rearrange("p (t n) -> p n t", t=4), SQUARE)
+
+        def quantise_h(b, tag=None):
             nc.vector.quantize_mx(
                 out=hw[:, b * P : (b + 1) * P].bitcast(FP8X4),
                 scales=hs[:, b * P : (b + 1) * P],
-                in_=hb[:].rearrange("p n t -> p (n t)"),
+                in_=hb[b][:].rearrange("p n t -> p (n t)"),
             )
 
-        def result(experts, j, engine):
+        def result(experts, j, engine, b):
             n = len(experts) * C
-            bank = aux.tile([P, H], F32, name="aux")
-            for i, e in enumerate(experts):
+            sums = bank(b)
+            for i, e in reversed(list(enumerate(experts))):
                 w = e * N + j * P
                 nc.tensor.matmul_mx(
-                    out=bank[:, i * C : (i + 1) * C],
+                    out=sums[:, i * C : (i + 1) * C],
                     lhsT=w2w[:, 2 * w : 2 * (w + P)].bitcast(FP4X4),
                     lhsT_scale=w2s[:, w : w + P],
                     rhs=hw[:, e * C : (e + 1) * C].bitcast(FP8X4),
@@ -198,91 +200,145 @@ def tile_moe_pln_mlp_relu2_kernel(
                 )
             lo = experts[0] * C
             if engine == "v":
-                nc.vector.tensor_copy(y[j][:, lo : lo + n], bank[:, 0:n])
+                nc.vector.tensor_copy(y[j][:, lo : lo + n], sums[:, 0:n])
             else:
-                nc.scalar.copy(y[j][:, lo : lo + n], bank[:, 0:n])
+                nc.scalar.copy(y[j][:, lo : lo + n], sums[:, 0:n])
 
-        for i, v in enumerate((128, 64)):
+        def load_w2(tag):
+            w2w = hold([P, E * 2 * N], U8, "w2w", tag)
+            nc.sync.dma_start(
+                out=w2w[:].bitcast(I32).rearrange("p (e b) -> p e b", e=E),
+                in_=w2w_v[:, 0].rearrange("e p b -> p e b"),
+            )
+            return w2w
+
+        def load_gate(tag):
+            g = hold([P, 2, T], F32, "g", tag)
+            nc.sync.dma_start(out=g[:], in_=gate[:, 0:P, :].rearrange("g p t -> p g t"))
+            return g
+
+        def combine():
+            for j in range(N // P):
+                for lo, hi in ((0, T),) if j < 2 else ((0, T // 2), (T // 2, T)):
+                    a = work.tile([P, T], F32, name="a")
+                    b = work.tile([P, T], F32, name="b")
+                    o = work.tile([P, T], F32, name="o")
+                    n = slice(0, hi - lo)
+                    cols = slice(lo // 16, hi // 16)
+                    nc.vector.tensor_tensor(a[:, n], y[j][:].indirect(pos1_t[:, cols]), g[:, 0, lo:hi], MULT)
+                    nc.vector.tensor_tensor(b[:, n], y[j][:].indirect(pos2_t[:, cols]), g[:, 1, lo:hi], MULT)
+                    nc.vector.tensor_tensor(o[:, n], a[:, n], b[:, n], ADD)
+                    nc.sync.dma_start(out=out[j * P : (j + 1) * P, lo:hi], in_=o[:, n])
+
+        load_x(0, 0)
+        load_x(0, 1)
+        nc.sync.dma_start(offs_t[:], offs)
+        nc.vector.memset(w1s[0][:].bitcast(I32), 0)
+        nc.vector.memset(w1s[1][:].bitcast(I32), 0)
+        nc.gpsimd.memset(xs[:].bitcast(I32), 0)
+        for h in range(2):
+            nc.gpsimd.memset(gp[h][:].bitcast(I32), 0)
+        make_identity(nc, ident[:])
+        load_x(1)
+        load_x(2)
+        load_x(3)
+        load_w1_scales(0, nc.sync)
+        for i, v in enumerate((128, 128)):
             cast(0, i * half, i * half + v, "v")
             cast(0, i * half + v, (i + 1) * half, "s")
             quantise(0, i * half, (i + 1) * half)
-        for e in range(4):
+        load_w1(0, "raw00")
+        load_w1(1, "raw01")
+        load_w1_scales(1, nc.sync)
+        for e in range(3):
             words(0, (e,))
-        cast(1, 0, 128, "v")
-        cast(1, 128, T, "s")
+        cast(1, 0, 160, "v")
+        cast(1, 160, T, "s")
         quantise(1, 0, T)
-        load_w1(1, "raw1")
+        load_w1(2, "raw1")
         for e in (0, 1):
             scales(0, (e,))
-            pass
-        unpack(0, (0, 1))
+        unpack(0, (0, 1), nc.gpsimd)
         for e in (0, 1):
             words(1, (e,))
-            for b in (2 * e, 2 * e + 1):
-                first(0, b)
-                first(1, b)
-        cast(2, 0, 0, "v")
+        for e in (2, 3):
+            scales(0, (e,))
+        unpack(0, (2, 3), nc.gpsimd)
         cast(2, 0, T, "s")
         quantise(2, 0, T)
-        for e in (0, 1):
-            words(2, (e,), 1)
-        load_w1(2, "raw2")
-        cast(3, 0, 192, "v")
-        cast(3, 192, T, "s")
+        load_w1(3, "raw2")
+        cast(3, 0, T, "s")
         quantise(3, 0, T)
         for e in (0, 1):
             scales(1, (e,))
-            unpack(1, (e,))
-            words(3, (e,))
-            for b in (2 * e, 2 * e + 1):
-                first(2, b)
-        load_w1(3, "raw3")
-        scales(0, (2, 3), 2)
-        unpack(0, (2, 3))
+        unpack4(1, (0, 1), nc.scalar)
+        words(1, (2,), 3)
+        words(3, (0,))
+        words(2, (0,), 2)
+        words(2, (1,), 2)
+        words(3, (1,))
         scales(1, (2,))
         scales(1, (3,))
-        unpack(1, (2, 3))
-        for e in (2, 3):
-            for s in range(1, PASSES):
-                words(s, (e,), PASSES - s)
-        g = hold([P, N // P, 2, T], F32, "g", "xs")
-        for j in range(N // P):
-            nc.sync.dma_start(out=g[:, j], in_=gate[:, j * P : (j + 1) * P, :].rearrange("g p t -> p g t"))
-        for b in range(4):
-            first(3, b)
-            hidden(b, "ssssssss"[b])
-        w2w = hold([P, E * 2 * N], U8, "w2w", "xb3")
-        nc.sync.dma_start(
-            out=w2w[:].bitcast(I32).rearrange("p (e b) -> p e b", e=E),
-            in_=w2w_v[:, 0].rearrange("e p b -> p e b"),
-        )
+        unpack4(1, (2, 3), nc.sync)
+        for s in (0, 1):
+            words(s, (3,), PASSES - s)
+        w2s = hold([P, E * N], U8, "w2s", "gw30")
+        nc.gpsimd.memset(w2s[:].bitcast(I32), 0)
+        load_w2_scales(nc.sync)
+        w2w = load_w2("gw20")
+        g = load_gate("gw31")
+
+        def passes(e, which):
+            for s in which:
+                for b in (2 * e, 2 * e + 1):
+                    first(s, b)
+
+        passes(0, (0, 1))
+        passes(1, (0, 1))
+        passes(0, (3,))
+        passes(2, (0, 1))
+        passes(0, (2,))
+        rectify(0, "s")
+        rectify(1, "s")
+        passes(1, (2, 3))
+        turn(0)
+        turn(1)
+        rectify(2, "s")
+        rectify(3, "s")
+        square(0)
+        square(1)
+        turn(2)
+        turn(3)
+        square(2)
+        square(3)
+        words(3, (2,), 1, "r0")
+        words(2, (2,), 1, "r1")
+        words(2, (3,), 1, "r2")
+        words(3, (3,), 1, "r3")
+        passes(3, (0, 1))
+        passes(2, (3, 2))
+        rectify(4, "s")
+        rectify(5, "s")
+        turn(4)
+        turn(5)
+        square(4)
+        square(5)
+        for b in (6, 7):
+            for s in (2, 3):
+                first(s, b)
+            rectify(b, "v")
+        for b in range(6):
+            quantise_h(b)
+        result((0, 1), 0, "v", 6)
+        result((2,), 0, "v", 7)
+        for b in (6, 7):
+            turn(b)
+            square(b)
+            quantise_h(b)
         nc.sync.dma_start(pos1_t[:], pos1)
         nc.sync.dma_start(pos2_t[:], pos2)
-        for b in (4, 5):
-            for s in range(PASSES):
-                first(s, b)
-            hidden(b, "ssssssss"[b])
-        for b in (6, 7):
-            for s in range(PASSES):
-                first(s, b)
-        for j in range(N // P):
-            result((0, 1), j, "vvv"[j])
-        for b in (6, 7):
-            hidden(b, "ssssssss"[b])
-
-        for j in range(N // P):
-            result((2,), j, "sss"[j])
-        for j in range(N // P):
-            result((3,), j, "vss"[j])
-
-        for j in range(N // P):
-            for lo, hi in ((0, T),) if j < 2 else ((0, T // 2), (T // 2, T)):
-                a = work.tile([P, T], F32, name="a")
-                b = work.tile([P, T], F32, name="b")
-                o = work.tile([P, T], F32, name="o")
-                n = slice(0, hi - lo)
-                cols = slice(lo // 16, hi // 16)
-                nc.vector.tensor_tensor(a[:, n], y[j][:].indirect(pos1_t[:, cols]), g[:, j, 0, lo:hi], MULT)
-                nc.vector.tensor_tensor(b[:, n], y[j][:].indirect(pos2_t[:, cols]), g[:, j, 1, lo:hi], MULT)
-                nc.vector.tensor_tensor(o[:, n], a[:, n], b[:, n], ADD)
-                nc.sync.dma_start(out=out[j * P : (j + 1) * P, lo:hi], in_=o[:, n])
+        result((3,), 0, "v", 4)
+        for j in (1, 2):
+            result((0, 1), j, "s", 1 + j)
+            result((2, 3), j, "s", j - 1)
+        combine()

@@ -7,6 +7,7 @@ K, T, E, C, H, N = 2048, 512, 4, 256, 512, 384
 P = 128
 PASSES = K // 512
 SLOTS = E * C
+CUTS = (((0, 512),), ((0, 512),), ((0, 512),), ((0, 512),))
 LIFT = (0, 4, 4, 0)
 FLOPS = 2 * SLOTS * (K * H + H * N)
 
@@ -50,12 +51,10 @@ def tile_moe_pln_mlp_relu2_kernel(
         w2w_v = w2_words.bitcast(I32)
         w2s_v = w2_scales.bitcast(I32)
 
-        half = T // 2
         raw = {}
-        for i in range(2):
-            raw[0, i] = hold([P, 4, half], F32, "raw0%d" % i)
-        for s in range(1, PASSES):
-            raw[s, 0] = hold([P, 4, T], F32, "raw%d" % s)
+        for s in range(PASSES):
+            for lo, hi in CUTS[s]:
+                raw[s, lo] = hold([P, 4, hi - lo], F32, "raw%d_%d" % (s, lo))
         xb = [hold([P, T, 4], BF16, "xb%d" % s) for s in range(PASSES)]
         xw = hold([P, PASSES * T], U32, "xw")
         xs = hold([P, 2 * T], U8, "xs")
@@ -69,10 +68,9 @@ def tile_moe_pln_mlp_relu2_kernel(
         y = [hold([P, SLOTS], F32, "y%d" % j) for j in range(N // P)]
         ident = hold([P, P], F32, "ident")
 
-        def load_x(s, i=0):
-            lo = i * half
-            n = half if s == 0 else T
-            nc.sync.dma_start(out=raw[s, i][:], in_=xT_v[s][:, :, lo : lo + n])
+        def load_x(s):
+            for lo, hi in CUTS[s]:
+                nc.sync.dma_start(out=raw[s, lo][:], in_=xT_v[s][:, :, lo:hi])
 
         def load_w1(e, tag=None):
             w1w[e] = hold([P, PASSES * 2 * H], U8, "w1w%d" % e, tag)
@@ -96,9 +94,9 @@ def tile_moe_pln_mlp_relu2_kernel(
                 )
 
         def cast(s, lo, hi, engine):
-            i, base = (lo // half, lo // half * half) if s == 0 else (0, 0)
+            base = max(a for a, b in CUTS[s] if a <= lo)
             dst = xb[s][:, lo:hi, :].rearrange("p (c i) t -> p c t i", i=4)
-            src = raw[s, i][:, :, lo - base : hi - base].rearrange("p t (c i) -> p c t i", i=4)
+            src = raw[s, base][:, :, lo - base : hi - base].rearrange("p t (c i) -> p c t i", i=4)
             if engine == "v":
                 nc.vector.tensor_copy(dst, src)
             else:
@@ -230,8 +228,7 @@ def tile_moe_pln_mlp_relu2_kernel(
                     nc.vector.tensor_tensor(o[:, n], a[:, n], b[:, n], ADD)
                     nc.sync.dma_start(out=out[j * P : (j + 1) * P, lo:hi], in_=o[:, n])
 
-        load_x(0, 0)
-        load_x(0, 1)
+        load_x(0)
         nc.sync.dma_start(offs_t[:], offs)
         nc.vector.memset(w1s[0][:].bitcast(I32), 0)
         nc.vector.memset(w1s[1][:].bitcast(I32), 0)
@@ -242,20 +239,21 @@ def tile_moe_pln_mlp_relu2_kernel(
         load_x(1)
         load_x(2)
         load_x(3)
+        load_w1(0)
         load_w1_scales(0, nc.sync)
-        for i, v in enumerate((128, 128)):
-            cast(0, i * half, i * half + v, "v")
-            cast(0, i * half + v, (i + 1) * half, "s")
-            quantise(0, i * half, (i + 1) * half)
-        load_w1(0, "raw00")
-        load_w1(1, "raw01")
+        cast(0, 0, 320, "v")
+        cast(0, 320, T, "s")
+        quantise(0, 0, 256)
+        quantise(0, 256, T)
+        load_w1(1, "raw0_0")
         load_w1_scales(1, nc.sync)
+        load_w1(2, "xb0")
         for e in range(3):
             words(0, (e,))
-        cast(1, 0, 160, "v")
-        cast(1, 160, T, "s")
+        cast(1, 0, 128, "v")
+        cast(1, 128, T, "s")
         quantise(1, 0, T)
-        load_w1(2, "raw1")
+        load_w1(3, "raw1_0")
         for e in (0, 1):
             scales(0, (e,))
         unpack(0, (0, 1), nc.gpsimd)
@@ -266,79 +264,70 @@ def tile_moe_pln_mlp_relu2_kernel(
         unpack(0, (2, 3), nc.gpsimd)
         cast(2, 0, T, "s")
         quantise(2, 0, T)
-        load_w1(3, "raw2")
         cast(3, 0, T, "s")
         quantise(3, 0, T)
         for e in (0, 1):
             scales(1, (e,))
         unpack4(1, (0, 1), nc.scalar)
         words(1, (2,), 3)
-        words(3, (0,))
         words(2, (0,), 2)
+        words(3, (0,))
         words(2, (1,), 2)
         words(3, (1,))
         scales(1, (2,))
         scales(1, (3,))
         unpack4(1, (2, 3), nc.sync)
-        for s in (0, 1):
-            words(s, (3,), PASSES - s)
-        w2s = hold([P, E * N], U8, "w2s", "gw30")
+        w2s = hold([P, E * N], U8, "w2s", "xs")
         nc.gpsimd.memset(w2s[:].bitcast(I32), 0)
         load_w2_scales(nc.sync)
-        w2w = load_w2("gw20")
-        g = load_gate("gw31")
+        w2w = load_w2("gw12")
+        g = load_gate("gw02")
 
         def passes(e, which):
             for s in which:
                 for b in (2 * e, 2 * e + 1):
                     first(s, b)
 
-        passes(0, (0, 1))
-        passes(1, (0, 1))
-        passes(0, (3,))
-        passes(2, (0, 1))
-        passes(0, (2,))
-        rectify(0, "s")
-        rectify(1, "s")
-        passes(1, (2, 3))
-        turn(0)
-        turn(1)
-        rectify(2, "s")
-        rectify(3, "s")
-        square(0)
-        square(1)
-        turn(2)
-        turn(3)
-        square(2)
-        square(3)
-        words(3, (2,), 1, "r0")
-        words(2, (2,), 1, "r1")
-        words(2, (3,), 1, "r2")
-        words(3, (3,), 1, "r3")
-        passes(3, (0, 1))
-        passes(2, (3, 2))
+        def finish(e):
+            for b in (2 * e, 2 * e + 1):
+                for s in (2, 3):
+                    first(s, b)
+                rectify(b, "v" if e == 3 else "s")
+
+        def hidden(e):
+            for b in (2 * e, 2 * e + 1):
+                turn(b)
+                square(b)
+
+        for e in range(3):
+            passes(e, (0, 1))
+        finish(0)
+        finish(1)
+        hidden(0)
+        words(3, (2,), 1, "gw20")
+        words(0, (3,), 1, "gw30")
+        words(2, (2,), 1, "gw21")
+        words(1, (3,), 1, "gw31")
+        words(2, (3,), 1, "r0")
+        words(3, (3,), 1, "r1")
+        passes(2, (3,))
+        hidden(1)
+        passes(3, (0,))
+        passes(2, (2,))
         rectify(4, "s")
         rectify(5, "s")
-        turn(4)
-        turn(5)
-        square(4)
-        square(5)
-        for b in (6, 7):
-            for s in (2, 3):
-                first(s, b)
-            rectify(b, "v")
-        for b in range(6):
-            quantise_h(b)
-        result((0, 1), 0, "v", 6)
-        result((2,), 0, "v", 7)
-        for b in (6, 7):
-            turn(b)
-            square(b)
+        passes(3, (1,))
+        finish(3)
+        hidden(2)
+        hidden(3)
+        for b in range(8):
             quantise_h(b)
         nc.sync.dma_start(pos1_t[:], pos1)
         nc.sync.dma_start(pos2_t[:], pos2)
-        result((3,), 0, "v", 4)
+        result((0, 1), 0, "v", 4)
+        result((2,), 0, "v", 5)
+        result((3,), 0, "v", 0)
         for j in (1, 2):
-            result((0, 1), j, "s", 1 + j)
-            result((2, 3), j, "s", j - 1)
+            result((0, 1), j, "s", 5 + j)
+            result((2, 3), j, "s", j)
         combine()

@@ -8,6 +8,7 @@ P = 128
 PASSES = K // 512
 SLOTS = E * C
 CUTS = (((0, 512),), ((0, 512),), ((0, 512),), ((0, 512),))
+SPARE = 192
 LIFT = (0, 4, 4, 0)
 FLOPS = 2 * SLOTS * (K * H + H * N)
 
@@ -56,8 +57,8 @@ def tile_moe_pln_mlp_relu2_kernel(
             for lo, hi in CUTS[s]:
                 raw[s, lo] = hold([P, 4, hi - lo], F32, "raw%d_%d" % (s, lo))
         xb = [hold([P, T, 4], BF16, "xb%d" % s) for s in range(PASSES)]
-        xw = hold([P, PASSES * T], U32, "xw")
-        xs = hold([P, 2 * T], U8, "xs")
+        xw = hold([P, PASSES * T + SPARE], U32, "xw")
+        xs = hold([P, 3 * T], U8, "xs")
         gw = {}
         gs = [hold([P, SLOTS], U8, "gs%d" % h) for h in range(2)]
         gp = [hold([P, SLOTS], U8, "gp%d" % h) for h in range(2)]
@@ -72,11 +73,11 @@ def tile_moe_pln_mlp_relu2_kernel(
             for lo, hi in CUTS[s]:
                 nc.sync.dma_start(out=raw[s, lo][:], in_=xT_v[s][:, :, lo:hi])
 
-        def load_w1(e, tag=None):
-            w1w[e] = hold([P, PASSES * 2 * H], U8, "w1w%d" % e, tag)
+        def load_w1(s, tag=None):
+            w1w[s] = hold([P, E * 2 * H], U8, "w1w%d" % s, tag)
             nc.sync.dma_start(
-                out=w1w[e][:].bitcast(I32).rearrange("p (s b) -> p s b", s=PASSES),
-                in_=w1w_v[e].rearrange("s p b -> p s b"),
+                out=w1w[s][:].bitcast(I32).rearrange("p (e b) -> p e b", e=E),
+                in_=w1w_v[:, s].rearrange("e p b -> p e b"),
             )
 
         def load_w1_scales(i, queue):
@@ -109,19 +110,19 @@ def tile_moe_pln_mlp_relu2_kernel(
                 in_=xb[s][:, lo:hi, :].rearrange("p c t -> p (c t)"),
             )
 
-        def words(s, experts, reach=1, tag=None):
+        def words(s, experts, reach=T, tag=None):
             n = len(experts) * C
             lo = experts[0] * C // 16
             codes = hold([P, n], U32, "gw%d%d" % (s, experts[0]), tag)
-            nc.vector.tensor_copy(codes[:], xw[:, s * T : (s + reach) * T].indirect(offs_t[:, lo : lo + n // 16]))
+            nc.vector.tensor_copy(codes[:], xw[:, s * T : s * T + reach].indirect(offs_t[:, lo : lo + n // 16]))
             for i, e in enumerate(experts):
                 gw[s, e] = codes[:, i * C : (i + 1) * C]
 
-        def scales(h, experts, reach=1):
+        def scales(h, experts, reach=T):
             n = len(experts) * C
             lo = experts[0] * C
             nc.vector.tensor_copy(
-                gs[h][:, lo : lo + n], xs[:, h * T : (h + reach) * T].indirect(offs_t[:, lo // 16 : (lo + n) // 16])
+                gs[h][:, lo : lo + n], xs[:, h * T : h * T + reach].indirect(offs_t[:, lo // 16 : (lo + n) // 16])
             )
 
         def unpack(h, experts, queue):
@@ -141,14 +142,14 @@ def tile_moe_pln_mlp_relu2_kernel(
             e = b // 2
             done[b] = done.get(b, 0) + 1
             if done[b] == 1:
-                acc[b] = bank((0, 1, 2, 3, 6, 7, 0, 1)[b])
+                acc[b] = bank(b)
             lo = b % 2 * P
             w = (e % 2 * PASSES + s) * H
             nc.tensor.matmul_mx(
                 out=acc[b][:],
                 lhsT=gw[s, e][:, lo : lo + P].bitcast(FP8X4),
                 lhsT_scale=(gp if LIFT[s] else gs)[s // 2][:, b * P : (b + 1) * P],
-                rhs=w1w[e][:, s * 2 * H : (s + 1) * 2 * H].bitcast(FP4X4),
+                rhs=w1w[s][:, e * 2 * H : (e + 1) * 2 * H].bitcast(FP4X4),
                 rhs_scale=w1s[e // 2][:, w : w + H],
                 start=(done[b] == 1),
                 stop=(done[b] == PASSES),
@@ -165,7 +166,7 @@ def tile_moe_pln_mlp_relu2_kernel(
         turned = {}
 
         def turn(b):
-            turned[b] = bank((4, 5, 2, 3)[b % 4])
+            turned[b] = bank(b)
             for t in range(4):
                 nc.tensor.transpose(turned[b][:, t * P : (t + 1) * P], relu[b][:, t, :], ident[:])
 
@@ -232,6 +233,7 @@ def tile_moe_pln_mlp_relu2_kernel(
         nc.sync.dma_start(offs_t[:], offs)
         nc.vector.memset(w1s[0][:].bitcast(I32), 0)
         nc.vector.memset(w1s[1][:].bitcast(I32), 0)
+        nc.vector.memset(xw[:, T:].bitcast(I32), 0)
         nc.gpsimd.memset(xs[:].bitcast(I32), 0)
         for h in range(2):
             nc.gpsimd.memset(gp[h][:].bitcast(I32), 0)
@@ -241,47 +243,38 @@ def tile_moe_pln_mlp_relu2_kernel(
         load_x(3)
         load_w1(0)
         load_w1_scales(0, nc.sync)
+        load_w1_scales(1, nc.sync)
         cast(0, 0, 320, "v")
         cast(0, 320, T, "s")
         quantise(0, 0, 256)
         quantise(0, 256, T)
         load_w1(1, "raw0_0")
-        load_w1_scales(1, nc.sync)
         load_w1(2, "xb0")
-        for e in range(3):
-            words(0, (e,))
-        cast(1, 0, 128, "v")
-        cast(1, 128, T, "s")
+        words(0, (0, 1, 2, 3), 1408)
+        cast(1, 0, 64, "v")
+        cast(1, 64, T, "s")
         quantise(1, 0, T)
         load_w1(3, "raw1_0")
-        for e in (0, 1):
-            scales(0, (e,))
-        unpack(0, (0, 1), nc.gpsimd)
-        for e in (0, 1):
-            words(1, (e,))
-        for e in (2, 3):
-            scales(0, (e,))
-        unpack(0, (2, 3), nc.gpsimd)
+        w2w = load_w2("xb1")
+        scales(0, (0, 1, 2, 3), 1408)
+        unpack(0, (0, 1, 2, 3), nc.gpsimd)
+        words(1, (0, 1), 704)
         cast(2, 0, T, "s")
         quantise(2, 0, T)
+        g = load_gate("raw2_0")
         cast(3, 0, T, "s")
         quantise(3, 0, T)
-        for e in (0, 1):
-            scales(1, (e,))
+        scales(1, (0, 1), 704)
         unpack4(1, (0, 1), nc.scalar)
-        words(1, (2,), 3)
-        words(2, (0,), 2)
-        words(3, (0,))
-        words(2, (1,), 2)
-        words(3, (1,))
-        scales(1, (2,))
-        scales(1, (3,))
+        words(1, (2, 3), 1536)
+        for e in (0, 1):
+            words(2, (e,), 1024)
+            words(3, (e,))
+        scales(1, (2, 3), 704)
         unpack4(1, (2, 3), nc.sync)
         w2s = hold([P, E * N], U8, "w2s", "xs")
         nc.gpsimd.memset(w2s[:].bitcast(I32), 0)
         load_w2_scales(nc.sync)
-        w2w = load_w2("gw12")
-        g = load_gate("gw02")
 
         def passes(e, which):
             for s in which:
@@ -292,42 +285,37 @@ def tile_moe_pln_mlp_relu2_kernel(
             for b in (2 * e, 2 * e + 1):
                 for s in (2, 3):
                     first(s, b)
-                rectify(b, "v" if e == 3 else "s")
+                rectify(b, "s")
 
         def hidden(e):
             for b in (2 * e, 2 * e + 1):
                 turn(b)
                 square(b)
 
-        for e in range(3):
-            passes(e, (0, 1))
+        for s in (0, 1):
+            for e in range(E):
+                passes(e, (s,))
         finish(0)
         finish(1)
+        words(3, (2, 3), 704, "gw30")
+        words(2, (2, 3), 704, "gw31")
         hidden(0)
-        words(3, (2,), 1, "gw20")
-        words(0, (3,), 1, "gw30")
-        words(2, (2,), 1, "gw21")
-        words(1, (3,), 1, "gw31")
-        words(2, (3,), 1, "r0")
-        words(3, (3,), 1, "r1")
-        passes(2, (3,))
         hidden(1)
-        passes(3, (0,))
-        passes(2, (2,))
-        rectify(4, "s")
-        rectify(5, "s")
-        passes(3, (1,))
-        finish(3)
+        for s in (3, 2):
+            for e in (2, 3):
+                passes(e, (s,))
+        for b in range(4, 8):
+            rectify(b, "sv"[b % 2])
         hidden(2)
         hidden(3)
         for b in range(8):
             quantise_h(b)
         nc.sync.dma_start(pos1_t[:], pos1)
         nc.sync.dma_start(pos2_t[:], pos2)
-        result((0, 1), 0, "v", 4)
-        result((2,), 0, "v", 5)
-        result((3,), 0, "v", 0)
+        result((0, 1), 0, "v", 0)
+        result((2,), 0, "v", 3)
+        result((3,), 0, "v", 4)
         for j in (1, 2):
-            result((0, 1), j, "s", 5 + j)
-            result((2, 3), j, "s", j)
+            result((0, 1), j, "s", j)
+            result((2, 3), j, "s", 4 + j)
         combine()

@@ -242,30 +242,31 @@ def tile_moe_pln_mlp_relu2_kernel(
         load_x(2)
         load_x(3)
         load_w1(0)
+        nc.sync.dma_start(pos1_t[:], pos1)
+        nc.sync.dma_start(pos2_t[:], pos2)
         load_w1_scales(0, nc.sync)
         load_w1_scales(1, nc.sync)
+        for s in range(1, PASSES):
+            load_w1(s)
         cast(0, 0, 320, "v")
         cast(0, 320, T, "s")
         quantise(0, 0, 256)
         quantise(0, 256, T)
-        load_w1(1, "raw0_0")
-        load_w1(2, "xb0")
         words(0, (0, 1, 2, 3), 1408)
         cast(1, 0, 64, "v")
         cast(1, 64, T, "s")
         quantise(1, 0, T)
-        load_w1(3, "raw1_0")
-        w2w = load_w2("xb1")
         scales(0, (0, 1, 2, 3), 1408)
         unpack(0, (0, 1, 2, 3), nc.gpsimd)
         words(1, (0, 1), 704)
         cast(2, 0, T, "s")
         quantise(2, 0, T)
-        g = load_gate("raw2_0")
         cast(3, 0, T, "s")
         quantise(3, 0, T)
         scales(1, (0, 1), 704)
-        unpack4(1, (0, 1), nc.scalar)
+        unpack4(1, (0, 1), nc.sync)
+        w2w = load_w2(None)
+        g = load_gate(None)
         words(1, (2, 3), 1536)
         for e in (0, 1):
             words(2, (e,), 1024)
@@ -297,8 +298,8 @@ def tile_moe_pln_mlp_relu2_kernel(
                 passes(e, (s,))
         finish(0)
         finish(1)
-        words(3, (2, 3), 704, "gw30")
-        words(2, (2, 3), 704, "gw31")
+        words(3, (2, 3), 704, "gw31")
+        words(2, (2, 3), 704, "r0")
         hidden(0)
         hidden(1)
         for s in (3, 2):
@@ -310,12 +311,10 @@ def tile_moe_pln_mlp_relu2_kernel(
         hidden(3)
         for b in range(8):
             quantise_h(b)
-        nc.sync.dma_start(pos1_t[:], pos1)
-        nc.sync.dma_start(pos2_t[:], pos2)
-        result((0, 1), 0, "v", 0)
+        result((0, 1), 0, "v", 4)
         result((2,), 0, "v", 3)
-        result((3,), 0, "v", 4)
+        result((3,), 0, "v", 1)
         for j in (1, 2):
-            result((0, 1), j, "s", j)
-            result((2, 3), j, "s", 4 + j)
+            result((0, 1), j, "s", (5, 6)[j - 1])
+            result((2, 3), j, "s", (0, 2)[j - 1])
         combine()

@@ -229,6 +229,7 @@ def tile_moe_pln_mlp_relu2_kernel(
                     nc.vector.tensor_tensor(o[:, n], a[:, n], b[:, n], ADD)
                     nc.sync.dma_start(out=out[j * P : (j + 1) * P, lo:hi], in_=o[:, n])
 
+        w2s = hold([P, E * N], U8, "w2s")
         load_x(0)
         nc.sync.dma_start(offs_t[:], offs)
         nc.vector.memset(w1s[0][:].bitcast(I32), 0)
@@ -237,17 +238,14 @@ def tile_moe_pln_mlp_relu2_kernel(
         nc.gpsimd.memset(xs[:].bitcast(I32), 0)
         for h in range(2):
             nc.gpsimd.memset(gp[h][:].bitcast(I32), 0)
+        nc.gpsimd.memset(w2s[:].bitcast(I32), 0)
         make_identity(nc, ident[:])
         load_x(1)
         load_x(2)
         load_x(3)
         load_w1(0)
-        nc.sync.dma_start(pos1_t[:], pos1)
-        nc.sync.dma_start(pos2_t[:], pos2)
         load_w1_scales(0, nc.sync)
         load_w1_scales(1, nc.sync)
-        for s in range(1, PASSES):
-            load_w1(s)
         cast(0, 0, 320, "v")
         cast(0, 320, T, "s")
         quantise(0, 0, 256)
@@ -257,7 +255,9 @@ def tile_moe_pln_mlp_relu2_kernel(
         cast(1, 64, T, "s")
         quantise(1, 0, T)
         scales(0, (0, 1, 2, 3), 1408)
-        unpack(0, (0, 1, 2, 3), nc.gpsimd)
+        unpack(0, (0, 1, 2, 3), nc.sync)
+        for s in range(1, PASSES):
+            load_w1(s)
         words(1, (0, 1), 704)
         cast(2, 0, T, "s")
         quantise(2, 0, T)
@@ -266,16 +266,18 @@ def tile_moe_pln_mlp_relu2_kernel(
         scales(1, (0, 1), 704)
         unpack4(1, (0, 1), nc.sync)
         w2w = load_w2(None)
-        g = load_gate(None)
+        load_w2_scales(nc.sync)
         words(1, (2, 3), 1536)
         for e in (0, 1):
             words(2, (e,), 1024)
             words(3, (e,))
         scales(1, (2, 3), 704)
         unpack4(1, (2, 3), nc.sync)
-        w2s = hold([P, E * N], U8, "w2s", "xs")
-        nc.gpsimd.memset(w2s[:].bitcast(I32), 0)
-        load_w2_scales(nc.sync)
+        g = load_gate(None)
+        nc.sync.dma_start(pos1_t[:], pos1)
+        nc.sync.dma_start(pos2_t[:], pos2)
+        words(2, (2, 3), 704)
+        words(3, (2, 3), 704)
 
         def passes(e, which):
             for s in which:
@@ -286,7 +288,7 @@ def tile_moe_pln_mlp_relu2_kernel(
             for b in (2 * e, 2 * e + 1):
                 for s in (2, 3):
                     first(s, b)
-                rectify(b, "s")
+                rectify(b, "s" if e < 2 else "sv"[b % 2])
 
         def hidden(e):
             for b in (2 * e, 2 * e + 1):
@@ -298,15 +300,10 @@ def tile_moe_pln_mlp_relu2_kernel(
                 passes(e, (s,))
         finish(0)
         finish(1)
-        words(3, (2, 3), 704, "gw31")
-        words(2, (2, 3), 704, "r0")
         hidden(0)
         hidden(1)
-        for s in (3, 2):
-            for e in (2, 3):
-                passes(e, (s,))
-        for b in range(4, 8):
-            rectify(b, "sv"[b % 2])
+        finish(2)
+        finish(3)
         hidden(2)
         hidden(3)
         for b in range(8):

@@ -276,8 +276,6 @@ def tile_moe_pln_mlp_relu2_kernel(
         g = load_gate(None)
         nc.sync.dma_start(pos1_t[:], pos1)
         nc.sync.dma_start(pos2_t[:], pos2)
-        words(2, (2, 3), 704)
-        words(3, (2, 3), 704)
 
         def passes(e, which):
             for s in which:
@@ -301,9 +299,14 @@ def tile_moe_pln_mlp_relu2_kernel(
         finish(0)
         finish(1)
         hidden(0)
+        words(3, (2, 3), 704, "gw31")
+        words(2, (2, 3), 704, "r0")
         hidden(1)
-        finish(2)
-        finish(3)
+        for s in (3, 2):
+            for e in (2, 3):
+                passes(e, (s,))
+        for b in range(4, 8):
+            rectify(b, "sv"[b % 2])
         hidden(2)
         hidden(3)
         for b in range(8):

@@ -8,7 +8,8 @@ P = 128
 PASSES = K // 512
 SLOTS = E * C
 CUTS = (((0, 512),), ((0, 512),), ((0, 512),), ((0, 512),))
-SPARE = 192
+WORDS_AT = (0, 1408, 2112, 2624)
+PLANE_AT = (0, 1408)
 LIFT = (0, 4, 4, 0)
 FLOPS = 2 * SLOTS * (K * H + H * N)
 
@@ -57,8 +58,8 @@ def tile_moe_pln_mlp_relu2_kernel(
             for lo, hi in CUTS[s]:
                 raw[s, lo] = hold([P, 4, hi - lo], F32, "raw%d_%d" % (s, lo))
         xb = [hold([P, T, 4], BF16, "xb%d" % s) for s in range(PASSES)]
-        xw = hold([P, PASSES * T + SPARE], U32, "xw")
-        xs = hold([P, 3 * T], U8, "xs")
+        xw = hold([P, WORDS_AT[3] + 704], U32, "xw")
+        xs = hold([P, 1408 + 704], U8, "xs")
         gw = {}
         gs = [hold([P, SLOTS], U8, "gs%d" % h) for h in range(2)]
         gp = [hold([P, SLOTS], U8, "gp%d" % h) for h in range(2)]
@@ -73,12 +74,14 @@ def tile_moe_pln_mlp_relu2_kernel(
             for lo, hi in CUTS[s]:
                 nc.sync.dma_start(out=raw[s, lo][:], in_=xT_v[s][:, :, lo:hi])
 
-        def load_w1(s, tag=None):
-            w1w[s] = hold([P, E * 2 * H], U8, "w1w%d" % s, tag)
+        def load_w1(s, lo, hi):
+            words1 = hold([P, (hi - lo) * 2 * H], U8, "w1w%d%d" % (s, lo))
             nc.sync.dma_start(
-                out=w1w[s][:].bitcast(I32).rearrange("p (e b) -> p e b", e=E),
-                in_=w1w_v[:, s].rearrange("e p b -> p e b"),
+                out=words1[:].bitcast(I32).rearrange("p (e b) -> p e b", e=hi - lo),
+                in_=w1w_v[lo:hi, s].rearrange("e p b -> p e b"),
             )
+            for e in range(lo, hi):
+                w1w[s, e] = words1[:, (e - lo) * 2 * H : (e - lo + 1) * 2 * H]
 
         def load_w1_scales(i, queue):
             for r in range(4):
@@ -105,8 +108,8 @@ def tile_moe_pln_mlp_relu2_kernel(
 
         def quantise(s, lo, hi):
             nc.vector.quantize_mx(
-                out=xw[:, s * T + lo : s * T + hi].bitcast(FP8X4),
-                scales=xs[LIFT[s] : P, s // 2 * T + lo : s // 2 * T + hi],
+                out=xw[:, WORDS_AT[s] + lo : WORDS_AT[s] + hi].bitcast(FP8X4),
+                scales=xs[LIFT[s] : P, PLANE_AT[s // 2] + lo : PLANE_AT[s // 2] + hi],
                 in_=xb[s][:, lo:hi, :].rearrange("p c t -> p (c t)"),
             )
 
@@ -114,7 +117,7 @@ def tile_moe_pln_mlp_relu2_kernel(
             n = len(experts) * C
             lo = experts[0] * C // 16
             codes = hold([P, n], U32, "gw%d%d" % (s, experts[0]), tag)
-            nc.vector.tensor_copy(codes[:], xw[:, s * T : s * T + reach].indirect(offs_t[:, lo : lo + n // 16]))
+            nc.vector.tensor_copy(codes[:], xw[:, WORDS_AT[s] : WORDS_AT[s] + reach].indirect(offs_t[:, lo : lo + n // 16]))
             for i, e in enumerate(experts):
                 gw[s, e] = codes[:, i * C : (i + 1) * C]
 
@@ -122,7 +125,7 @@ def tile_moe_pln_mlp_relu2_kernel(
             n = len(experts) * C
             lo = experts[0] * C
             nc.vector.tensor_copy(
-                gs[h][:, lo : lo + n], xs[:, h * T : h * T + reach].indirect(offs_t[:, lo // 16 : (lo + n) // 16])
+                gs[h][:, lo : lo + n], xs[:, PLANE_AT[h] : PLANE_AT[h] + reach].indirect(offs_t[:, lo // 16 : (lo + n) // 16])
             )
 
         def unpack(h, experts, queue):
@@ -149,7 +152,7 @@ def tile_moe_pln_mlp_relu2_kernel(
                 out=acc[b][:],
                 lhsT=gw[s, e][:, lo : lo + P].bitcast(FP8X4),
                 lhsT_scale=(gp if LIFT[s] else gs)[s // 2][:, b * P : (b + 1) * P],
-                rhs=w1w[s][:, e * 2 * H : (e + 1) * 2 * H].bitcast(FP4X4),
+                rhs=w1w[s, e].bitcast(FP4X4),
                 rhs_scale=w1s[e // 2][:, w : w + H],
                 start=(done[b] == 1),
                 stop=(done[b] == PASSES),
@@ -234,7 +237,8 @@ def tile_moe_pln_mlp_relu2_kernel(
         nc.sync.dma_start(offs_t[:], offs)
         nc.vector.memset(w1s[0][:].bitcast(I32), 0)
         nc.vector.memset(w1s[1][:].bitcast(I32), 0)
-        nc.vector.memset(xw[:, T:].bitcast(I32), 0)
+        for lo, hi in ((T, 1408), (1408 + T, 2112), (2624 + T, 2624 + 704)):
+            nc.vector.memset(xw[:, lo:hi].bitcast(I32), 0)
         nc.gpsimd.memset(xs[:].bitcast(I32), 0)
         for h in range(2):
             nc.gpsimd.memset(gp[h][:].bitcast(I32), 0)
@@ -243,7 +247,7 @@ def tile_moe_pln_mlp_relu2_kernel(
         load_x(1)
         load_x(2)
         load_x(3)
-        load_w1(0)
+        load_w1(0, 0, E)
         load_w1_scales(0, nc.sync)
         load_w1_scales(1, nc.sync)
         cast(0, 0, 320, "v")
@@ -256,18 +260,20 @@ def tile_moe_pln_mlp_relu2_kernel(
         quantise(1, 0, T)
         scales(0, (0, 1, 2, 3), 1408)
         unpack(0, (0, 1, 2, 3), nc.sync)
-        for s in range(1, PASSES):
-            load_w1(s)
-        words(1, (0, 1), 704)
+        load_w1(1, 0, E)
+        for s in (2, 3):
+            load_w1(s, 0, 2)
         cast(2, 0, T, "s")
         quantise(2, 0, T)
+        words(1, (0, 1), 704, "raw2_0")
         cast(3, 0, T, "s")
         quantise(3, 0, T)
         scales(1, (0, 1), 704)
         unpack4(1, (0, 1), nc.sync)
+        for s in (3, 2):
+            load_w1(s, 2, E)
         w2w = load_w2(None)
         load_w2_scales(nc.sync)
-        words(1, (2, 3), 1536)
         for e in (0, 1):
             words(2, (e,), 1024)
             words(3, (e,))
@@ -286,27 +292,30 @@ def tile_moe_pln_mlp_relu2_kernel(
             for b in (2 * e, 2 * e + 1):
                 for s in (2, 3):
                     first(s, b)
-                rectify(b, "s" if e < 2 else "sv"[b % 2])
+                rectify(b, "sssssvvv"[b])
 
         def hidden(e):
             for b in (2 * e, 2 * e + 1):
                 turn(b)
                 square(b)
 
-        for s in (0, 1):
-            for e in range(E):
-                passes(e, (s,))
+        for e in range(E):
+            passes(e, (0,))
+        for e in (0, 1):
+            passes(e, (1,))
         finish(0)
         finish(1)
         hidden(0)
-        words(3, (2, 3), 704, "gw31")
-        words(2, (2, 3), 704, "r0")
+        words(1, (2, 3), 704, "gw30")
+        words(2, (2,), T, "gw21")
+        words(3, (2,), T, "gw31")
+        words(2, (3,), T, "r0")
+        words(3, (3,), T, "r1")
         hidden(1)
-        for s in (3, 2):
-            for e in (2, 3):
-                passes(e, (s,))
-        for b in range(4, 8):
-            rectify(b, "sv"[b % 2])
+        passes(2, (1,))
+        finish(2)
+        passes(3, (1,))
+        finish(3)
         hidden(2)
         hidden(3)
         for b in range(8):

@@ -34,7 +34,7 @@ def tile_moe_pln_mlp_relu2_kernel(
     with ExitStack() as ctx:
         lists = ctx.enter_context(tc.tile_pool(name="lists", bufs=1))
         keep = ctx.enter_context(tc.tile_pool(name="keep", bufs=1))
-        work = ctx.enter_context(tc.tile_pool(name="work", bufs=4))
+        work = ctx.enter_context(tc.tile_pool(name="work", bufs=6))
         psum = ctx.enter_context(tc.psum_pool(name="psum", bufs=1))
 
         def hold(shape, dtype, name, tag=None):
@@ -221,16 +221,39 @@ def tile_moe_pln_mlp_relu2_kernel(
 
         def combine():
             for j in range(N // P):
-                for lo, hi in ((0, T),) if j < 2 else ((0, T // 2), (T // 2, T)):
+                for lo, hi in ((0, T),) if j == 0 else ((0, T // 2), (T // 2, T)):
                     a = work.tile([P, T], F32, name="a")
                     b = work.tile([P, T], F32, name="b")
-                    o = work.tile([P, T], F32, name="o")
                     n = slice(0, hi - lo)
                     cols = slice(lo // 16, hi // 16)
                     nc.vector.tensor_tensor(a[:, n], y[j][:].indirect(pos1_t[:, cols]), g[:, 0, lo:hi], MULT)
                     nc.vector.tensor_tensor(b[:, n], y[j][:].indirect(pos2_t[:, cols]), g[:, 1, lo:hi], MULT)
-                    nc.vector.tensor_tensor(o[:, n], a[:, n], b[:, n], ADD)
-                    nc.sync.dma_start(out=out[j * P : (j + 1) * P, lo:hi], in_=o[:, n])
+                    if j == 2:
+                        o = work.tile([P, 2 * P], F32, name="o")
+                        nc.vector.tensor_tensor(o[:], a[:, n], b[:, n], ADD)
+                        nc.sync.dma_start(out=out[j * P : (j + 1) * P, lo:hi], in_=o[:])
+                        continue
+                    for at in range(0, hi - lo, 2 * P):
+                        k = (lo + at) // (2 * P)
+                        across = bank(2 * k)
+                        for c in range(2):
+                            for i, term in enumerate((b, a)):
+                                nc.tensor.matmul(
+                                    across[:, c * P : (c + 1) * P],
+                                    lhsT=term[:, at + c * P : at + (c + 1) * P],
+                                    rhs=ident[:],
+                                    is_transpose=True,
+                                    start=(i == 0),
+                                    stop=(i == 1),
+                                )
+                        total = work.tile([P, 2 * P], F32, name="total")
+                        nc.scalar.copy(total[:], across[:, 0 : 2 * P])
+                        back = bank(4 * j + 2 * k + 1)
+                        for c in range(2):
+                            nc.tensor.transpose(back[:, c * P : (c + 1) * P], total[:, c * P : (c + 1) * P], ident[:])
+                        summed = work.tile([P, 2 * P], F32, name="summed")
+                        nc.scalar.copy(summed[:], back[:, 0 : 2 * P])
+                        nc.scalar.dma_start(out=out[j * P : (j + 1) * P, lo + at : lo + at + 2 * P], in_=summed[:])
 
         w2s = hold([P, E * N], U8, "w2s")
         load_x(0)

@@ -283,7 +283,7 @@ def tile_moe_pln_mlp_relu2_kernel(
         quantise(1, 0, T)
         scales(0, (0, 1, 2, 3), 1408)
         unpack(0, (0, 1, 2, 3), nc.sync)
-        load_w1(1, 0, E)
+        load_w1(1, 0, 2)
         for s in (2, 3):
             load_w1(s, 0, 2)
         cast(2, 0, T, "s")
@@ -293,15 +293,15 @@ def tile_moe_pln_mlp_relu2_kernel(
         quantise(3, 0, T)
         scales(1, (0, 1), 704)
         unpack4(1, (0, 1), nc.sync)
-        for s in (3, 2):
+        for s in (1, 2, 3):
             load_w1(s, 2, E)
-        w2w = load_w2(None)
-        load_w2_scales(nc.sync)
         for e in (0, 1):
             words(2, (e,), 1024)
             words(3, (e,))
         scales(1, (2, 3), 704)
         unpack4(1, (2, 3), nc.sync)
+        w2w = load_w2(None)
+        load_w2_scales(nc.sync)
         g = load_gate(None)
         nc.sync.dma_start(pos1_t[:], pos1)
         nc.sync.dma_start(pos2_t[:], pos2)

@@ -284,7 +284,7 @@ def tile_moe_pln_mlp_relu2_kernel(
         scales(0, (0, 1, 2, 3), 1408)
         unpack(0, (0, 1, 2, 3), nc.sync)
         load_w1(1, 0, 2)
-        for s in (2, 3):
+        for s in (3, 2):
             load_w1(s, 0, 2)
         cast(2, 0, T, "s")
         quantise(2, 0, T)
@@ -293,11 +293,11 @@ def tile_moe_pln_mlp_relu2_kernel(
         quantise(3, 0, T)
         scales(1, (0, 1), 704)
         unpack4(1, (0, 1), nc.sync)
-        for s in (1, 2, 3):
+        for s in (1, 3, 2):
             load_w1(s, 2, E)
-        for e in (0, 1):
-            words(2, (e,), 1024)
-            words(3, (e,))
+        words(3, (0, 1), 704)
+        words(2, (0, 1), 1024)
+        words(1, (2, 3), 1728)
         scales(1, (2, 3), 704)
         unpack4(1, (2, 3), nc.sync)
         w2w = load_w2(None)
@@ -326,19 +326,25 @@ def tile_moe_pln_mlp_relu2_kernel(
             passes(e, (0,))
         for e in (0, 1):
             passes(e, (1,))
-        finish(0)
-        finish(1)
+        for e in (0, 1):
+            passes(e, (3,))
+        for b in range(4):
+            first(2, b)
+            rectify(b, "s")
         hidden(0)
-        words(1, (2, 3), 704, "gw30")
-        words(2, (2,), T, "gw21")
-        words(3, (2,), T, "gw31")
-        words(2, (3,), T, "r0")
+        words(3, (2,), T, "gw20")
+        words(2, (2,), T, "r0")
         words(3, (3,), T, "r1")
+        for e in (2, 3):
+            passes(e, (1,))
+        passes(2, (3,))
         hidden(1)
-        passes(2, (1,))
-        finish(2)
-        passes(3, (1,))
-        finish(3)
+        words(2, (3,), T, "gw12")
+        passes(3, (3,))
+        passes(2, (2,))
+        passes(3, (2,))
+        for b in range(4, 8):
+            rectify(b, "svsv"[b - 4])
         hidden(2)
         hidden(3)
         for b in range(8):

@@ -7,10 +7,6 @@ K, T, E, C, H, N = 2048, 512, 4, 256, 512, 384
 P = 128
 PASSES = K // 512
 SLOTS = E * C
-CUTS = (((0, 512),), ((0, 512),), ((0, 512),), ((0, 512),))
-WORDS_AT = (0, 1408, 2112, 2624)
-PLANE_AT = (0, 1408)
-LIFT = (0, 4, 4, 0)
 FLOPS = 2 * SLOTS * (K * H + H * N)
 
 F32 = mybir.dt.float32
@@ -25,6 +21,11 @@ RELU = mybir.ActivationFunctionType.Relu
 SQUARE = mybir.ActivationFunctionType.Square
 MULT = mybir.AluOpType.mult
 ADD = mybir.AluOpType.add
+WORDS_AT = (0, 1408, 2112, 2624)
+XW = 2624 + 704
+PLANE_AT = (0, 0, 1408, 1408)
+XS = 2112
+LIFT = (0, 4, 4, 0)
 
 
 def tile_moe_pln_mlp_relu2_kernel(
@@ -34,7 +35,6 @@ def tile_moe_pln_mlp_relu2_kernel(
     with ExitStack() as ctx:
         lists = ctx.enter_context(tc.tile_pool(name="lists", bufs=1))
         keep = ctx.enter_context(tc.tile_pool(name="keep", bufs=1))
-        work = ctx.enter_context(tc.tile_pool(name="work", bufs=6))
         psum = ctx.enter_context(tc.psum_pool(name="psum", bufs=1))
 
         def hold(shape, dtype, name, tag=None):
@@ -54,25 +54,25 @@ def tile_moe_pln_mlp_relu2_kernel(
         w2s_v = w2_scales.bitcast(I32)
 
         raw = {}
-        for s in range(PASSES):
-            for lo, hi in CUTS[s]:
-                raw[s, lo] = hold([P, 4, hi - lo], F32, "raw%d_%d" % (s, lo))
         xb = [hold([P, T, 4], BF16, "xb%d" % s) for s in range(PASSES)]
-        xw = hold([P, WORDS_AT[3] + 704], U32, "xw")
-        xs = hold([P, 1408 + 704], U8, "xs")
+        xw = hold([P, XW], U32, "xw")
+        xs = hold([P, XS], U8, "xs")
         gw = {}
-        gs = [hold([P, SLOTS], U8, "gs%d" % h) for h in range(2)]
-        gp = [hold([P, SLOTS], U8, "gp%d" % h) for h in range(2)]
-        w1s = [hold([P, 2 * PASSES * H], U8, "w1s%d" % i) for i in range(2)]
+        gs = {}
+        low = {}
+        w1s = {}
         w1w = {}
         hw = hold([P, SLOTS], U32, "hw")
         hs = hold([P, SLOTS], U8, "hs")
         y = [hold([P, SLOTS], F32, "y%d" % j) for j in range(N // P)]
         ident = hold([P, P], F32, "ident")
+        w2s = hold([P, E * N], U8, "w2s")
+        w2w = hold([P, E * 2 * N], U8, "w2w")
+        g = hold([P, 2, T], F32, "g")
 
-        def load_x(s):
-            for lo, hi in CUTS[s]:
-                nc.sync.dma_start(out=raw[s, lo][:], in_=xT_v[s][:, :, lo:hi])
+        def load_x(s, lo=0, hi=T):
+            raw[s, lo] = hold([P, 4, hi - lo], F32, "raw%d_%d" % (s, lo))
+            nc.sync.dma_start(out=raw[s, lo][:], in_=xT_v[s][:, :, lo:hi])
 
         def load_w1(s, lo, hi):
             words1 = hold([P, (hi - lo) * 2 * H], U8, "w1w%d%d" % (s, lo))
@@ -83,22 +83,50 @@ def tile_moe_pln_mlp_relu2_kernel(
             for e in range(lo, hi):
                 w1w[s, e] = words1[:, (e - lo) * 2 * H : (e - lo + 1) * 2 * H]
 
-        def load_w1_scales(i, queue):
+        def load_w1e(e, lo, hi):
+            words1 = hold([P, (hi - lo) * 2 * H], U8, "w1e%d%d" % (e, lo))
+            nc.sync.dma_start(
+                out=words1[:].bitcast(I32).rearrange("p (s b) -> p s b", s=hi - lo),
+                in_=w1w_v[e, lo:hi].rearrange("s p b -> p s b"),
+            )
+            for s in range(lo, hi):
+                w1w[s, e] = words1[:, (s - lo) * 2 * H : (s - lo + 1) * 2 * H]
+
+        def zero_w1_scales(lo, hi, engine):
+            plane = hold([P, (hi - lo) * PASSES * H], U8, "w1s%d" % lo)
+            engine.memset(plane[:].bitcast(I32), 0)
+            for e in range(lo, hi):
+                w1s[e] = (plane, lo)
+
+        def load_w1_scales(lo, hi):
             for r in range(4):
-                queue.dma_start(
-                    out=w1s[i][r:P:32, :].bitcast(I32).rearrange("p (a b) -> p a b", b=H // 4),
-                    in_=w1s_v[2 * i : 2 * i + 2, :, r:16:4, :].rearrange("e s q b -> q (e s) b"),
+                nc.sync.dma_start(
+                    out=w1s[lo][0][r:P:32, :].bitcast(I32).rearrange("p (a b) -> p a b", b=H // 4),
+                    in_=w1s_v[lo:hi, :, r:16:4, :].rearrange("e s q b -> q (e s) b"),
                 )
 
-        def load_w2_scales(queue):
+        def load_w2():
+            nc.sync.dma_start(
+                out=w2w[:].bitcast(I32).rearrange("p (e b) -> p e b", e=E),
+                in_=w2w_v[:, 0].rearrange("e p b -> p e b"),
+            )
+
+        def load_w2_scales():
             for r in range(4):
-                queue.dma_start(
+                nc.sync.dma_start(
                     out=w2s[r:P:32, :].bitcast(I32).rearrange("p (a b) -> p a b", b=N // 4),
                     in_=w2s_v[:, 0, r:16:4, :].rearrange("e q b -> q e b"),
                 )
 
+        def load_gate():
+            nc.sync.dma_start(out=g[:], in_=gate[:, 0:P, :].rearrange("g p t -> p g t"))
+
+        def load_pos():
+            nc.sync.dma_start(pos1_t[:], pos1)
+            nc.sync.dma_start(pos2_t[:], pos2)
+
         def cast(s, lo, hi, engine):
-            base = max(a for a, b in CUTS[s] if a <= lo)
+            base = max(a for r, a in raw if r == s and a <= lo)
             dst = xb[s][:, lo:hi, :].rearrange("p (c i) t -> p c t i", i=4)
             src = raw[s, base][:, :, lo - base : hi - base].rearrange("p t (c i) -> p c t i", i=4)
             if engine == "v":
@@ -106,36 +134,45 @@ def tile_moe_pln_mlp_relu2_kernel(
             else:
                 nc.scalar.copy(dst, src)
 
-        def quantise(s, lo, hi):
+        def quantise(s, lo=0, hi=T):
             nc.vector.quantize_mx(
                 out=xw[:, WORDS_AT[s] + lo : WORDS_AT[s] + hi].bitcast(FP8X4),
-                scales=xs[LIFT[s] : P, PLANE_AT[s // 2] + lo : PLANE_AT[s // 2] + hi],
+                scales=xs[LIFT[s] : P, PLANE_AT[s] + lo : PLANE_AT[s] + hi],
                 in_=xb[s][:, lo:hi, :].rearrange("p c t -> p (c t)"),
             )
 
-        def words(s, experts, reach=T, tag=None):
-            n = len(experts) * C
-            lo = experts[0] * C // 16
-            codes = hold([P, n], U32, "gw%d%d" % (s, experts[0]), tag)
-            nc.vector.tensor_copy(codes[:], xw[:, WORDS_AT[s] : WORDS_AT[s] + reach].indirect(offs_t[:, lo : lo + n // 16]))
-            for i, e in enumerate(experts):
-                gw[s, e] = codes[:, i * C : (i + 1) * C]
+        def words(s, lo, hi, reach, tag=None):
+            n = (hi - lo) * P
+            codes = hold([P, n], U32, "gw%d_%d" % (s, lo), tag)
+            nc.vector.tensor_copy(codes[:], xw[:, WORDS_AT[s] : WORDS_AT[s] + reach].indirect(offs_t[:, lo * 8 : hi * 8]))
+            for b in range(lo, hi):
+                gw[s, b] = codes[:, (b - lo) * P : (b - lo + 1) * P]
 
-        def scales(h, experts, reach=T):
-            n = len(experts) * C
-            lo = experts[0] * C
-            nc.vector.tensor_copy(
-                gs[h][:, lo : lo + n], xs[:, PLANE_AT[h] : PLANE_AT[h] + reach].indirect(offs_t[:, lo // 16 : (lo + n) // 16])
-            )
+        def scales(passes, lo, hi, reach, tag=None):
+            n = (hi - lo) * P
+            at = PLANE_AT[passes[0]]
+            rows = hold([P, n], U8, "gs%d_%d" % (passes[0], lo), tag)
+            nc.vector.tensor_copy(rows[:], xs[:, at : at + reach].indirect(offs_t[:, lo * 8 : hi * 8]))
+            for s in passes:
+                for b in range(lo, hi):
+                    gs[s, b] = (rows, lo)
 
-        def unpack(h, experts, queue):
-            cols = slice(experts[0] * C, (experts[-1] + 1) * C)
-            queue.dma_start(out=gp[h][0:112, cols].bitcast(I32), in_=gs[h][4:116, cols].bitcast(I32))
+        def zero_low(s, lo, hi):
+            low[s, lo] = hold([P, (hi - lo) * P], U8, "low%d_%d" % (s, lo))
+            nc.gpsimd.memset(low[s, lo][:].bitcast(I32), 0)
 
-        def unpack4(h, experts, queue):
-            cols = slice(experts[0] * C, (experts[-1] + 1) * C)
-            for r in range(4):
-                queue.dma_start(out=gp[h][r:P:32, cols].bitcast(I32), in_=gs[h][4 + r : P : 32, cols].bitcast(I32))
+        def lower(s, lo, hi, four=False, queue=None):
+            queue = queue or nc.sync
+            rows, base = gs[s, lo]
+            cols = slice((lo - base) * P, (hi - base) * P)
+            k = LIFT[s]
+            if four:
+                for r in range(4):
+                    queue.dma_start(out=low[s, lo][r:P:32, :].bitcast(I32), in_=rows[k + r : P : 32, cols].bitcast(I32))
+            else:
+                queue.dma_start(out=low[s, lo][0:112, :].bitcast(I32), in_=rows[k : k + 112, cols].bitcast(I32))
+            for b in range(lo, hi):
+                gs[s, b] = (low[s, lo], lo)
 
         acc = {}
         relu = {}
@@ -146,17 +183,23 @@ def tile_moe_pln_mlp_relu2_kernel(
             done[b] = done.get(b, 0) + 1
             if done[b] == 1:
                 acc[b] = bank(b)
-            lo = b % 2 * P
-            w = (e % 2 * PASSES + s) * H
+            plane, e0 = w1s[e]
+            w = ((e - e0) * PASSES + s) * H
+            rows, base = gs[s, b]
             nc.tensor.matmul_mx(
                 out=acc[b][:],
-                lhsT=gw[s, e][:, lo : lo + P].bitcast(FP8X4),
-                lhsT_scale=(gp if LIFT[s] else gs)[s // 2][:, b * P : (b + 1) * P],
+                lhsT=gw[s, b].bitcast(FP8X4),
+                lhsT_scale=rows[:, (b - base) * P : (b - base + 1) * P],
                 rhs=w1w[s, e].bitcast(FP4X4),
-                rhs_scale=w1s[e // 2][:, w : w + H],
+                rhs_scale=plane[:, w : w + H],
                 start=(done[b] == 1),
                 stop=(done[b] == PASSES),
             )
+
+        def firsts(which, blocks):
+            for s in which:
+                for b in blocks:
+                    first(s, b)
 
         def rectify(b, engine):
             relu[b] = hold([P, 4, P], F32, "r%d" % b)
@@ -168,191 +211,215 @@ def tile_moe_pln_mlp_relu2_kernel(
 
         turned = {}
 
-        def turn(b):
-            turned[b] = bank(b)
+        def turn(b, into=None):
+            turned[b] = bank(b if into is None else into)
             for t in range(4):
                 nc.tensor.transpose(turned[b][:, t * P : (t + 1) * P], relu[b][:, t, :], ident[:])
 
         hb = {}
 
-        def square(b):
-            hb[b] = hold([P, P, 4], BF16, "hb%d" % b)
-            nc.scalar.activation(hb[b][:], turned[b][:].rearrange("p (t n) -> p n t", t=4), SQUARE)
+        def square(b, pair=None):
+            if pair is None:
+                hb[b] = hold([P, P, 4], BF16, "hb%d" % b)[:]
+            else:
+                if b % 2 == 0:
+                    hb["pair", b] = hold([P, 2 * P, 4], BF16, "hb%d" % b)
+                hb[b] = hb["pair", b - b % 2][:, b % 2 * P : (b % 2 + 1) * P, :]
+            nc.scalar.activation(hb[b], turned[b][:].rearrange("p (t n) -> p n t", t=4), SQUARE)
 
-        def quantise_h(b, tag=None):
+        def square_v(b):
+            kept = hold([P, P, 4], F32, "kept%d" % b)
+            nc.vector.tensor_copy(kept[:], turned[b][:].rearrange("p (t n) -> p n t", t=4))
+            hb[b] = hold([P, P, 4], BF16, "hb%d" % b)[:]
+            nc.vector.tensor_tensor(hb[b], kept[:], kept[:], MULT)
+
+        def quantise_h(b, pair=False):
+            src = hb["pair", b][:] if pair else hb[b]
+            n = 2 if pair else 1
             nc.vector.quantize_mx(
-                out=hw[:, b * P : (b + 1) * P].bitcast(FP8X4),
-                scales=hs[:, b * P : (b + 1) * P],
-                in_=hb[b][:].rearrange("p n t -> p (n t)"),
+                out=hw[:, b * P : (b + n) * P].bitcast(FP8X4),
+                scales=hs[:, b * P : (b + n) * P],
+                in_=src.rearrange("p n t -> p (n t)"),
             )
 
-        def result(experts, j, engine, b):
-            n = len(experts) * C
-            sums = bank(b)
-            for i, e in reversed(list(enumerate(experts))):
-                w = e * N + j * P
+        sums = {}
+
+        def second(j, lo, hi, b, width=C):
+            sums[j, lo] = bank(b)
+            for at in reversed(range(lo, hi, width)):
+                w = at // C * N + j * P
                 nc.tensor.matmul_mx(
-                    out=sums[:, i * C : (i + 1) * C],
+                    out=sums[j, lo][:, at - lo : at - lo + width],
                     lhsT=w2w[:, 2 * w : 2 * (w + P)].bitcast(FP4X4),
                     lhsT_scale=w2s[:, w : w + P],
-                    rhs=hw[:, e * C : (e + 1) * C].bitcast(FP8X4),
-                    rhs_scale=hs[:, e * C : (e + 1) * C],
+                    rhs=hw[:, at : at + width].bitcast(FP8X4),
+                    rhs_scale=hs[:, at : at + width],
                     start=True,
                     stop=True,
                 )
-            lo = experts[0] * C
+
+        def fetch(j, lo, hi, engine):
             if engine == "v":
-                nc.vector.tensor_copy(y[j][:, lo : lo + n], sums[:, 0:n])
+                nc.vector.tensor_copy(y[j][:, lo:hi], sums[j, lo][:, 0 : hi - lo])
             else:
-                nc.scalar.copy(y[j][:, lo : lo + n], sums[:, 0:n])
+                nc.scalar.copy(y[j][:, lo:hi], sums[j, lo][:, 0 : hi - lo])
 
-        def load_w2(tag):
-            w2w = hold([P, E * 2 * N], U8, "w2w", tag)
-            nc.sync.dma_start(
-                out=w2w[:].bitcast(I32).rearrange("p (e b) -> p e b", e=E),
-                in_=w2w_v[:, 0].rearrange("e p b -> p e b"),
+        def result(j, lo, hi, b, engine, width=C):
+            second(j, lo, hi, b, width)
+            fetch(j, lo, hi, engine)
+
+        terms = {}
+
+        def term(j, i, lo, hi):
+            terms[j, i, lo] = hold([P, hi - lo], F32, "term%d%d_%d" % (j, i, lo))
+            nc.vector.tensor_tensor(
+                terms[j, i, lo][:], y[j][:].indirect((pos1_t, pos2_t)[i][:, lo // 16 : hi // 16]), g[:, i, lo:hi], MULT
             )
-            return w2w
 
-        def load_gate(tag):
-            g = hold([P, 2, T], F32, "g", tag)
-            nc.sync.dma_start(out=g[:], in_=gate[:, 0:P, :].rearrange("g p t -> p g t"))
-            return g
+        def part(j, i, lo, hi):
+            base = max(a for r, c, a in terms if (r, c) == (j, i) and a <= lo)
+            return terms[j, i, base][:, lo - base : hi - base]
 
-        def combine():
-            for j in range(N // P):
-                for lo, hi in ((0, T),) if j == 0 else ((0, T // 2), (T // 2, T)):
-                    a = work.tile([P, T], F32, name="a")
-                    b = work.tile([P, T], F32, name="b")
-                    n = slice(0, hi - lo)
-                    cols = slice(lo // 16, hi // 16)
-                    nc.vector.tensor_tensor(a[:, n], y[j][:].indirect(pos1_t[:, cols]), g[:, 0, lo:hi], MULT)
-                    nc.vector.tensor_tensor(b[:, n], y[j][:].indirect(pos2_t[:, cols]), g[:, 1, lo:hi], MULT)
-                    if j == 2:
-                        o = work.tile([P, 2 * P], F32, name="o")
-                        nc.vector.tensor_tensor(o[:], a[:, n], b[:, n], ADD)
-                        nc.sync.dma_start(out=out[j * P : (j + 1) * P, lo:hi], in_=o[:])
-                        continue
-                    for at in range(0, hi - lo, 2 * P):
-                        k = (lo + at) // (2 * P)
-                        across = bank(2 * k)
-                        for c in range(2):
-                            for i, term in enumerate((b, a)):
-                                nc.tensor.matmul(
-                                    across[:, c * P : (c + 1) * P],
-                                    lhsT=term[:, at + c * P : at + (c + 1) * P],
-                                    rhs=ident[:],
-                                    is_transpose=True,
-                                    start=(i == 0),
-                                    stop=(i == 1),
-                                )
-                        total = work.tile([P, 2 * P], F32, name="total")
-                        nc.scalar.copy(total[:], across[:, 0 : 2 * P])
-                        back = bank(4 * j + 2 * k + 1)
-                        for c in range(2):
-                            nc.tensor.transpose(back[:, c * P : (c + 1) * P], total[:, c * P : (c + 1) * P], ident[:])
-                        summed = work.tile([P, 2 * P], F32, name="summed")
-                        nc.scalar.copy(summed[:], back[:, 0 : 2 * P])
-                        nc.scalar.dma_start(out=out[j * P : (j + 1) * P, lo + at : lo + at + 2 * P], in_=summed[:])
+        def add(j, lo, hi, queue=None):
+            o = hold([P, hi - lo], F32, "o%d_%d" % (j, lo))
+            nc.vector.tensor_tensor(o[:], part(j, 0, lo, hi), part(j, 1, lo, hi), ADD)
+            (queue or nc.sync).dma_start(out=out[j * P : (j + 1) * P, lo:hi], in_=o[:])
 
-        w2s = hold([P, E * N], U8, "w2s")
+        def add_turned(j, lo, hi, b1, b2, queue=None):
+            n = hi - lo
+            across = bank(b1)
+            for c in range(n // P):
+                for i in (1, 0):
+                    nc.tensor.matmul(
+                        across[:, c * P : (c + 1) * P],
+                        lhsT=part(j, i, lo + c * P, lo + (c + 1) * P),
+                        rhs=ident[:],
+                        is_transpose=True,
+                        start=(i == 1),
+                        stop=(i == 0),
+                    )
+            total = hold([P, n], F32, "total%d_%d" % (j, lo))
+            nc.scalar.copy(total[:], across[:, 0:n])
+            back = bank(b2)
+            for c in range(n // P):
+                nc.tensor.transpose(back[:, c * P : (c + 1) * P], total[:, c * P : (c + 1) * P], ident[:])
+            summed = hold([P, n], F32, "summed%d_%d" % (j, lo))
+            nc.scalar.copy(summed[:], back[:, 0:n])
+            (queue or nc.scalar).dma_start(out=out[j * P : (j + 1) * P, lo:hi], in_=summed[:])
+
+        def zero_words(lo, hi):
+            nc.vector.memset(xw[:, lo:hi].bitcast(I32), 0)
+
         load_x(0)
         nc.sync.dma_start(offs_t[:], offs)
-        nc.vector.memset(w1s[0][:].bitcast(I32), 0)
-        nc.vector.memset(w1s[1][:].bitcast(I32), 0)
-        for lo, hi in ((T, 1408), (1408 + T, 2112), (2624 + T, 2624 + 704)):
-            nc.vector.memset(xw[:, lo:hi].bitcast(I32), 0)
+        zero_w1_scales(0, 2, nc.vector)
+        zero_w1_scales(2, 4, nc.vector)
+        zero_words(T, 1408)
+        zero_words(1408 + T, 2112)
+        zero_words(2624 + T, XW)
         nc.gpsimd.memset(xs[:].bitcast(I32), 0)
-        for h in range(2):
-            nc.gpsimd.memset(gp[h][:].bitcast(I32), 0)
+        zero_low(1, 0, 8)
+        zero_low(2, 0, 4)
+        zero_low(2, 4, 8)
         nc.gpsimd.memset(w2s[:].bitcast(I32), 0)
         make_identity(nc, ident[:])
         load_x(1)
         load_x(2)
         load_x(3)
         load_w1(0, 0, E)
-        load_w1_scales(0, nc.sync)
-        load_w1_scales(1, nc.sync)
+        load_w1_scales(0, 2)
+        load_w1_scales(2, 4)
         cast(0, 0, 320, "v")
         cast(0, 320, T, "s")
         quantise(0, 0, 256)
         quantise(0, 256, T)
-        words(0, (0, 1, 2, 3), 1408)
+        words(0, 0, 8, 1408)
         cast(1, 0, 64, "v")
         cast(1, 64, T, "s")
-        quantise(1, 0, T)
-        scales(0, (0, 1, 2, 3), 1408)
-        unpack(0, (0, 1, 2, 3), nc.sync)
+        quantise(1)
+        scales((0, 1), 0, 8, 1408)
+        lower(1, 0, 8)
         load_w1(1, 0, 2)
-        for s in (3, 2):
-            load_w1(s, 0, 2)
+        load_w1(3, 0, 2)
+        load_w1(2, 0, 2)
         cast(2, 0, T, "s")
-        quantise(2, 0, T)
-        words(1, (0, 1), 704, "raw2_0")
+        quantise(2)
+        words(1, 0, 4, 704, "raw2_0")
         cast(3, 0, T, "s")
-        quantise(3, 0, T)
-        scales(1, (0, 1), 704)
-        unpack4(1, (0, 1), nc.sync)
-        for s in (1, 3, 2):
-            load_w1(s, 2, E)
-        words(3, (0, 1), 704)
-        words(2, (0, 1), 1024)
-        words(1, (2, 3), 1728)
-        scales(1, (2, 3), 704)
-        unpack4(1, (2, 3), nc.sync)
-        w2w = load_w2(None)
-        load_w2_scales(nc.sync)
-        g = load_gate(None)
-        nc.sync.dma_start(pos1_t[:], pos1)
-        nc.sync.dma_start(pos2_t[:], pos2)
-
-        def passes(e, which):
-            for s in which:
-                for b in (2 * e, 2 * e + 1):
-                    first(s, b)
-
-        def finish(e):
-            for b in (2 * e, 2 * e + 1):
-                for s in (2, 3):
-                    first(s, b)
-                rectify(b, "sssssvvv"[b])
-
-        def hidden(e):
-            for b in (2 * e, 2 * e + 1):
-                turn(b)
-                square(b)
-
-        for e in range(E):
-            passes(e, (0,))
-        for e in (0, 1):
-            passes(e, (1,))
-        for e in (0, 1):
-            passes(e, (3,))
+        quantise(3)
+        scales((2, 3), 0, 4, 704)
+        lower(2, 0, 4, True)
+        load_w1(1, 2, 4)
+        load_w1(3, 2, 4)
+        load_w1(2, 2, 4)
+        words(3, 0, 4, 704)
+        words(2, 0, 4, 1024)
+        words(1, 4, 8, 1728)
+        scales((2, 3), 4, 8, 704)
+        lower(2, 4, 8, True)
+        load_pos()
+        load_w2()
+        load_w2_scales()
+        load_gate()
+        firsts((0,), range(8))
+        firsts((1, 3), range(4))
         for b in range(4):
             first(2, b)
             rectify(b, "s")
-        hidden(0)
-        words(3, (2,), T, "gw20")
-        words(2, (2,), T, "r0")
-        words(3, (3,), T, "r1")
-        for e in (2, 3):
-            passes(e, (1,))
-        passes(2, (3,))
-        hidden(1)
-        words(2, (3,), T, "gw12")
-        passes(3, (3,))
-        passes(2, (2,))
-        passes(3, (2,))
-        for b in range(4, 8):
-            rectify(b, "svsv"[b - 4])
-        hidden(2)
-        hidden(3)
-        for b in range(8):
+        for b in (0, 1):
+            turn(b)
+            square(b)
+        words(3, 4, 6, T, "gw2_0")
+        words(2, 4, 6, T, "r0")
+        words(3, 6, 8, T, "r1")
+        firsts((1,), range(4, 8))
+        firsts((3,), (4, 5))
+        for b in (2, 3):
+            turn(b)
+            square(b)
+        words(2, 6, 8, T, "gw1_4")
+        firsts((2,), (4, 5))
+        firsts((3,), (6, 7))
+        firsts((2,), (6, 7))
+        for b in range(3):
             quantise_h(b)
-        result((0, 1), 0, "v", 4)
-        result((2,), 0, "v", 3)
-        result((3,), 0, "v", 1)
-        for j in (1, 2):
-            result((0, 1), j, "s", (5, 6)[j - 1])
-            result((2, 3), j, "s", (0, 2)[j - 1])
-        combine()
+        rectify(4, "v")
+        rectify(5, "s")
+        quantise_h(3)
+        rectify(6, "v")
+        rectify(7, "s")
+        for b in range(4, 8):
+            turn(b)
+        square_v(4)
+        square(5)
+        square(6)
+        square(7)
+        result(0, 0, 512, 0, "s")
+        second(1, 0, 512, 1)
+        for b in (4, 5):
+            quantise_h(b)
+        second(0, 512, 768, 2)
+        quantise_h(6)
+        second(0, 768, 896, 3, 128)
+        fetch(0, 512, 768, "v")
+        quantise_h(7)
+        second(0, 896, 1024, 4, 128)
+        fetch(0, 768, 896, "v")
+        fetch(0, 896, 1024, "v")
+        fetch(1, 0, 512, "s")
+        result(1, 512, 1024, 5, "s")
+        result(2, 0, 512, 3, "s")
+        result(2, 512, 1024, 7, "s")
+        term(0, 0, 0, T)
+        term(0, 1, 0, T)
+        add_turned(0, 0, 256, 4, 6, nc.sync)
+        add_turned(0, 256, T, 0, 2, nc.sync)
+        term(1, 0, 0, T)
+        term(1, 1, 0, T)
+        add_turned(1, 0, 256, 6, 4)
+        term(2, 0, 0, T)
+        add(1, 256, T)
+        term(2, 1, 0, 384)
+        term(2, 1, 384, T)
+        add(2, 0, 384)
+        add(2, 384, T)

@@ -326,9 +326,10 @@ def tile_moe_pln_mlp_relu2_kernel(
         load_x(1)
         load_x(2)
         load_x(3)
-        load_w1(0, 0, E)
         load_w1_scales(0, 2)
+        load_w1(0, 0, 2)
         load_w1_scales(2, 4)
+        load_w1(0, 2, 4)
         cast(0, 0, 320, "v")
         cast(0, 320, T, "s")
         quantise(0, 0, 256)
@@ -412,14 +413,14 @@ def tile_moe_pln_mlp_relu2_kernel(
         result(2, 512, 1024, 7, "s")
         term(0, 0, 0, T)
         term(0, 1, 0, T)
-        add_turned(0, 0, 256, 4, 6, nc.sync)
-        add_turned(0, 256, T, 0, 2, nc.sync)
+        add_turned(0, 0, 256, 4, 6)
+        add_turned(0, 256, T, 0, 2)
         term(1, 0, 0, T)
         term(1, 1, 0, T)
         add_turned(1, 0, 256, 6, 4)
         term(2, 0, 0, T)
-        add(1, 256, T)
         term(2, 1, 0, 384)
-        term(2, 1, 384, T)
+        add(1, 256, T)
         add(2, 0, 384)
+        term(2, 1, 384, T)
         add(2, 384, T)

@@ -21,10 +21,10 @@ RELU = mybir.ActivationFunctionType.Relu
 SQUARE = mybir.ActivationFunctionType.Square
 MULT = mybir.AluOpType.mult
 ADD = mybir.AluOpType.add
-WORDS_AT = (0, 1408, 2112, 2624)
-XW = 2624 + 704
-PLANE_AT = (0, 0, 1408, 1408)
-XS = 2112
+WORDS_AT = (1536, 1024, 0, 512)
+XW = 1536 + 1408
+PLANE_AT = (512, 512, 0, 0)
+XS = 512 + 1408
 LIFT = (0, 4, 4, 0)
 
 
@@ -125,9 +125,16 @@ def tile_moe_pln_mlp_relu2_kernel(
             nc.sync.dma_start(pos1_t[:], pos1)
             nc.sync.dma_start(pos2_t[:], pos2)
 
-        def cast(s, lo, hi, engine):
+        own = {}
+
+        def rounded(s, lo, hi):
+            return own[s, lo][:] if (s, lo) in own else xb[s][:, lo:hi, :]
+
+        def cast(s, lo, hi, engine, tag=None):
             base = max(a for r, a in raw if r == s and a <= lo)
-            dst = xb[s][:, lo:hi, :].rearrange("p (c i) t -> p c t i", i=4)
+            if tag:
+                own[s, lo] = hold([P, hi - lo, 4], BF16, "own%d_%d" % (s, lo), tag)
+            dst = rounded(s, lo, hi).rearrange("p (c i) t -> p c t i", i=4)
             src = raw[s, base][:, :, lo - base : hi - base].rearrange("p t (c i) -> p c t i", i=4)
             if engine == "v":
                 nc.vector.tensor_copy(dst, src)
@@ -138,7 +145,7 @@ def tile_moe_pln_mlp_relu2_kernel(
             nc.vector.quantize_mx(
                 out=xw[:, WORDS_AT[s] + lo : WORDS_AT[s] + hi].bitcast(FP8X4),
                 scales=xs[LIFT[s] : P, PLANE_AT[s] + lo : PLANE_AT[s] + hi],
-                in_=xb[s][:, lo:hi, :].rearrange("p c t -> p (c t)"),
+                in_=rounded(s, lo, hi).rearrange("p c t -> p (c t)"),
             )
 
         def words(s, lo, hi, reach, tag=None):
@@ -157,9 +164,9 @@ def tile_moe_pln_mlp_relu2_kernel(
                 for b in range(lo, hi):
                     gs[s, b] = (rows, lo)
 
-        def zero_low(s, lo, hi):
+        def zero_low(s, lo, hi, engine=nc.gpsimd):
             low[s, lo] = hold([P, (hi - lo) * P], U8, "low%d_%d" % (s, lo))
-            nc.gpsimd.memset(low[s, lo][:].bitcast(I32), 0)
+            engine.memset(low[s, lo][:].bitcast(I32), 0)
 
         def lower(s, lo, hi, four=False, queue=None):
             queue = queue or nc.sync
@@ -232,6 +239,38 @@ def tile_moe_pln_mlp_relu2_kernel(
             nc.vector.tensor_copy(kept[:], turned[b][:].rearrange("p (t n) -> p n t", t=4))
             hb[b] = hold([P, P, 4], BF16, "hb%d" % b)[:]
             nc.vector.tensor_tensor(hb[b], kept[:], kept[:], MULT)
+
+        paired = {}
+
+        def rectify_w(b, engine):
+            relu[b] = hold([P, 2, P, 2], F32, "r%d" % b)
+            lanes = acc[b][:].rearrange("p (m u e) -> p u m e", u=2, e=2)
+            if engine == "v":
+                nc.vector.tensor_scalar_max(relu[b][:], lanes, 0.0)
+            else:
+                nc.scalar.activation(relu[b][:], lanes, RELU)
+
+        def square_w(b, engine):
+            paired[b] = hold([P, H], BF16, "paired%d" % b)
+            flat = relu[b][:].rearrange("p u m e -> p (u m e)")
+            if engine == "v":
+                nc.vector.tensor_tensor(paired[b][:], flat, flat, MULT)
+            else:
+                nc.scalar.activation(paired[b][:], flat, SQUARE)
+
+        def turn_w(b, into=None):
+            turned[b] = bank(b if into is None else into)
+            for u in range(2):
+                nc.tensor.transpose(turned[b][:, u * P : (u + 1) * P], paired[b][:].bitcast(F32)[:, u * P : (u + 1) * P], ident[:])
+
+        def weave_w(b, engine):
+            hb[b] = hold([P, P, 4], BF16, "hb%d" % b)[:]
+            dst = hb[b].rearrange("p n t -> p (n t)").bitcast(F32).rearrange("p (n u) -> p n u", u=2)
+            src = turned[b][:, 0 : 2 * P].rearrange("p (u n) -> p n u", u=2)
+            if engine == "v":
+                nc.vector.tensor_copy(dst, src)
+            else:
+                nc.scalar.copy(dst, src)
 
         def quantise_h(b, pair=False):
             src = hb["pair", b][:] if pair else hb[b]
@@ -314,14 +353,12 @@ def tile_moe_pln_mlp_relu2_kernel(
         nc.sync.dma_start(offs_t[:], offs)
         zero_w1_scales(0, 2, nc.vector)
         zero_w1_scales(2, 4, nc.vector)
-        zero_words(T, 1408)
-        zero_words(1408 + T, 2112)
-        zero_words(2624 + T, XW)
+        zero_words(1536 + T, XW)
         nc.gpsimd.memset(xs[:].bitcast(I32), 0)
-        zero_low(1, 0, 8)
-        zero_low(2, 0, 4)
-        zero_low(2, 4, 8)
-        nc.gpsimd.memset(w2s[:].bitcast(I32), 0)
+        zero_low(1, 0, 8, nc.vector)
+        zero_low(2, 0, 4, nc.vector)
+        zero_low(2, 4, 8, nc.vector)
+        nc.vector.memset(w2s[:].bitcast(I32), 0)
         make_identity(nc, ident[:])
         load_x(1)
         load_x(2)
@@ -355,7 +392,7 @@ def tile_moe_pln_mlp_relu2_kernel(
         load_w1(2, 2, 4)
         words(3, 0, 4, 704)
         words(2, 0, 4, 1024)
-        words(1, 4, 8, 1728)
+        words(1, 4, 8, 704, "xb3")
         scales((2, 3), 4, 8, 704)
         lower(2, 4, 8, True)
         load_pos()
@@ -378,7 +415,7 @@ def tile_moe_pln_mlp_relu2_kernel(
         for b in (2, 3):
             turn(b)
             square(b)
-        words(2, 6, 8, T, "gw1_4")
+        words(2, 6, 8, T, "xb3")
         firsts((2,), (4, 5))
         firsts((3,), (6, 7))
         firsts((2,), (6, 7))

@@ -367,14 +367,16 @@ def tile_moe_pln_mlp_relu2_kernel(
         load_w1(0, 0, 2)
         load_w1_scales(2, 4)
         load_w1(0, 2, 4)
-        cast(0, 0, 320, "v")
-        cast(0, 320, T, "s")
+        cast(0, 0, 352, "v")
+        cast(0, 352, T, "s")
         quantise(0, 0, 256)
         quantise(0, 256, T)
         words(0, 0, 8, 1408)
-        cast(1, 0, 64, "v")
-        cast(1, 64, T, "s")
-        quantise(1)
+        cast(1, 0, 256, "s")
+        cast(1, 256, 448, "s")
+        cast(1, 448, T, "v")
+        quantise(1, 0, 256)
+        quantise(1, 256, T)
         scales((0, 1), 0, 8, 1408)
         lower(1, 0, 8)
         load_w1(1, 0, 2)
@@ -404,60 +406,50 @@ def tile_moe_pln_mlp_relu2_kernel(
         for b in range(4):
             first(2, b)
             rectify(b, "s")
-        for b in (0, 1):
-            turn(b)
-            square(b)
-        words(3, 4, 6, T, "gw2_0")
-        words(2, 4, 6, T, "r0")
-        words(3, 6, 8, T, "r1")
         firsts((1,), range(4, 8))
-        firsts((3,), (4, 5))
-        for b in (2, 3):
+        for b in range(4):
             turn(b)
             square(b)
+        words(3, 4, 8, 704, "gw2_0")
+        words(2, 4, 6, T, "r0")
         words(2, 6, 8, T, "xb3")
-        firsts((2,), (4, 5))
-        firsts((3,), (6, 7))
-        firsts((2,), (6, 7))
+        firsts((3, 2), range(4, 8))
         for b in range(3):
             quantise_h(b)
-        rectify(4, "v")
-        rectify(5, "s")
         quantise_h(3)
+        rectify(4, "s")
+        rectify(5, "v")
         rectify(6, "v")
         rectify(7, "s")
         for b in range(4, 8):
             turn(b)
-        square_v(4)
-        square(5)
+        square(4)
+        square_v(5)
         square(6)
         square(7)
         result(0, 0, 512, 0, "s")
         second(1, 0, 512, 1)
-        for b in (4, 5):
+        for b in (4, 6, 5):
             quantise_h(b)
-        second(0, 512, 768, 2)
-        quantise_h(6)
-        second(0, 768, 896, 3, 128)
-        fetch(0, 512, 768, "v")
+        second(0, 512, 896, 2, 128)
         quantise_h(7)
         second(0, 896, 1024, 4, 128)
-        fetch(0, 768, 896, "v")
+        fetch(0, 512, 896, "s")
         fetch(0, 896, 1024, "v")
         fetch(1, 0, 512, "s")
         result(1, 512, 1024, 5, "s")
-        result(2, 0, 512, 3, "s")
+        result(2, 0, 512, 2, "s")
         result(2, 512, 1024, 7, "s")
         term(0, 0, 0, T)
         term(0, 1, 0, T)
         add_turned(0, 0, 256, 4, 6)
-        add_turned(0, 256, T, 0, 2)
+        add_turned(0, 256, T, 0, 3)
         term(1, 0, 0, T)
         term(1, 1, 0, T)
         add_turned(1, 0, 256, 6, 4)
         term(2, 0, 0, T)
-        term(2, 1, 0, 384)
         add(1, 256, T)
-        add(2, 0, 384)
-        term(2, 1, 384, T)
-        add(2, 384, T)
+        term(2, 1, 0, 256)
+        term(2, 1, 256, T)
+        add(2, 0, 256)
+        add(2, 256, T)

@@ -309,11 +309,12 @@ def tile_moe_pln_mlp_relu2_kernel(
 
         terms = {}
 
-        def term(j, i, lo, hi):
-            terms[j, i, lo] = hold([P, hi - lo], F32, "term%d%d_%d" % (j, i, lo))
-            nc.vector.tensor_tensor(
-                terms[j, i, lo][:], y[j][:].indirect((pos1_t, pos2_t)[i][:, lo // 16 : hi // 16]), g[:, i, lo:hi], MULT
-            )
+        def term(j, i, lo, hi, tag=None, cuts=None):
+            terms[j, i, lo] = hold([P, hi - lo], F32, "term%d%d_%d" % (j, i, lo), tag)
+            for a, b in cuts or ((lo, hi),):
+                nc.vector.tensor_tensor(
+                    terms[j, i, lo][:, a - lo : b - lo], y[j][:].indirect((pos1_t, pos2_t)[i][:, a // 16 : b // 16]), g[:, i, a:b], MULT
+                )
 
         def part(j, i, lo, hi):
             base = max(a for r, c, a in terms if (r, c) == (j, i) and a <= lo)
@@ -326,11 +327,11 @@ def tile_moe_pln_mlp_relu2_kernel(
 
         def add_turned(j, lo, hi, b1, b2, queue=None):
             n = hi - lo
-            across = bank(b1)
+            both = bank(b1)
             for c in range(n // P):
                 for i in (1, 0):
                     nc.tensor.matmul(
-                        across[:, c * P : (c + 1) * P],
+                        both[:, c * P : (c + 1) * P],
                         lhsT=part(j, i, lo + c * P, lo + (c + 1) * P),
                         rhs=ident[:],
                         is_transpose=True,
@@ -338,8 +339,35 @@ def tile_moe_pln_mlp_relu2_kernel(
                         stop=(i == 0),
                     )
             total = hold([P, n], F32, "total%d_%d" % (j, lo))
-            nc.scalar.copy(total[:], across[:, 0:n])
+            nc.scalar.copy(total[:], both[:, 0:n])
             back = bank(b2)
+            for c in range(n // P):
+                nc.tensor.transpose(back[:, c * P : (c + 1) * P], total[:, c * P : (c + 1) * P], ident[:])
+            summed = hold([P, n], F32, "summed%d_%d" % (j, lo))
+            nc.scalar.copy(summed[:], back[:, 0:n])
+            (queue or nc.scalar).dma_start(out=out[j * P : (j + 1) * P, lo:hi], in_=summed[:])
+
+        across = {}
+
+        def turn_term(j, i, banks):
+            for c in range(T // P):
+                if i == 0:
+                    across[j, c] = bank(banks[c])
+                nc.tensor.matmul(
+                    across[j, c][:, 0:P],
+                    lhsT=part(j, i, c * P, (c + 1) * P),
+                    rhs=ident[:],
+                    is_transpose=True,
+                    start=(i == 0),
+                    stop=(i == 1),
+                )
+
+        def turn_back(j, lo, hi, b, queue=None):
+            n = hi - lo
+            total = hold([P, n], F32, "total%d_%d" % (j, lo))
+            back = bank(b)
+            for c in range(n // P):
+                nc.scalar.copy(total[:, c * P : (c + 1) * P], across[j, lo // P + c][:, 0:P])
             for c in range(n // P):
                 nc.tensor.transpose(back[:, c * P : (c + 1) * P], total[:, c * P : (c + 1) * P], ident[:])
             summed = hold([P, n], F32, "summed%d_%d" % (j, lo))
@@ -363,8 +391,8 @@ def tile_moe_pln_mlp_relu2_kernel(
         load_x(1)
         load_x(2)
         load_x(3)
-        load_w1_scales(0, 2)
         load_w1(0, 0, 2)
+        load_w1_scales(0, 2)
         load_w1_scales(2, 4)
         load_w1(0, 2, 4)
         cast(0, 0, 352, "v")
@@ -441,15 +469,17 @@ def tile_moe_pln_mlp_relu2_kernel(
         result(2, 0, 512, 2, "s")
         result(2, 512, 1024, 7, "s")
         term(0, 0, 0, T)
+        turn_term(0, 0, (4, 6, 0, 3))
         term(0, 1, 0, T)
-        add_turned(0, 0, 256, 4, 6)
-        add_turned(0, 256, T, 0, 3)
+        turn_term(0, 1, None)
+        turn_back(0, 0, T, 1, nc.sync)
         term(1, 0, 0, T)
-        term(1, 1, 0, T)
-        add_turned(1, 0, 256, 6, 4)
-        term(2, 0, 0, T)
-        add(1, 256, T)
-        term(2, 1, 0, 256)
-        term(2, 1, 256, T)
+        turn_term(1, 0, (4, 6, 0, 3))
+        term(1, 1, 0, T, "term01_0")
+        turn_term(1, 1, None)
+        turn_back(1, 0, 256, 5)
+        turn_back(1, 256, T, 7)
+        term(2, 0, 0, T, "total0_0")
+        term(2, 1, 0, T, "term10_0", ((0, 256), (256, T)))
         add(2, 0, 256)
         add(2, 256, T)

@@ -203,6 +203,20 @@ def tile_moe_pln_mlp_relu2_kernel(
                 stop=(done[b] == PASSES),
             )
 
+        def warm(n, b):
+            spare = bank(b)
+            rows, base = gs[0, 0]
+            for i in range(n):
+                nc.tensor.matmul_mx(
+                    out=spare[:],
+                    lhsT=gw[0, i].bitcast(FP8X4),
+                    lhsT_scale=rows[:, i * P : (i + 1) * P],
+                    rhs=w1w[0, 0].bitcast(FP4X4),
+                    rhs_scale=rows[:, 0:H],
+                    start=True,
+                    stop=True,
+                )
+
         def firsts(which, blocks):
             for s in which:
                 for b in blocks:
@@ -283,9 +297,9 @@ def tile_moe_pln_mlp_relu2_kernel(
 
         sums = {}
 
-        def second(j, lo, hi, b, width=C):
+        def second(j, lo, hi, b, width=C, forward=False):
             sums[j, lo] = bank(b)
-            for at in reversed(range(lo, hi, width)):
+            for at in range(lo, hi, width) if forward else reversed(range(lo, hi, width)):
                 w = at // C * N + j * P
                 nc.tensor.matmul_mx(
                     out=sums[j, lo][:, at - lo : at - lo + width],
@@ -296,6 +310,18 @@ def tile_moe_pln_mlp_relu2_kernel(
                     start=True,
                     stop=True,
                 )
+
+        def more(j, lo, at, width):
+            w = at // C * N + j * P
+            nc.tensor.matmul_mx(
+                out=sums[j, lo][:, at - lo : at - lo + width],
+                lhsT=w2w[:, 2 * w : 2 * (w + P)].bitcast(FP4X4),
+                lhsT_scale=w2s[:, w : w + P],
+                rhs=hw[:, at : at + width].bitcast(FP8X4),
+                rhs_scale=hs[:, at : at + width],
+                start=True,
+                stop=True,
+            )
 
         def fetch(j, lo, hi, engine):
             if engine == "v":
@@ -412,8 +438,9 @@ def tile_moe_pln_mlp_relu2_kernel(
         load_w1(2, 0, 2)
         cast(2, 0, T, "s")
         quantise(2)
+        cast(3, 0, 448, "s")
+        cast(3, 448, T, "v")
         words(1, 0, 4, 704, "raw2_0")
-        cast(3, 0, T, "s")
         quantise(3)
         scales((2, 3), 0, 4, 704)
         lower(2, 0, 4, True)
@@ -439,9 +466,10 @@ def tile_moe_pln_mlp_relu2_kernel(
             turn(b)
             square(b)
         words(3, 4, 8, 704, "gw2_0")
-        words(2, 4, 6, T, "r0")
-        words(2, 6, 8, T, "xb3")
-        firsts((3, 2), range(4, 8))
+        words(2, 4, 6, T, "xb3")
+        words(2, 6, 8, T, "r0")
+        firsts((3, 2), (4, 5))
+        firsts((3, 2), (6, 7))
         for b in range(3):
             quantise_h(b)
         quantise_h(3)
@@ -457,13 +485,17 @@ def tile_moe_pln_mlp_relu2_kernel(
         square(7)
         result(0, 0, 512, 0, "s")
         second(1, 0, 512, 1)
-        for b in (4, 6, 5):
-            quantise_h(b)
-        second(0, 512, 896, 2, 128)
+        quantise_h(4)
+        second(0, 512, 640, 2, 128)
+        quantise_h(6)
+        second(0, 768, 896, 3, 128)
+        quantise_h(5)
+        more(0, 512, 640, 128)
         quantise_h(7)
         second(0, 896, 1024, 4, 128)
-        fetch(0, 512, 896, "s")
-        fetch(0, 896, 1024, "v")
+        fetch(0, 768, 896, "s")
+        fetch(0, 512, 768, "v")
+        fetch(0, 896, 1024, "s")
         fetch(1, 0, 512, "s")
         result(1, 512, 1024, 5, "s")
         result(2, 0, 512, 2, "s")

@@ -38,7 +38,7 @@ def tile_moe_pln_mlp_relu2_kernel(
         psum = ctx.enter_context(tc.psum_pool(name="psum", bufs=1))
 
         def hold(shape, dtype, name, tag=None):
-            return keep.tile(shape, dtype, name=name, tag=tag or name, align_bytes=64)
+            return keep.tile(shape, dtype, name=name, tag=tag or name, align_bytes=256)
 
         def bank(b):
             return psum.tile([P, H], F32, name="bank%d" % b)

@@ -105,6 +105,26 @@ def tile_moe_pln_mlp_relu2_kernel(
                     in_=w1s_v[lo:hi, :, r:16:4, :].rearrange("e s q b -> q (e s) b"),
                 )
 
+        cut = {}
+
+        def zero_cut(name, es, ss):
+            plane = hold([P, len(es) * len(ss) * H], U8, name)
+            nc.vector.memset(plane[:].bitcast(I32), 0)
+            for i, e in enumerate(es):
+                for k, s in enumerate(ss):
+                    at = (i * len(ss) + k) * H
+                    cut[e, s] = plane[:, at : at + H]
+            cut[name] = plane
+
+        def load_cut(name, es, ss):
+            for r in range(4):
+                nc.sync.dma_start(
+                    out=cut[name][r:P:32, :].bitcast(I32).rearrange("p (a b) -> p a b", b=H // 4),
+                    in_=w1s_v[es[0] : es[-1] + 1, ss[0] : ss[-1] + 1, r:16:4, :].rearrange("e s q b -> q (e s) b")
+                    if len(es) == 1 or len(ss) == PASSES
+                    else w1s_v[es[0] : es[-1] + 1, ss[0], r:16:4, :].rearrange("e q b -> q e b"),
+                )
+
         def load_w2():
             nc.sync.dma_start(
                 out=w2w[:].bitcast(I32).rearrange("p (e b) -> p e b", e=E),
@@ -190,8 +210,11 @@ def tile_moe_pln_mlp_relu2_kernel(
             done[b] = done.get(b, 0) + 1
             if done[b] == 1:
                 acc[b] = bank(b)
-            plane, e0 = w1s[e]
-            w = ((e - e0) * PASSES + s) * H
+            if (e, s) in cut:
+                plane, w = cut[e, s], 0
+            else:
+                plane, e0 = w1s[e]
+                w = ((e - e0) * PASSES + s) * H
             rows, base = gs[s, b]
             nc.tensor.matmul_mx(
                 out=acc[b][:],
@@ -420,7 +443,9 @@ def tile_moe_pln_mlp_relu2_kernel(
         load_w1(0, 0, 2)
         load_w1_scales(0, 2)
         load_w1_scales(2, 4)
-        load_w1(0, 2, 4)
+        load_w1(0, 2, 3)
+        load_w1(0, 3, 4)
+        load_w1(1, 0, 2)
         cast(0, 0, 352, "v")
         cast(0, 352, T, "s")
         quantise(0, 0, 256)
@@ -433,7 +458,6 @@ def tile_moe_pln_mlp_relu2_kernel(
         quantise(1, 256, T)
         scales((0, 1), 0, 8, 1408)
         lower(1, 0, 8)
-        load_w1(1, 0, 2)
         load_w1(3, 0, 2)
         load_w1(2, 0, 2)
         cast(2, 0, T, "s")

@@ -175,6 +175,14 @@ def tile_moe_pln_mlp_relu2_kernel(
             for b in range(lo, hi):
                 gw[s, b] = codes[:, (b - lo) * P : (b - lo + 1) * P]
 
+        def words_into(codes, s, base, lo, hi, reach):
+            nc.vector.tensor_copy(
+                codes[:, (lo - base) * P : (hi - base) * P],
+                xw[:, WORDS_AT[s] : WORDS_AT[s] + reach].indirect(offs_t[:, lo * 8 : hi * 8]),
+            )
+            for b in range(lo, hi):
+                gw[s, b] = codes[:, (b - base) * P : (b - base + 1) * P]
+
         def scales(passes, lo, hi, reach, tag=None):
             n = (hi - lo) * P
             at = PLANE_AT[passes[0]]
@@ -432,7 +440,8 @@ def tile_moe_pln_mlp_relu2_kernel(
         zero_w1_scales(2, 4, nc.vector)
         zero_words(1536 + T, XW)
         nc.gpsimd.memset(xs[:].bitcast(I32), 0)
-        zero_low(1, 0, 8, nc.vector)
+        zero_low(1, 0, 4, nc.vector)
+        zero_low(1, 4, 8, nc.vector)
         zero_low(2, 0, 4, nc.vector)
         zero_low(2, 4, 8, nc.vector)
         nc.vector.memset(w2s[:].bitcast(I32), 0)
@@ -457,9 +466,10 @@ def tile_moe_pln_mlp_relu2_kernel(
         quantise(1, 0, 256)
         quantise(1, 256, T)
         scales((0, 1), 0, 8, 1408)
-        lower(1, 0, 8)
+        lower(1, 0, 4)
         load_w1(3, 0, 2)
         load_w1(2, 0, 2)
+        lower(1, 4, 8)
         cast(2, 0, T, "s")
         quantise(2)
         cast(3, 0, 448, "s")
@@ -492,8 +502,10 @@ def tile_moe_pln_mlp_relu2_kernel(
         words(3, 4, 8, 704, "gw2_0")
         words(2, 4, 6, T, "xb3")
         words(2, 6, 8, T, "r0")
-        firsts((3, 2), (4, 5))
-        firsts((3, 2), (6, 7))
+        firsts((3,), (4, 5, 6))
+        firsts((2,), (4, 5))
+        firsts((3,), (7,))
+        firsts((2,), (6, 7))
         for b in range(3):
             quantise_h(b)
         quantise_h(3)

@@ -472,10 +472,11 @@ def tile_moe_pln_mlp_relu2_kernel(
         lower(1, 4, 8)
         cast(2, 0, T, "s")
         quantise(2)
-        cast(3, 0, 448, "s")
-        cast(3, 448, T, "v")
         words(1, 0, 4, 704, "raw2_0")
-        quantise(3)
+        cast(3, 0, 256, "s")
+        cast(3, 256, T, "s")
+        quantise(3, 0, 256)
+        quantise(3, 256, T)
         scales((2, 3), 0, 4, 704)
         lower(2, 0, 4, True)
         load_w1(1, 2, 4)

@@ -201,7 +201,10 @@ def tile_moe_pln_mlp_relu2_kernel(
             rows, base = gs[s, lo]
             cols = slice((lo - base) * P, (hi - base) * P)
             k = LIFT[s]
-            if four:
+            if four == 3:
+                for a, n in ((0, 32), (32, 64), (96, 16)):
+                    queue.dma_start(out=low[s, lo][a : a + n, :].bitcast(I32), in_=rows[k + a : k + a + n, cols].bitcast(I32))
+            elif four:
                 for r in range(4):
                     queue.dma_start(out=low[s, lo][r:P:32, :].bitcast(I32), in_=rows[k + r : P : 32, cols].bitcast(I32))
             else:
@@ -283,7 +286,7 @@ def tile_moe_pln_mlp_relu2_kernel(
             kept = hold([P, P, 4], F32, "kept%d" % b)
             nc.vector.tensor_copy(kept[:], turned[b][:].rearrange("p (t n) -> p n t", t=4))
             hb[b] = hold([P, P, 4], BF16, "hb%d" % b)[:]
-            nc.vector.tensor_tensor(hb[b], kept[:], kept[:], MULT)
+            nc.vector.tensor_tensor(hb[b], turned[b][:].rearrange("p (t n) -> p n t", t=4), kept[:], MULT)
 
         paired = {}
 

@@ -202,7 +202,7 @@ def tile_moe_pln_mlp_relu2_kernel(
             cols = slice((lo - base) * P, (hi - base) * P)
             k = LIFT[s]
             if four == 3:
-                for a, n in ((0, 32), (32, 64), (96, 16)):
+                for a, n in ((0, 4), (32, 64), (96, 4)):
                     queue.dma_start(out=low[s, lo][a : a + n, :].bitcast(I32), in_=rows[k + a : k + a + n, cols].bitcast(I32))
             elif four:
                 for r in range(4):
@@ -363,6 +363,12 @@ def tile_moe_pln_mlp_relu2_kernel(
             else:
                 nc.scalar.copy(y[j][:, lo:hi], sums[j, lo][:, 0 : hi - lo])
 
+        def fetch2(j, base, lo, hi, engine):
+            if engine == "v":
+                nc.vector.tensor_copy(y[j][:, lo:hi], sums[j, base][:, lo - base : hi - base])
+            else:
+                nc.scalar.copy(y[j][:, lo:hi], sums[j, base][:, lo - base : hi - base])
+
         def result(j, lo, hi, b, engine, width=C):
             second(j, lo, hi, b, width)
             fetch(j, lo, hi, engine)
@@ -409,8 +415,8 @@ def tile_moe_pln_mlp_relu2_kernel(
 
         across = {}
 
-        def turn_term(j, i, banks):
-            for c in range(T // P):
+        def turn_term(j, i, banks, lo=0, hi=T):
+            for c in range(lo // P, hi // P):
                 if i == 0:
                     across[j, c] = bank(banks[c])
                 nc.tensor.matmul(
@@ -443,8 +449,7 @@ def tile_moe_pln_mlp_relu2_kernel(
         zero_w1_scales(2, 4, nc.vector)
         zero_words(1536 + T, XW)
         nc.gpsimd.memset(xs[:].bitcast(I32), 0)
-        zero_low(1, 0, 4, nc.vector)
-        zero_low(1, 4, 8, nc.vector)
+        zero_low(1, 0, 8, nc.vector)
         zero_low(2, 0, 4, nc.vector)
         zero_low(2, 4, 8, nc.vector)
         nc.vector.memset(w2s[:].bitcast(I32), 0)
@@ -455,10 +460,9 @@ def tile_moe_pln_mlp_relu2_kernel(
         load_w1(0, 0, 2)
         load_w1_scales(0, 2)
         load_w1_scales(2, 4)
-        load_w1(0, 2, 3)
-        load_w1(0, 3, 4)
-        load_w1(1, 0, 2)
-        cast(0, 0, 352, "v")
+        load_w1(0, 2, 4)
+        cast(0, 0, 256, "v")
+        cast(0, 256, 352, "v")
         cast(0, 352, T, "s")
         quantise(0, 0, 256)
         quantise(0, 256, T)
@@ -469,10 +473,10 @@ def tile_moe_pln_mlp_relu2_kernel(
         quantise(1, 0, 256)
         quantise(1, 256, T)
         scales((0, 1), 0, 8, 1408)
-        lower(1, 0, 4)
+        lower(1, 0, 8)
+        load_w1(1, 0, 2)
         load_w1(3, 0, 2)
         load_w1(2, 0, 2)
-        lower(1, 4, 8)
         cast(2, 0, T, "s")
         quantise(2)
         words(1, 0, 4, 704, "raw2_0")
@@ -481,7 +485,7 @@ def tile_moe_pln_mlp_relu2_kernel(
         quantise(3, 0, 256)
         quantise(3, 256, T)
         scales((2, 3), 0, 4, 704)
-        lower(2, 0, 4, True)
+        lower(2, 0, 4, 3)
         load_w1(1, 2, 4)
         load_w1(3, 2, 4)
         load_w1(2, 2, 4)
@@ -489,7 +493,7 @@ def tile_moe_pln_mlp_relu2_kernel(
         words(2, 0, 4, 1024)
         words(1, 4, 8, 704, "xb3")
         scales((2, 3), 4, 8, 704)
-        lower(2, 4, 8, True)
+        lower(2, 4, 8, 3)
         load_pos()
         load_w2()
         load_w2_scales()
@@ -547,11 +551,12 @@ def tile_moe_pln_mlp_relu2_kernel(
         turn_back(0, 0, T, 1, nc.sync)
         term(1, 0, 0, T)
         turn_term(1, 0, (4, 6, 0, 3))
-        term(1, 1, 0, T, "term01_0")
-        turn_term(1, 1, None)
+        term(1, 1, 0, T, "term00_0", ((0, 256), (256, T)))
+        turn_term(1, 1, None, 0, 256)
         turn_back(1, 0, 256, 5)
+        turn_term(1, 1, None, 256, T)
         turn_back(1, 256, T, 7)
-        term(2, 0, 0, T, "total0_0")
+        term(2, 0, 0, T, "term01_0")
         term(2, 1, 0, T, "term10_0", ((0, 256), (256, T)))
         add(2, 0, 256)
         add(2, 256, T)

@@ -19,9 +19,10 @@ FP8X4 = mybir.dt.float8_e4m3fn_x4
 FP4X4 = mybir.dt.float4_e2m1fn_x4
 RELU = mybir.ActivationFunctionType.Relu
 SQUARE = mybir.ActivationFunctionType.Square
+COPY = mybir.ActivationFunctionType.Copy
 MULT = mybir.AluOpType.mult
 ADD = mybir.AluOpType.add
-WORDS_AT = (1536, 1024, 0, 512)
+WORDS_AT = (1536, 0, 512, 1024)
 XW = 1536 + 1408
 PLANE_AT = (512, 512, 0, 0)
 XS = 512 + 1408
@@ -44,8 +45,7 @@ def tile_moe_pln_mlp_relu2_kernel(
             return psum.tile([P, H], F32, name="bank%d" % b)
 
         offs_t = lists.tile([P, SLOTS // 16], U16, name="offs_t")
-        pos1_t = lists.tile([P, T // 16], U16, name="pos1_t")
-        pos2_t = lists.tile([P, T // 16], U16, name="pos2_t")
+        pos_t = [lists.tile([P, T // 16], U16, name="pos%d_t" % i) for i in range(2)]
 
         xT_v = xT.rearrange("(s p j) t -> s p j t", p=P, j=4)
         w1w_v = w1_words.bitcast(I32)
@@ -53,15 +53,10 @@ def tile_moe_pln_mlp_relu2_kernel(
         w2w_v = w2_words.bitcast(I32)
         w2s_v = w2_scales.bitcast(I32)
 
-        raw = {}
+        raw = [hold([P, 4, T], F32, "raw%d" % s) for s in range(PASSES)]
         xb = [hold([P, T, 4], BF16, "xb%d" % s) for s in range(PASSES)]
         xw = hold([P, XW], U32, "xw")
         xs = hold([P, XS], U8, "xs")
-        gw = {}
-        gs = {}
-        low = {}
-        w1s = {}
-        w1w = {}
         hw = hold([P, SLOTS], U32, "hw")
         hs = hold([P, SLOTS], U8, "hs")
         y = [hold([P, SLOTS], F32, "y%d" % j) for j in range(N // P)]
@@ -69,10 +64,11 @@ def tile_moe_pln_mlp_relu2_kernel(
         w2s = hold([P, E * N], U8, "w2s")
         w2w = hold([P, E * 2 * N], U8, "w2w")
         g = hold([P, 2, T], F32, "g")
+        gcol = hold([P, T // P], F32, "gcol")
+        gw, gs, w1w, w1s = {}, {}, {}, {}
 
-        def load_x(s, lo=0, hi=T):
-            raw[s, lo] = hold([P, 4, hi - lo], F32, "raw%d_%d" % (s, lo))
-            nc.sync.dma_start(out=raw[s, lo][:], in_=xT_v[s][:, :, lo:hi])
+        def load_x(s):
+            nc.sync.dma_start(out=raw[s][:], in_=xT_v[s])
 
         def load_w1(s, lo, hi):
             words1 = hold([P, (hi - lo) * 2 * H], U8, "w1w%d%d" % (s, lo))
@@ -92,46 +88,23 @@ def tile_moe_pln_mlp_relu2_kernel(
             for s in range(lo, hi):
                 w1w[s, e] = words1[:, (s - lo) * 2 * H : (s - lo + 1) * 2 * H]
 
-        def zero_w1_scales(lo, hi, engine):
-            plane = hold([P, (hi - lo) * PASSES * H], U8, "w1s%d" % lo)
-            engine.memset(plane[:].bitcast(I32), 0)
-            for e in range(lo, hi):
-                w1s[e] = (plane, lo)
-
         def load_w1_scales(lo, hi):
+            plane = hold([P, (hi - lo) * PASSES * H], U8, "w1s%d" % lo)
             for r in range(4):
                 nc.sync.dma_start(
-                    out=w1s[lo][0][r:P:32, :].bitcast(I32).rearrange("p (a b) -> p a b", b=H // 4),
+                    out=plane[r:P:32, :].bitcast(I32).rearrange("p (a b) -> p a b", b=H // 4),
                     in_=w1s_v[lo:hi, :, r:16:4, :].rearrange("e s q b -> q (e s) b"),
                 )
-
-        cut = {}
-
-        def zero_cut(name, es, ss):
-            plane = hold([P, len(es) * len(ss) * H], U8, name)
-            nc.vector.memset(plane[:].bitcast(I32), 0)
-            for i, e in enumerate(es):
-                for k, s in enumerate(ss):
-                    at = (i * len(ss) + k) * H
-                    cut[e, s] = plane[:, at : at + H]
-            cut[name] = plane
-
-        def load_cut(name, es, ss):
-            for r in range(4):
-                nc.sync.dma_start(
-                    out=cut[name][r:P:32, :].bitcast(I32).rearrange("p (a b) -> p a b", b=H // 4),
-                    in_=w1s_v[es[0] : es[-1] + 1, ss[0] : ss[-1] + 1, r:16:4, :].rearrange("e s q b -> q (e s) b")
-                    if len(es) == 1 or len(ss) == PASSES
-                    else w1s_v[es[0] : es[-1] + 1, ss[0], r:16:4, :].rearrange("e q b -> q e b"),
-                )
+            for e in range(lo, hi):
+                for s in range(PASSES):
+                    at = ((e - lo) * PASSES + s) * H
+                    w1s[s, e] = plane[:, at : at + H]
 
         def load_w2():
             nc.sync.dma_start(
                 out=w2w[:].bitcast(I32).rearrange("p (e b) -> p e b", e=E),
                 in_=w2w_v[:, 0].rearrange("e p b -> p e b"),
             )
-
-        def load_w2_scales():
             for r in range(4):
                 nc.sync.dma_start(
                     out=w2s[r:P:32, :].bitcast(I32).rearrange("p (a b) -> p a b", b=N // 4),
@@ -140,121 +113,72 @@ def tile_moe_pln_mlp_relu2_kernel(
 
         def load_gate():
             nc.sync.dma_start(out=g[:], in_=gate[:, 0:P, :].rearrange("g p t -> p g t"))
+            with nc.allow_non_contiguous_dma(reason="one gate value a partition"):
+                nc.sync.dma_start(out=gcol[:], in_=gate[1, P, :].rearrange("(c p) -> p c", p=P))
 
         def load_pos():
-            nc.sync.dma_start(pos1_t[:], pos1)
-            nc.sync.dma_start(pos2_t[:], pos2)
+            nc.sync.dma_start(pos_t[0][:], pos1)
+            nc.sync.dma_start(pos_t[1][:], pos2)
 
-        own = {}
-
-        def rounded(s, lo, hi):
-            return own[s, lo][:] if (s, lo) in own else xb[s][:, lo:hi, :]
-
-        def cast(s, lo, hi, engine, tag=None):
-            base = max(a for r, a in raw if r == s and a <= lo)
-            if tag:
-                own[s, lo] = hold([P, hi - lo, 4], BF16, "own%d_%d" % (s, lo), tag)
-            dst = rounded(s, lo, hi).rearrange("p (c i) t -> p c t i", i=4)
-            src = raw[s, base][:, :, lo - base : hi - base].rearrange("p t (c i) -> p c t i", i=4)
-            if engine == "v":
+        def cast(s, lo, hi, engine):
+            dst = xb[s][:, lo:hi, :].rearrange("p (c i) t -> p c t i", i=4)
+            src = raw[s][:, :, lo:hi].rearrange("p t (c i) -> p c t i", i=4)
+            if engine == "s":
+                nc.scalar.copy(dst, src)
+            elif engine == "v":
                 nc.vector.tensor_copy(dst, src)
             else:
-                nc.scalar.copy(dst, src)
+                nc.gpsimd.tensor_copy(dst, src)
 
         def quantise(s, lo=0, hi=T):
             nc.vector.quantize_mx(
                 out=xw[:, WORDS_AT[s] + lo : WORDS_AT[s] + hi].bitcast(FP8X4),
                 scales=xs[LIFT[s] : P, PLANE_AT[s] + lo : PLANE_AT[s] + hi],
-                in_=rounded(s, lo, hi).rearrange("p c t -> p (c t)"),
+                in_=xb[s][:, lo:hi, :].rearrange("p c t -> p (c t)"),
             )
 
         def words(s, lo, hi, reach, tag=None):
-            n = (hi - lo) * P
-            codes = hold([P, n], U32, "gw%d_%d" % (s, lo), tag)
+            codes = hold([P, (hi - lo) * P], U32, "gw%d_%d" % (s, lo), tag)
             nc.vector.tensor_copy(codes[:], xw[:, WORDS_AT[s] : WORDS_AT[s] + reach].indirect(offs_t[:, lo * 8 : hi * 8]))
             for b in range(lo, hi):
                 gw[s, b] = codes[:, (b - lo) * P : (b - lo + 1) * P]
 
-        def words_into(codes, s, base, lo, hi, reach):
-            nc.vector.tensor_copy(
-                codes[:, (lo - base) * P : (hi - base) * P],
-                xw[:, WORDS_AT[s] : WORDS_AT[s] + reach].indirect(offs_t[:, lo * 8 : hi * 8]),
-            )
-            for b in range(lo, hi):
-                gw[s, b] = codes[:, (b - base) * P : (b - base + 1) * P]
-
         def scales(passes, lo, hi, reach, tag=None):
-            n = (hi - lo) * P
             at = PLANE_AT[passes[0]]
-            rows = hold([P, n], U8, "gs%d_%d" % (passes[0], lo), tag)
+            rows = hold([P, (hi - lo) * P], U8, "gs%d_%d" % (passes[0], lo), tag)
             nc.vector.tensor_copy(rows[:], xs[:, at : at + reach].indirect(offs_t[:, lo * 8 : hi * 8]))
             for s in passes:
                 for b in range(lo, hi):
                     gs[s, b] = (rows, lo)
 
-        def zero_low(s, lo, hi, engine=nc.gpsimd):
-            low[s, lo] = hold([P, (hi - lo) * P], U8, "low%d_%d" % (s, lo))
-            engine.memset(low[s, lo][:].bitcast(I32), 0)
-
-        def lower(s, lo, hi, four=False, queue=None):
-            queue = queue or nc.sync
+        def lower(s, lo, hi, pieces):
             rows, base = gs[s, lo]
+            low = hold([P, (hi - lo) * P], U8, "low%d_%d" % (s, lo))
             cols = slice((lo - base) * P, (hi - base) * P)
-            k = LIFT[s]
-            if four == 3:
-                for a, n in ((0, 4), (32, 64), (96, 4)):
-                    queue.dma_start(out=low[s, lo][a : a + n, :].bitcast(I32), in_=rows[k + a : k + a + n, cols].bitcast(I32))
-            elif four:
-                for r in range(4):
-                    queue.dma_start(out=low[s, lo][r:P:32, :].bitcast(I32), in_=rows[k + r : P : 32, cols].bitcast(I32))
-            else:
-                queue.dma_start(out=low[s, lo][0:112, :].bitcast(I32), in_=rows[k : k + 112, cols].bitcast(I32))
+            for a, n in pieces:
+                nc.sync.dma_start(out=low[a : a + n, :].bitcast(I32), in_=rows[LIFT[s] + a : LIFT[s] + a + n, cols].bitcast(I32))
             for b in range(lo, hi):
-                gs[s, b] = (low[s, lo], lo)
+                gs[s, b] = (low, lo)
 
-        acc = {}
-        relu = {}
-        done = {}
+        one = ((0, 112),)
+        three = ((0, 4), (32, 64), (96, 4))
+        acc, done, relu, turned, hb, sums, terms = {}, {}, {}, {}, {}, {}, {}
 
-        def first(s, b):
-            e = b // 2
-            done[b] = done.get(b, 0) + 1
-            if done[b] == 1:
-                acc[b] = bank(b)
-            if (e, s) in cut:
-                plane, w = cut[e, s], 0
-            else:
-                plane, e0 = w1s[e]
-                w = ((e - e0) * PASSES + s) * H
-            rows, base = gs[s, b]
-            nc.tensor.matmul_mx(
-                out=acc[b][:],
-                lhsT=gw[s, b].bitcast(FP8X4),
-                lhsT_scale=rows[:, (b - base) * P : (b - base + 1) * P],
-                rhs=w1w[s, e].bitcast(FP4X4),
-                rhs_scale=plane[:, w : w + H],
-                start=(done[b] == 1),
-                stop=(done[b] == PASSES),
-            )
-
-        def warm(n, b):
-            spare = bank(b)
-            rows, base = gs[0, 0]
-            for i in range(n):
+        def first(s, blocks):
+            for b in blocks:
+                done[b] = done.get(b, 0) + 1
+                if done[b] == 1:
+                    acc[b] = bank(b)
+                rows, base = gs[s, b]
                 nc.tensor.matmul_mx(
-                    out=spare[:],
-                    lhsT=gw[0, i].bitcast(FP8X4),
-                    lhsT_scale=rows[:, i * P : (i + 1) * P],
-                    rhs=w1w[0, 0].bitcast(FP4X4),
-                    rhs_scale=rows[:, 0:H],
-                    start=True,
-                    stop=True,
+                    out=acc[b][:],
+                    lhsT=gw[s, b].bitcast(FP8X4),
+                    lhsT_scale=rows[:, (b - base) * P : (b - base + 1) * P],
+                    rhs=w1w[s, b // 2].bitcast(FP4X4),
+                    rhs_scale=w1s[s, b // 2],
+                    start=(done[b] == 1),
+                    stop=(done[b] == PASSES),
                 )
-
-        def firsts(which, blocks):
-            for s in which:
-                for b in blocks:
-                    first(s, b)
 
         def rectify(b, engine):
             relu[b] = hold([P, 4, P], F32, "r%d" % b)
@@ -264,76 +188,31 @@ def tile_moe_pln_mlp_relu2_kernel(
             else:
                 nc.scalar.activation(relu[b][:], lanes, RELU)
 
-        turned = {}
-
-        def turn(b, into=None):
-            turned[b] = bank(b if into is None else into)
+        def turn(b):
+            turned[b] = bank(b)
             for t in range(4):
                 nc.tensor.transpose(turned[b][:, t * P : (t + 1) * P], relu[b][:, t, :], ident[:])
 
-        hb = {}
-
-        def square(b, pair=None):
-            if pair is None:
-                hb[b] = hold([P, P, 4], BF16, "hb%d" % b)[:]
+        def square(b, engine="s"):
+            hb[b] = hold([P, P, 4], BF16, "hb%d" % b)
+            src = turned[b][:].rearrange("p (t n) -> p n t", t=4)
+            if engine == "s":
+                nc.scalar.activation(hb[b][:], src, SQUARE)
             else:
-                if b % 2 == 0:
-                    hb["pair", b] = hold([P, 2 * P, 4], BF16, "hb%d" % b)
-                hb[b] = hb["pair", b - b % 2][:, b % 2 * P : (b % 2 + 1) * P, :]
-            nc.scalar.activation(hb[b], turned[b][:].rearrange("p (t n) -> p n t", t=4), SQUARE)
+                kept = hold([P, P, 4], F32, "kept%d" % b)
+                nc.vector.tensor_copy(kept[:], src)
+                nc.vector.tensor_tensor(hb[b][:], src, kept[:], MULT)
 
-        def square_v(b):
-            kept = hold([P, P, 4], F32, "kept%d" % b)
-            nc.vector.tensor_copy(kept[:], turned[b][:].rearrange("p (t n) -> p n t", t=4))
-            hb[b] = hold([P, P, 4], BF16, "hb%d" % b)[:]
-            nc.vector.tensor_tensor(hb[b], turned[b][:].rearrange("p (t n) -> p n t", t=4), kept[:], MULT)
-
-        paired = {}
-
-        def rectify_w(b, engine):
-            relu[b] = hold([P, 2, P, 2], F32, "r%d" % b)
-            lanes = acc[b][:].rearrange("p (m u e) -> p u m e", u=2, e=2)
-            if engine == "v":
-                nc.vector.tensor_scalar_max(relu[b][:], lanes, 0.0)
-            else:
-                nc.scalar.activation(relu[b][:], lanes, RELU)
-
-        def square_w(b, engine):
-            paired[b] = hold([P, H], BF16, "paired%d" % b)
-            flat = relu[b][:].rearrange("p u m e -> p (u m e)")
-            if engine == "v":
-                nc.vector.tensor_tensor(paired[b][:], flat, flat, MULT)
-            else:
-                nc.scalar.activation(paired[b][:], flat, SQUARE)
-
-        def turn_w(b, into=None):
-            turned[b] = bank(b if into is None else into)
-            for u in range(2):
-                nc.tensor.transpose(turned[b][:, u * P : (u + 1) * P], paired[b][:].bitcast(F32)[:, u * P : (u + 1) * P], ident[:])
-
-        def weave_w(b, engine):
-            hb[b] = hold([P, P, 4], BF16, "hb%d" % b)[:]
-            dst = hb[b].rearrange("p n t -> p (n t)").bitcast(F32).rearrange("p (n u) -> p n u", u=2)
-            src = turned[b][:, 0 : 2 * P].rearrange("p (u n) -> p n u", u=2)
-            if engine == "v":
-                nc.vector.tensor_copy(dst, src)
-            else:
-                nc.scalar.copy(dst, src)
-
-        def quantise_h(b, pair=False):
-            src = hb["pair", b][:] if pair else hb[b]
-            n = 2 if pair else 1
+        def quantise_h(b):
             nc.vector.quantize_mx(
-                out=hw[:, b * P : (b + n) * P].bitcast(FP8X4),
-                scales=hs[:, b * P : (b + n) * P],
-                in_=src.rearrange("p n t -> p (n t)"),
+                out=hw[:, b * P : (b + 1) * P].bitcast(FP8X4),
+                scales=hs[:, b * P : (b + 1) * P],
+                in_=hb[b][:].rearrange("p n t -> p (n t)"),
             )
 
-        sums = {}
-
-        def second(j, lo, hi, b, width=C, forward=False):
+        def second(j, lo, hi, b, width=C):
             sums[j, lo] = bank(b)
-            for at in range(lo, hi, width) if forward else reversed(range(lo, hi, width)):
+            for at in range(lo, hi, width):
                 w = at // C * N + j * P
                 nc.tensor.matmul_mx(
                     out=sums[j, lo][:, at - lo : at - lo + width],
@@ -345,118 +224,49 @@ def tile_moe_pln_mlp_relu2_kernel(
                     stop=True,
                 )
 
-        def more(j, lo, at, width):
-            w = at // C * N + j * P
-            nc.tensor.matmul_mx(
-                out=sums[j, lo][:, at - lo : at - lo + width],
-                lhsT=w2w[:, 2 * w : 2 * (w + P)].bitcast(FP4X4),
-                lhsT_scale=w2s[:, w : w + P],
-                rhs=hw[:, at : at + width].bitcast(FP8X4),
-                rhs_scale=hs[:, at : at + width],
-                start=True,
-                stop=True,
-            )
-
         def fetch(j, lo, hi, engine):
             if engine == "v":
                 nc.vector.tensor_copy(y[j][:, lo:hi], sums[j, lo][:, 0 : hi - lo])
             else:
                 nc.scalar.copy(y[j][:, lo:hi], sums[j, lo][:, 0 : hi - lo])
 
-        def fetch2(j, base, lo, hi, engine):
-            if engine == "v":
-                nc.vector.tensor_copy(y[j][:, lo:hi], sums[j, base][:, lo - base : hi - base])
-            else:
-                nc.scalar.copy(y[j][:, lo:hi], sums[j, base][:, lo - base : hi - base])
-
-        def result(j, lo, hi, b, engine, width=C):
-            second(j, lo, hi, b, width)
-            fetch(j, lo, hi, engine)
-
-        terms = {}
-
-        def term(j, i, lo, hi, tag=None, cuts=None):
+        def term(j, i, lo=0, hi=T, tag=None):
             terms[j, i, lo] = hold([P, hi - lo], F32, "term%d%d_%d" % (j, i, lo), tag)
-            for a, b in cuts or ((lo, hi),):
-                nc.vector.tensor_tensor(
-                    terms[j, i, lo][:, a - lo : b - lo], y[j][:].indirect((pos1_t, pos2_t)[i][:, a // 16 : b // 16]), g[:, i, a:b], MULT
-                )
+            nc.vector.tensor_tensor(terms[j, i, lo][:], y[j][:].indirect(pos_t[i][:, lo // 16 : hi // 16]), g[:, i, lo:hi], MULT)
 
         def part(j, i, lo, hi):
             base = max(a for r, c, a in terms if (r, c) == (j, i) and a <= lo)
             return terms[j, i, base][:, lo - base : hi - base]
 
-        def add(j, lo, hi, queue=None):
-            o = hold([P, hi - lo], F32, "o%d_%d" % (j, lo))
-            nc.vector.tensor_tensor(o[:], part(j, 0, lo, hi), part(j, 1, lo, hi), ADD)
-            (queue or nc.sync).dma_start(out=out[j * P : (j + 1) * P, lo:hi], in_=o[:])
+        def pick(j, lo=0, hi=T, tag=None):
+            terms[j, 2, lo] = hold([P, hi - lo], F32, "picked%d_%d" % (j, lo), tag)
+            nc.scalar.activation(terms[j, 2, lo][:], y[j][:].indirect(pos_t[1][:, lo // 16 : hi // 16]), COPY)
 
-        def add_turned(j, lo, hi, b1, b2, queue=None):
+        def weigh(j, lo, hi, b1, b2):
             n = hi - lo
-            both = bank(b1)
+            across = bank(b1)
             for c in range(n // P):
-                for i in (1, 0):
-                    nc.tensor.matmul(
-                        both[:, c * P : (c + 1) * P],
-                        lhsT=part(j, i, lo + c * P, lo + (c + 1) * P),
-                        rhs=ident[:],
-                        is_transpose=True,
-                        start=(i == 1),
-                        stop=(i == 0),
-                    )
-            total = hold([P, n], F32, "total%d_%d" % (j, lo))
-            nc.scalar.copy(total[:], both[:, 0:n])
+                nc.tensor.transpose(across[:, c * P : (c + 1) * P], part(j, 2, lo + c * P, lo + (c + 1) * P), ident[:])
+            weighed = hold([P, n], F32, "weighed%d_%d" % (j, lo))
+            for c in range(n // P):
+                at = lo // P + c
+                nc.scalar.activation(weighed[:, c * P : (c + 1) * P], across[:, c * P : (c + 1) * P], COPY, scale=gcol[:, at : at + 1])
             back = bank(b2)
             for c in range(n // P):
-                nc.tensor.transpose(back[:, c * P : (c + 1) * P], total[:, c * P : (c + 1) * P], ident[:])
-            summed = hold([P, n], F32, "summed%d_%d" % (j, lo))
-            nc.scalar.copy(summed[:], back[:, 0:n])
-            (queue or nc.scalar).dma_start(out=out[j * P : (j + 1) * P, lo:hi], in_=summed[:])
+                nc.tensor.transpose(back[:, c * P : (c + 1) * P], weighed[:, c * P : (c + 1) * P], ident[:])
+            terms[j, 1, lo] = back
 
-        across = {}
-
-        def turn_term(j, i, banks, lo=0, hi=T):
-            for c in range(lo // P, hi // P):
-                if i == 0:
-                    across[j, c] = bank(banks[c])
-                nc.tensor.matmul(
-                    across[j, c][:, 0:P],
-                    lhsT=part(j, i, c * P, (c + 1) * P),
-                    rhs=ident[:],
-                    is_transpose=True,
-                    start=(i == 0),
-                    stop=(i == 1),
-                )
-
-        def turn_back(j, lo, hi, b, queue=None):
-            n = hi - lo
-            total = hold([P, n], F32, "total%d_%d" % (j, lo))
-            back = bank(b)
-            for c in range(n // P):
-                nc.scalar.copy(total[:, c * P : (c + 1) * P], across[j, lo // P + c][:, 0:P])
-            for c in range(n // P):
-                nc.tensor.transpose(back[:, c * P : (c + 1) * P], total[:, c * P : (c + 1) * P], ident[:])
-            summed = hold([P, n], F32, "summed%d_%d" % (j, lo))
-            nc.scalar.copy(summed[:], back[:, 0:n])
-            (queue or nc.scalar).dma_start(out=out[j * P : (j + 1) * P, lo:hi], in_=summed[:])
-
-        def zero_words(lo, hi):
-            nc.vector.memset(xw[:, lo:hi].bitcast(I32), 0)
+        def add(j, lo=0, hi=T, queue=None):
+            o = hold([P, hi - lo], F32, "o%d_%d" % (j, lo))
+            nc.vector.tensor_tensor(o[:], part(j, 1, lo, hi), part(j, 0, lo, hi), ADD)
+            (queue or nc.sync).dma_start(out=out[j * P : (j + 1) * P, lo:hi], in_=o[:])
 
         load_x(0)
         nc.sync.dma_start(offs_t[:], offs)
-        zero_w1_scales(0, 2, nc.vector)
-        zero_w1_scales(2, 4, nc.vector)
-        zero_words(1536 + T, XW)
         nc.gpsimd.memset(xs[:].bitcast(I32), 0)
-        zero_low(1, 0, 8, nc.vector)
-        zero_low(2, 0, 4, nc.vector)
-        zero_low(2, 4, 8, nc.vector)
-        nc.vector.memset(w2s[:].bitcast(I32), 0)
         make_identity(nc, ident[:])
-        load_x(1)
-        load_x(2)
-        load_x(3)
+        for s in (1, 2, 3):
+            load_x(s)
         load_w1(0, 0, 2)
         load_w1_scales(0, 2)
         load_w1_scales(2, 4)
@@ -473,50 +283,48 @@ def tile_moe_pln_mlp_relu2_kernel(
         quantise(1, 0, 256)
         quantise(1, 256, T)
         scales((0, 1), 0, 8, 1408)
-        lower(1, 0, 8)
+        lower(1, 0, 8, one)
         load_w1(1, 0, 2)
         load_w1(3, 0, 2)
         load_w1(2, 0, 2)
         cast(2, 0, T, "s")
         quantise(2)
-        words(1, 0, 4, 704, "raw2_0")
+        words(1, 0, 4, 704)
         cast(3, 0, 256, "s")
         cast(3, 256, T, "s")
         quantise(3, 0, 256)
         quantise(3, 256, T)
         scales((2, 3), 0, 4, 704)
-        lower(2, 0, 4, 3)
-        load_w1(1, 2, 4)
-        load_w1(3, 2, 4)
-        load_w1(2, 2, 4)
+        lower(2, 0, 4, three)
+        load_w1e(2, 1, 4)
+        load_w1e(3, 1, 4)
         words(3, 0, 4, 704)
         words(2, 0, 4, 1024)
-        words(1, 4, 8, 704, "xb3")
+        words(1, 4, 8, 1536)
         scales((2, 3), 4, 8, 704)
-        lower(2, 4, 8, 3)
+        lower(2, 4, 8, three)
         load_pos()
         load_w2()
-        load_w2_scales()
         load_gate()
-        firsts((0,), range(8))
-        firsts((1, 3), range(4))
+        first(0, range(8))
+        first(1, range(4))
+        first(3, range(4))
         for b in range(4):
-            first(2, b)
+            first(2, (b,))
             rectify(b, "s")
-        firsts((1,), range(4, 8))
+        first(1, range(4, 8))
         for b in range(4):
             turn(b)
             square(b)
         words(3, 4, 8, 704, "gw2_0")
         words(2, 4, 6, T, "xb3")
         words(2, 6, 8, T, "r0")
-        firsts((3,), (4, 5, 6))
-        firsts((2,), (4, 5))
-        firsts((3,), (7,))
-        firsts((2,), (6, 7))
-        for b in range(3):
+        first(3, (4, 5, 6))
+        first(2, (4, 5))
+        first(3, (7,))
+        first(2, (6, 7))
+        for b in range(4):
             quantise_h(b)
-        quantise_h(3)
         rectify(4, "s")
         rectify(5, "v")
         rectify(6, "v")
@@ -524,39 +332,39 @@ def tile_moe_pln_mlp_relu2_kernel(
         for b in range(4, 8):
             turn(b)
         square(4)
-        square_v(5)
+        square(5, "v")
         square(6)
         square(7)
-        result(0, 0, 512, 0, "s")
+        second(0, 0, 512, 0)
+        fetch(0, 0, 512, "s")
         second(1, 0, 512, 1)
         quantise_h(4)
-        second(0, 512, 640, 2, 128)
         quantise_h(6)
         second(0, 768, 896, 3, 128)
         quantise_h(5)
-        more(0, 512, 640, 128)
+        second(0, 512, 768, 2, 128)
         quantise_h(7)
         second(0, 896, 1024, 4, 128)
         fetch(0, 768, 896, "s")
         fetch(0, 512, 768, "v")
         fetch(0, 896, 1024, "s")
         fetch(1, 0, 512, "s")
-        result(1, 512, 1024, 5, "s")
-        result(2, 0, 512, 2, "s")
-        result(2, 512, 1024, 7, "s")
-        term(0, 0, 0, T)
-        turn_term(0, 0, (4, 6, 0, 3))
-        term(0, 1, 0, T)
-        turn_term(0, 1, None)
-        turn_back(0, 0, T, 1, nc.sync)
-        term(1, 0, 0, T)
-        turn_term(1, 0, (4, 6, 0, 3))
-        term(1, 1, 0, T, "term00_0", ((0, 256), (256, T)))
-        turn_term(1, 1, None, 0, 256)
-        turn_back(1, 0, 256, 5)
-        turn_term(1, 1, None, 256, T)
-        turn_back(1, 256, T, 7)
-        term(2, 0, 0, T, "term01_0")
-        term(2, 1, 0, T, "term10_0", ((0, 256), (256, T)))
+        second(1, 512, 1024, 5)
+        fetch(1, 512, 1024, "s")
+        second(2, 0, 512, 2)
+        second(2, 512, 1024, 7)
+        term(0, 0)
+        fetch(2, 0, 512, "s")
+        fetch(2, 512, 1024, "v")
+        pick(0)
+        pick(2)
+        term(1, 0)
+        term(1, 1)
+        term(2, 0)
+        add(1)
+        weigh(0, 0, T, 0, 1)
+        weigh(2, 0, 256, 3, 4)
+        weigh(2, 256, T, 6, 5)
+        add(0)
         add(2, 0, 256)
         add(2, 256, T)

@@ -128,7 +128,7 @@ def tile_moe_pln_mlp_relu2_kernel(
             elif engine == "v":
                 nc.vector.tensor_copy(dst, src)
             else:
-                nc.gpsimd.tensor_copy(dst, src)
+                nc.gpsimd.tensor_copy(xb[s][:, lo:hi, :], raw[s][:, :, lo:hi].rearrange("p t c -> p c t"))
 
         def quantise(s, lo=0, hi=T):
             nc.vector.quantize_mx(
@@ -278,8 +278,8 @@ def tile_moe_pln_mlp_relu2_kernel(
         quantise(0, 256, T)
         words(0, 0, 8, 1408)
         cast(1, 0, 256, "s")
-        cast(1, 256, 448, "s")
-        cast(1, 448, T, "v")
+        cast(1, 256, 384, "s")
+        cast(1, 384, T, "g")
         quantise(1, 0, 256)
         quantise(1, 256, T)
         scales((0, 1), 0, 8, 1408)
@@ -287,11 +287,14 @@ def tile_moe_pln_mlp_relu2_kernel(
         load_w1(1, 0, 2)
         load_w1(3, 0, 2)
         load_w1(2, 0, 2)
-        cast(2, 0, T, "s")
+        cast(2, 0, 256, "s")
+        cast(2, 256, 384, "g")
+        cast(2, 384, T, "g")
         quantise(2)
         words(1, 0, 4, 704)
         cast(3, 0, 256, "s")
-        cast(3, 256, T, "s")
+        cast(3, 256, 384, "g")
+        cast(3, 384, T, "g")
         quantise(3, 0, 256)
         quantise(3, 256, T)
         scales((2, 3), 0, 4, 704)

@@ -57,7 +57,7 @@ def tile_moe_pln_mlp_relu2_kernel(
         xb = [hold([P, T, 4], BF16, "xb%d" % s) for s in range(PASSES)]
         xw = hold([P, XW], U32, "xw")
         xs = hold([P, XS], U8, "xs")
-        hw = hold([P, SLOTS], U32, "hw")
+        late = {}
         hs = hold([P, SLOTS], U8, "hs")
         y = [hold([P, SLOTS], F32, "y%d" % j) for j in range(N // P)]
         ident = hold([P, P], F32, "ident")
@@ -65,7 +65,7 @@ def tile_moe_pln_mlp_relu2_kernel(
         w2w = hold([P, E * 2 * N], U8, "w2w")
         g = hold([P, 2, T], F32, "g")
         gcol = hold([P, T // P], F32, "gcol")
-        gw, gs, w1w, w1s = {}, {}, {}, {}
+        gw, gs, w1w, w1s, wide = {}, {}, {}, {}, {}
 
         def load_x(s):
             nc.sync.dma_start(out=raw[s][:], in_=xT_v[s])
@@ -90,6 +90,8 @@ def tile_moe_pln_mlp_relu2_kernel(
 
         def load_w1_scales(lo, hi):
             plane = hold([P, (hi - lo) * PASSES * H], U8, "w1s%d" % lo)
+            if lo == 0:
+                nc.vector.memset(plane[:, 0 : PASSES * H].bitcast(I32), 0)
             for r in range(4):
                 nc.sync.dma_start(
                     out=plane[r:P:32, :].bitcast(I32).rearrange("p (a b) -> p a b", b=H // 4),
@@ -140,6 +142,8 @@ def tile_moe_pln_mlp_relu2_kernel(
         def words(s, lo, hi, reach, tag=None):
             codes = hold([P, (hi - lo) * P], U32, "gw%d_%d" % (s, lo), tag)
             nc.vector.tensor_copy(codes[:], xw[:, WORDS_AT[s] : WORDS_AT[s] + reach].indirect(offs_t[:, lo * 8 : hi * 8]))
+            if lo == 0:
+                wide[s] = codes[:, 0:C]
             for b in range(lo, hi):
                 gw[s, b] = codes[:, (b - lo) * P : (b - lo + 1) * P]
 
@@ -180,6 +184,44 @@ def tile_moe_pln_mlp_relu2_kernel(
                     stop=(done[b] == PASSES),
                 )
 
+        still = {}
+
+        def deal(s):
+            codes = hold([P, 2 * H], U8, "dealt%d" % s)
+            nc.scalar.copy(
+                codes[:].bitcast(U16).rearrange("p (t c i) -> p c t i", t=4, i=8),
+                w1w[s, 0].bitcast(U16).rearrange("p (c i t) -> p c t i", t=4, i=8),
+            )
+            rows = hold([P, H], U8, "dealt_rows%d" % s)
+            nc.gpsimd.tensor_copy(rows[:].rearrange("p (t m) -> p t m", t=4), w1s[s, 0].rearrange("p (m t) -> p t m", t=4))
+            still[s] = (codes, rows)
+
+        def first_still(s):
+            done["still"] = done.get("still", 0) + 1
+            codes, rows = still[s]
+            token_rows, base = gs[s, 0]
+            for t in range(4):
+                if done["still"] == 1 and t % 2 == 0:
+                    acc[t // 2] = bank(t // 2)
+                nc.tensor.matmul_mx(
+                    out=acc[t // 2][:, t % 2 * C : (t % 2 + 1) * C],
+                    lhsT=codes[:, 2 * t * P : 2 * (t + 1) * P].bitcast(FP4X4),
+                    lhsT_scale=rows[:, t * P : (t + 1) * P],
+                    rhs=wide[s].bitcast(FP8X4),
+                    rhs_scale=token_rows[:, 0:C],
+                    start=(done["still"] == 1 and t % 2 == 0),
+                    stop=(done["still"] == PASSES and t % 2 == 1),
+                )
+
+        def finish_still():
+            lanes = hold([P, 4, C], F32, "lanes")
+            for u in range(2):
+                nc.scalar.activation(lanes[:, 2 * u : 2 * u + 2, :].rearrange("p t n -> p (t n)"), acc[u][:], RELU)
+            for b in range(2):
+                hb[b] = hold([P, P, 4], BF16, "hb%d" % b)
+                src = lanes[:, :, b * P : (b + 1) * P].rearrange("p t n -> p n t")
+                nc.gpsimd.tensor_tensor(hb[b][:], src, src, MULT)
+
         def rectify(b, engine):
             relu[b] = hold([P, 4, P], F32, "r%d" % b)
             lanes = acc[b][:].rearrange("p (m t) -> p t m", t=4)
@@ -205,7 +247,7 @@ def tile_moe_pln_mlp_relu2_kernel(
 
         def quantise_h(b):
             nc.vector.quantize_mx(
-                out=hw[:, b * P : (b + 1) * P].bitcast(FP8X4),
+                out=late[b // 2 == 0][:, b * P : (b + 1) * P].bitcast(FP8X4),
                 scales=hs[:, b * P : (b + 1) * P],
                 in_=hb[b][:].rearrange("p n t -> p (n t)"),
             )
@@ -218,7 +260,7 @@ def tile_moe_pln_mlp_relu2_kernel(
                     out=sums[j, lo][:, at - lo : at - lo + width],
                     lhsT=w2w[:, 2 * w : 2 * (w + P)].bitcast(FP4X4),
                     lhsT_scale=w2s[:, w : w + P],
-                    rhs=hw[:, at : at + width].bitcast(FP8X4),
+                    rhs=late[at < C][:, at : at + width].bitcast(FP8X4),
                     rhs_scale=hs[:, at : at + width],
                     start=True,
                     stop=True,
@@ -301,37 +343,50 @@ def tile_moe_pln_mlp_relu2_kernel(
         lower(2, 0, 4, three)
         load_w1e(2, 1, 4)
         load_w1e(3, 1, 4)
+        load_pos()
         words(3, 0, 4, 704)
         words(2, 0, 4, 1024)
-        words(1, 4, 8, 1536)
+        words(1, 4, 6, 1536)
         scales((2, 3), 4, 8, 704)
         lower(2, 4, 8, three)
-        load_pos()
+        words(1, 6, 8, 1536)
+        words(2, 4, 8, 1024)
         load_w2()
         load_gate()
-        first(0, range(8))
-        first(1, range(4))
-        first(3, range(4))
-        for b in range(4):
+        for s in (0, 1, 3, 2):
+            deal(s)
+        first(0, (2, 3))
+        first_still(0)
+        first(0, range(4, 8))
+        first(1, (2, 3))
+        first_still(1)
+        first(3, (2, 3))
+        first_still(3)
+        first_still(2)
+        finish_still()
+        for b in (2, 3):
             first(2, (b,))
             rectify(b, "s")
         first(1, range(4, 8))
-        for b in range(4):
+        for b in (2, 3):
             turn(b)
             square(b)
-        words(3, 4, 8, 704, "gw2_0")
-        words(2, 4, 6, T, "xb3")
-        words(2, 6, 8, T, "r0")
-        first(3, (4, 5, 6))
+        words(3, 4, 6, T, "gw1_6")
+        words(3, 6, 8, T, "r2")
+        first(3, (4, 5))
         first(2, (4, 5))
-        first(3, (7,))
         first(2, (6, 7))
-        for b in range(4):
+        first(3, (6, 7))
+        late[False] = hold([P, SLOTS], U32, "hw", "xw")
+        late[True] = hold([P, C], U32, "hw0", "r2")
+        for b in (2, 3):
             quantise_h(b)
         rectify(4, "s")
-        rectify(5, "v")
+        rectify(5, "s")
         rectify(6, "v")
         rectify(7, "s")
+        quantise_h(0)
+        quantise_h(1)
         for b in range(4, 8):
             turn(b)
         square(4)
@@ -340,14 +395,14 @@ def tile_moe_pln_mlp_relu2_kernel(
         square(7)
         second(0, 0, 512, 0)
         fetch(0, 0, 512, "s")
-        second(1, 0, 512, 1)
+        second(1, 0, 512, 4)
         quantise_h(4)
         quantise_h(6)
         second(0, 768, 896, 3, 128)
         quantise_h(5)
         second(0, 512, 768, 2, 128)
         quantise_h(7)
-        second(0, 896, 1024, 4, 128)
+        second(0, 896, 1024, 1, 128)
         fetch(0, 768, 896, "s")
         fetch(0, 512, 768, "v")
         fetch(0, 896, 1024, "s")

@@ -147,10 +147,14 @@ def tile_moe_pln_mlp_relu2_kernel(
             for b in range(lo, hi):
                 gw[s, b] = codes[:, (b - lo) * P : (b - lo + 1) * P]
 
-        def scales(passes, lo, hi, reach, tag=None):
+        def scales(passes, lo, hi, reach, tag=None, cut=1):
             at = PLANE_AT[passes[0]]
             rows = hold([P, (hi - lo) * P], U8, "gs%d_%d" % (passes[0], lo), tag)
-            nc.vector.tensor_copy(rows[:], xs[:, at : at + reach].indirect(offs_t[:, lo * 8 : hi * 8]))
+            n = (hi - lo) // cut
+            for c in range(cut):
+                nc.vector.tensor_copy(
+                    rows[:, c * n * P : (c + 1) * n * P], xs[:, at : at + reach].indirect(offs_t[:, (lo + c * n) * 8 : (lo + (c + 1) * n) * 8])
+                )
             for s in passes:
                 for b in range(lo, hi):
                     gs[s, b] = (rows, lo)
@@ -185,6 +189,10 @@ def tile_moe_pln_mlp_relu2_kernel(
                 )
 
         still = {}
+        early = hold([P, 2 * C, 4], BF16, "early")
+        hbe = [early[:, 0:C, :], early[:, C : 2 * C, :], hold([P, C, 4], BF16, "hbe2"), hold([P, C, 4], BF16, "hbe3")]
+        for b in range(2 * E):
+            hb[b] = hbe[b // 2][:, b % 2 * P : (b % 2 + 1) * P, :]
 
         def deal(s):
             codes = hold([P, 2 * H], U8, "dealt%d" % s)
@@ -218,9 +226,8 @@ def tile_moe_pln_mlp_relu2_kernel(
             for u in range(2):
                 nc.scalar.activation(lanes[:, 2 * u : 2 * u + 2, :].rearrange("p t n -> p (t n)"), acc[u][:], RELU)
             for b in range(2):
-                hb[b] = hold([P, P, 4], BF16, "hb%d" % b)
                 src = lanes[:, :, b * P : (b + 1) * P].rearrange("p t n -> p n t")
-                nc.gpsimd.tensor_tensor(hb[b][:], src, src, MULT)
+                nc.gpsimd.tensor_tensor(hb[b], src, src, MULT)
 
         def rectify(b, engine):
             relu[b] = hold([P, 4, P], F32, "r%d" % b)
@@ -236,20 +243,55 @@ def tile_moe_pln_mlp_relu2_kernel(
                 nc.tensor.transpose(turned[b][:, t * P : (t + 1) * P], relu[b][:, t, :], ident[:])
 
         def square(b, engine="s"):
-            hb[b] = hold([P, P, 4], BF16, "hb%d" % b)
             src = turned[b][:].rearrange("p (t n) -> p n t", t=4)
             if engine == "s":
-                nc.scalar.activation(hb[b][:], src, SQUARE)
+                nc.scalar.activation(hb[b], src, SQUARE)
             else:
                 kept = hold([P, P, 4], F32, "kept%d" % b)
                 nc.vector.tensor_copy(kept[:], src)
-                nc.vector.tensor_tensor(hb[b][:], src, kept[:], MULT)
+                nc.vector.tensor_tensor(hb[b], src, kept[:], MULT)
 
-        def quantise_h(b):
+        squared = {}
+
+        def rectify_pairs(b, engine):
+            relu[b] = hold([P, 2, P, 2], F32, "r%d" % b)
+            lanes = acc[b][:].rearrange("p (m u d) -> p u m d", u=2, d=2)
+            if engine == "v":
+                nc.vector.tensor_scalar_max(relu[b][:], lanes, 0.0)
+            else:
+                nc.scalar.activation(relu[b][:], lanes, RELU)
+
+        def square_pairs(b, engine, tag=None):
+            squared[b] = hold([P, H], BF16, "sq%d" % b, tag)
+            src = relu[b][:].rearrange("p u m d -> p (u m d)")
+            if engine == "s":
+                nc.scalar.activation(squared[b][:], src, SQUARE)
+            elif engine == "v":
+                nc.vector.tensor_tensor(squared[b][:], src, src, MULT)
+            else:
+                nc.gpsimd.tensor_tensor(squared[b][:], src, src, MULT)
+
+        def turn_pairs(b, into, at):
+            if at == 0:
+                turned["pairs", into] = bank(into)
+            turned[b] = turned["pairs", into][:, at * C : (at + 1) * C]
+            for u in range(2):
+                nc.tensor.transpose(turned[b][:, u * P : (u + 1) * P], squared[b][:].bitcast(F32)[:, u * P : (u + 1) * P], ident[:])
+
+        def weave(e, into, engine):
+            dst = hbe[e][:, :, :].rearrange("p n t -> p (n t)").bitcast(F32).rearrange("p (b n u) -> p b n u", b=2, u=2)
+            src = turned["pairs", into][:].rearrange("p (b u n) -> p b n u", b=2, u=2)
+            if engine == "s":
+                nc.scalar.copy(dst, src)
+            else:
+                nc.vector.tensor_copy(dst, src)
+
+        def quantise_h(lo, hi):
+            src = early[:, lo:hi, :] if lo < 2 * C else hbe[lo // C][:, lo % C : lo % C + hi - lo, :]
             nc.vector.quantize_mx(
-                out=late[b // 2 == 0][:, b * P : (b + 1) * P].bitcast(FP8X4),
-                scales=hs[:, b * P : (b + 1) * P],
-                in_=hb[b][:].rearrange("p n t -> p (n t)"),
+                out=late[lo < 2 * C][:, lo:hi].bitcast(FP8X4),
+                scales=hs[:, lo:hi],
+                in_=src.rearrange("p n t -> p (n t)"),
             )
 
         def second(j, lo, hi, b, width=C):
@@ -260,7 +302,7 @@ def tile_moe_pln_mlp_relu2_kernel(
                     out=sums[j, lo][:, at - lo : at - lo + width],
                     lhsT=w2w[:, 2 * w : 2 * (w + P)].bitcast(FP4X4),
                     lhsT_scale=w2s[:, w : w + P],
-                    rhs=late[at < C][:, at : at + width].bitcast(FP8X4),
+                    rhs=late[at < 2 * C][:, at : at + width].bitcast(FP8X4),
                     rhs_scale=hs[:, at : at + width],
                     start=True,
                     stop=True,
@@ -333,7 +375,7 @@ def tile_moe_pln_mlp_relu2_kernel(
         cast(2, 256, 384, "g")
         cast(2, 384, T, "g")
         quantise(2)
-        words(1, 0, 4, 704)
+        words(1, 2, 4, T)
         cast(3, 0, 256, "s")
         cast(3, 256, 384, "g")
         cast(3, 384, T, "g")
@@ -342,15 +384,23 @@ def tile_moe_pln_mlp_relu2_kernel(
         scales((2, 3), 0, 4, 704)
         lower(2, 0, 4, three)
         load_w1e(2, 1, 4)
+        words(1, 0, 2, 1536)
+        words(3, 2, 4, T)
+        words(2, 2, 4, 1024)
+        words(2, 0, 2, 1024)
+        scales((2, 3), 4, 6, T)
+        lower(2, 4, 6, one)
         load_w1e(3, 1, 4)
-        load_pos()
-        words(3, 0, 4, 704)
-        words(2, 0, 4, 1024)
+        words(3, 0, 2, T)
         words(1, 4, 6, 1536)
-        scales((2, 3), 4, 8, 704)
-        lower(2, 4, 8, three)
+        words(3, 4, 6, T)
+        scales((2, 3), 6, 8, T)
+        lower(2, 6, 8, one)
+        load_pos()
+        words(2, 4, 6, 1024)
         words(1, 6, 8, 1536)
-        words(2, 4, 8, 1024)
+        words(3, 6, 8, T)
+        words(2, 6, 8, 1024)
         load_w2()
         load_gate()
         for s in (0, 1, 3, 2):
@@ -361,55 +411,52 @@ def tile_moe_pln_mlp_relu2_kernel(
         first(1, (2, 3))
         first_still(1)
         first(3, (2, 3))
-        first_still(3)
-        first_still(2)
-        finish_still()
         for b in (2, 3):
             first(2, (b,))
-            rectify(b, "s")
-        first(1, range(4, 8))
-        for b in (2, 3):
-            turn(b)
-            square(b)
-        words(3, 4, 6, T, "gw1_6")
-        words(3, 6, 8, T, "r2")
+            rectify_pairs(b, "s")
+            square_pairs(b, "g")
+        first_still(2)
+        first_still(3)
+        finish_still()
+        first(1, (4, 5))
         first(3, (4, 5))
-        first(2, (4, 5))
-        first(2, (6, 7))
+        for b in (4, 5):
+            first(2, (b,))
+            rectify_pairs(b, "s")
+        turn_pairs(2, 1, 0)
+        turn_pairs(3, 1, 1)
+        first(1, (6, 7))
         first(3, (6, 7))
+        first(2, (6, 7))
+        for b in (4, 5):
+            square_pairs(b, "s")
+            turn_pairs(b, 4, b - 4)
         late[False] = hold([P, SLOTS], U32, "hw", "xw")
-        late[True] = hold([P, C], U32, "hw0", "r2")
-        for b in (2, 3):
-            quantise_h(b)
-        rectify(4, "s")
-        rectify(5, "s")
+        late[True] = hold([P, 2 * C], U32, "hw0", "gw2_6")
+        weave(1, 1, "v")
         rectify(6, "v")
         rectify(7, "s")
-        quantise_h(0)
-        quantise_h(1)
-        for b in range(4, 8):
+        quantise_h(0, 512)
+        weave(2, 4, "s")
+        for b in (6, 7):
             turn(b)
-        square(4)
-        square(5, "v")
-        square(6)
-        square(7)
+            square(b)
         second(0, 0, 512, 0)
-        fetch(0, 0, 512, "s")
-        second(1, 0, 512, 4)
-        quantise_h(4)
-        quantise_h(6)
+        quantise_h(512, 768)
+        fetch(0, 0, 512, "v")
+        second(0, 512, 768, 2)
+        quantise_h(768, 896)
         second(0, 768, 896, 3, 128)
-        quantise_h(5)
-        second(0, 512, 768, 2, 128)
-        quantise_h(7)
+        fetch(0, 512, 768, "s")
+        quantise_h(896, 1024)
         second(0, 896, 1024, 1, 128)
         fetch(0, 768, 896, "s")
-        fetch(0, 512, 768, "v")
         fetch(0, 896, 1024, "s")
+        second(1, 0, 512, 5)
         fetch(1, 0, 512, "s")
-        second(1, 512, 1024, 5)
+        second(1, 512, 1024, 4)
         fetch(1, 512, 1024, "s")
-        second(2, 0, 512, 2)
+        second(2, 0, 512, 6)
         second(2, 512, 1024, 7)
         term(0, 0)
         fetch(2, 0, 512, "s")

@@ -24,8 +24,8 @@ MULT = mybir.AluOpType.mult
 ADD = mybir.AluOpType.add
 WORDS_AT = (1536, 0, 512, 1024)
 XW = 1536 + 1408
-PLANE_AT = (512, 512, 0, 0)
-XS = 512 + 1408
+PLANE_AT = (0, 0, 1024, 1024)
+XS = 1024 + 704
 LIFT = (0, 4, 4, 0)
 
 
@@ -54,7 +54,7 @@ def tile_moe_pln_mlp_relu2_kernel(
         w2s_v = w2_scales.bitcast(I32)
 
         raw = [hold([P, 4, T], F32, "raw%d" % s) for s in range(PASSES)]
-        xb = [hold([P, T, 4], BF16, "xb%d" % s) for s in range(PASSES)]
+        xb = {}
         xw = hold([P, XW], U32, "xw")
         xs = hold([P, XS], U8, "xs")
         late = {}
@@ -122,21 +122,31 @@ def tile_moe_pln_mlp_relu2_kernel(
             nc.sync.dma_start(pos_t[0][:], pos1)
             nc.sync.dma_start(pos_t[1][:], pos2)
 
+        def rounded(s, lo, hi):
+            half = lo // 256
+            return xb[s, half][:, lo - 256 * half : hi - 256 * half, :]
+
         def cast(s, lo, hi, engine):
-            dst = xb[s][:, lo:hi, :].rearrange("p (c i) t -> p c t i", i=4)
-            src = raw[s][:, :, lo:hi].rearrange("p t (c i) -> p c t i", i=4)
+            src = raw[s][:, :, lo:hi]
+            if engine == "g":
+                nc.gpsimd.tensor_copy(rounded(s, lo, hi), src.rearrange("p t c -> p c t"))
+                return
+            dst = rounded(s, lo, hi).rearrange("p (c i) t -> p c t i", i=4)
+            src = src.rearrange("p t (c i) -> p c t i", i=4)
             if engine == "s":
                 nc.scalar.copy(dst, src)
-            elif engine == "v":
-                nc.vector.tensor_copy(dst, src)
             else:
-                nc.gpsimd.tensor_copy(xb[s][:, lo:hi, :], raw[s][:, :, lo:hi].rearrange("p t c -> p c t"))
+                nc.vector.tensor_copy(dst, src)
 
-        def quantise(s, lo=0, hi=T):
+        def halves(s, tag=None):
+            xb[s, 0] = hold([P, 256, 4], BF16, "xb%d_0" % s)
+            xb[s, 1] = hold([P, 256, 4], BF16, "xb%d_1" % s, tag)
+
+        def quantise(s, lo, hi):
             nc.vector.quantize_mx(
                 out=xw[:, WORDS_AT[s] + lo : WORDS_AT[s] + hi].bitcast(FP8X4),
                 scales=xs[LIFT[s] : P, PLANE_AT[s] + lo : PLANE_AT[s] + hi],
-                in_=xb[s][:, lo:hi, :].rearrange("p c t -> p (c t)"),
+                in_=rounded(s, lo, hi).rearrange("p c t -> p (c t)"),
             )
 
         def words(s, lo, hi, reach, tag=None):
@@ -147,14 +157,11 @@ def tile_moe_pln_mlp_relu2_kernel(
             for b in range(lo, hi):
                 gw[s, b] = codes[:, (b - lo) * P : (b - lo + 1) * P]
 
-        def scales(passes, lo, hi, reach, tag=None, cut=1):
+        def scales(passes, lo, hi, reach, rows=None):
             at = PLANE_AT[passes[0]]
-            rows = hold([P, (hi - lo) * P], U8, "gs%d_%d" % (passes[0], lo), tag)
-            n = (hi - lo) // cut
-            for c in range(cut):
-                nc.vector.tensor_copy(
-                    rows[:, c * n * P : (c + 1) * n * P], xs[:, at : at + reach].indirect(offs_t[:, (lo + c * n) * 8 : (lo + (c + 1) * n) * 8])
-                )
+            rows, base = rows or (hold([P, (hi - lo) * P], U8, "gs%d_%d" % (passes[0], lo)), lo)
+            nc.vector.tensor_copy(rows[:, (lo - base) * P : (hi - base) * P], xs[:, at : at + reach].indirect(offs_t[:, lo * 8 : hi * 8]))
+            lo = base
             for s in passes:
                 for b in range(lo, hi):
                     gs[s, b] = (rows, lo)
@@ -194,13 +201,13 @@ def tile_moe_pln_mlp_relu2_kernel(
         for b in range(2 * E):
             hb[b] = hbe[b // 2][:, b % 2 * P : (b % 2 + 1) * P, :]
 
-        def deal(s):
+        def deal(s, tag=None):
             codes = hold([P, 2 * H], U8, "dealt%d" % s)
             nc.scalar.copy(
                 codes[:].bitcast(U16).rearrange("p (t c i) -> p c t i", t=4, i=8),
                 w1w[s, 0].bitcast(U16).rearrange("p (c i t) -> p c t i", t=4, i=8),
             )
-            rows = hold([P, H], U8, "dealt_rows%d" % s)
+            rows = hold([P, H], U8, "dealt_rows%d" % s, tag)
             nc.gpsimd.tensor_copy(rows[:].rearrange("p (t m) -> p t m", t=4), w1s[s, 0].rearrange("p (m t) -> p t m", t=4))
             still[s] = (codes, rows)
 
@@ -222,12 +229,12 @@ def tile_moe_pln_mlp_relu2_kernel(
                 )
 
         def finish_still():
-            lanes = hold([P, 4, C], F32, "lanes")
+            lanes = hold([P, 2, C, 2], F32, "lanes")
             for u in range(2):
-                nc.scalar.activation(lanes[:, 2 * u : 2 * u + 2, :].rearrange("p t n -> p (t n)"), acc[u][:], RELU)
+                nc.scalar.activation(lanes[:, u, :, :], acc[u][:].rearrange("p (d n) -> p n d", d=2), RELU)
             for b in range(2):
-                src = lanes[:, :, b * P : (b + 1) * P].rearrange("p t n -> p n t")
-                nc.gpsimd.tensor_tensor(hb[b], src, src, MULT)
+                src = lanes[:, :, b * P : (b + 1) * P, :].rearrange("p u n d -> p n u d")
+                nc.gpsimd.tensor_tensor(hb[b].rearrange("p n (u d) -> p n u d", u=2), src, src, MULT)
 
         def rectify(b, engine):
             relu[b] = hold([P, 4, P], F32, "r%d" % b)
@@ -355,30 +362,37 @@ def tile_moe_pln_mlp_relu2_kernel(
         load_w1_scales(0, 2)
         load_w1_scales(2, 4)
         load_w1(0, 2, 4)
+        halves(0)
         cast(0, 0, 256, "v")
         cast(0, 256, 352, "v")
         cast(0, 352, T, "s")
         quantise(0, 0, 256)
         quantise(0, 256, T)
         words(0, 0, 8, 1408)
+        halves(1)
         cast(1, 0, 256, "s")
         cast(1, 256, 384, "s")
         cast(1, 384, T, "g")
         quantise(1, 0, 256)
         quantise(1, 256, T)
-        scales((0, 1), 0, 8, 1408)
-        lower(1, 0, 8, one)
+        first_rows = (hold([P, SLOTS], U8, "gs0_0"), 0)
+        scales((0, 1), 0, 6, 1024, first_rows)
+        halves(2, "xb1_1")
+        cast(2, 0, 256, "s")
+        cast(2, 256, 352, "s")
+        cast(2, 352, T, "g")
+        quantise(2, 0, 256)
+        quantise(2, 256, T)
+        halves(3, "xb1_1")
+        cast(3, 0, 256, "s")
+        cast(3, 256, 384, "s")
+        cast(3, 384, T, "g")
+        scales((0, 1), 6, 8, 1536, first_rows)
         load_w1(1, 0, 2)
+        lower(1, 0, 8, one)
         load_w1(3, 0, 2)
         load_w1(2, 0, 2)
-        cast(2, 0, 256, "s")
-        cast(2, 256, 384, "g")
-        cast(2, 384, T, "g")
-        quantise(2)
-        words(1, 2, 4, T)
-        cast(3, 0, 256, "s")
-        cast(3, 256, 384, "g")
-        cast(3, 384, T, "g")
+        words(1, 2, 4, 1024)
         quantise(3, 0, 256)
         quantise(3, 256, T)
         scales((2, 3), 0, 4, 704)
@@ -403,8 +417,10 @@ def tile_moe_pln_mlp_relu2_kernel(
         words(2, 6, 8, 1024)
         load_w2()
         load_gate()
-        for s in (0, 1, 3, 2):
-            deal(s)
+        deal(0)
+        deal(1, "xb1_1")
+        deal(3)
+        deal(2)
         first(0, (2, 3))
         first_still(0)
         first(0, range(4, 8))

@@ -49,7 +49,7 @@ def tile_moe_pln_mlp_relu2_kernel(
 
         xT_v = xT.rearrange("(s p j) t -> s p j t", p=P, j=4)
         w1w_v = w1_words.bitcast(I32)
-        w1s_v = w1_scales.bitcast(I32)
+        w1s_v = w1_scales.bitcast(I32).rearrange("e s q b -> (e s) q b")
         w2w_v = w2_words.bitcast(I32)
         w2s_v = w2_scales.bitcast(I32)
 
@@ -88,19 +88,16 @@ def tile_moe_pln_mlp_relu2_kernel(
             for s in range(lo, hi):
                 w1w[s, e] = words1[:, (s - lo) * 2 * H : (s - lo + 1) * 2 * H]
 
-        def load_w1_scales(lo, hi):
-            plane = hold([P, (hi - lo) * PASSES * H], U8, "w1s%d" % lo)
-            if lo == 0:
-                nc.vector.memset(plane[:, 0 : PASSES * H].bitcast(I32), 0)
+        def load_w1_scales(odd):
+            plane = hold([P, 2 * E * H], U8, "w1s%d" % odd)
+            nc.vector.memset(plane[:, 0 : 2 * H].bitcast(I32), 0)
             for r in range(4):
                 nc.sync.dma_start(
                     out=plane[r:P:32, :].bitcast(I32).rearrange("p (a b) -> p a b", b=H // 4),
-                    in_=w1s_v[lo:hi, :, r:16:4, :].rearrange("e s q b -> q (e s) b"),
+                    in_=w1s_v[odd : E * PASSES : 2, r:16:4, :].rearrange("a q b -> q a b"),
                 )
-            for e in range(lo, hi):
-                for s in range(PASSES):
-                    at = ((e - lo) * PASSES + s) * H
-                    w1s[s, e] = plane[:, at : at + H]
+            for a in range(2 * E):
+                w1s[2 * (a % 2) + odd, a // 2] = plane[:, a * H : (a + 1) * H]
 
         def load_w2():
             nc.sync.dma_start(
@@ -195,6 +192,20 @@ def tile_moe_pln_mlp_relu2_kernel(
                     stop=(done[b] == PASSES),
                 )
 
+        def warm(n):
+            rows, base = gs[0, 2]
+            idle = bank(7)
+            for i in range(n):
+                nc.tensor.matmul_mx(
+                    out=idle[:],
+                    lhsT=gw[0, 2].bitcast(FP8X4),
+                    lhsT_scale=rows[:, 0:P],
+                    rhs=w1w[0, 0].bitcast(FP4X4),
+                    rhs_scale=rows[:, 0:H],
+                    start=True,
+                    stop=True,
+                )
+
         still = {}
         early = hold([P, 2 * C, 4], BF16, "early")
         hbe = [early[:, 0:C, :], early[:, C : 2 * C, :], hold([P, C, 4], BF16, "hbe2"), hold([P, C, 4], BF16, "hbe3")]
@@ -234,7 +245,7 @@ def tile_moe_pln_mlp_relu2_kernel(
                 nc.scalar.activation(lanes[:, u, :, :], acc[u][:].rearrange("p (d n) -> p n d", d=2), RELU)
             for b in range(2):
                 src = lanes[:, :, b * P : (b + 1) * P, :].rearrange("p u n d -> p n u d")
-                nc.gpsimd.tensor_tensor(hb[b].rearrange("p n (u d) -> p n u d", u=2), src, src, MULT)
+                nc.scalar.activation(hb[b].rearrange("p n (u d) -> p n u d", u=2), src, SQUARE)
 
         def rectify(b, engine):
             relu[b] = hold([P, 4, P], F32, "r%d" % b)
@@ -281,7 +292,7 @@ def tile_moe_pln_mlp_relu2_kernel(
         def turn_pairs(b, into, at):
             if at == 0:
                 turned["pairs", into] = bank(into)
-            turned[b] = turned["pairs", into][:, at * C : (at + 1) * C]
+            turned[b] = turned["pairs", into][:, b % 2 * C : (b % 2 + 1) * C]
             for u in range(2):
                 nc.tensor.transpose(turned[b][:, u * P : (u + 1) * P], squared[b][:].bitcast(F32)[:, u * P : (u + 1) * P], ident[:])
 
@@ -356,12 +367,14 @@ def tile_moe_pln_mlp_relu2_kernel(
         nc.sync.dma_start(offs_t[:], offs)
         nc.gpsimd.memset(xs[:].bitcast(I32), 0)
         make_identity(nc, ident[:])
-        for s in (1, 2, 3):
-            load_x(s)
-        load_w1(0, 0, 2)
-        load_w1_scales(0, 2)
-        load_w1_scales(2, 4)
-        load_w1(0, 2, 4)
+        load_x(1)
+        load_x(2)
+        load_w1(0, 0, 1)
+        load_x(3)
+        load_w1(0, 1, 3)
+        load_w1_scales(0)
+        load_w1_scales(1)
+        load_w1(0, 3, 4)
         halves(0)
         cast(0, 0, 256, "v")
         cast(0, 256, 352, "v")
@@ -377,6 +390,7 @@ def tile_moe_pln_mlp_relu2_kernel(
         quantise(1, 256, T)
         first_rows = (hold([P, SLOTS], U8, "gs0_0"), 0)
         scales((0, 1), 0, 6, 1024, first_rows)
+        warm(3)
         halves(2, "xb1_1")
         cast(2, 0, 256, "s")
         cast(2, 256, 352, "s")
@@ -392,38 +406,37 @@ def tile_moe_pln_mlp_relu2_kernel(
         lower(1, 0, 8, one)
         load_w1(3, 0, 2)
         load_w1(2, 0, 2)
-        words(1, 2, 4, 1024)
+        words(1, 0, 4, 1024)
         quantise(3, 0, 256)
         quantise(3, 256, T)
         scales((2, 3), 0, 4, 704)
         lower(2, 0, 4, three)
+        load_pos()
         load_w1e(2, 1, 4)
-        words(1, 0, 2, 1536)
         words(3, 2, 4, T)
-        words(2, 2, 4, 1024)
-        words(2, 0, 2, 1024)
+        words(2, 0, 4, 1024)
         scales((2, 3), 4, 6, T)
         lower(2, 4, 6, one)
         load_w1e(3, 1, 4)
         words(3, 0, 2, T)
-        words(1, 4, 6, 1536)
-        words(3, 4, 6, T)
         scales((2, 3), 6, 8, T)
         lower(2, 6, 8, one)
-        load_pos()
+        words(1, 4, 6, 1536)
+        words(3, 4, 6, T)
         words(2, 4, 6, 1024)
         words(1, 6, 8, 1536)
-        words(3, 6, 8, T)
-        words(2, 6, 8, 1024)
+        for b in (6, 7):
+            words(3, b, b + 1, T)
+            words(2, b, b + 1, 1024)
         load_w2()
         load_gate()
-        deal(0)
-        deal(1, "xb1_1")
+        deal(0, "xb1_1")
+        deal(1)
         deal(3)
         deal(2)
-        first(0, (2, 3))
+        first(0, range(2, 6))
         first_still(0)
-        first(0, range(4, 8))
+        first(0, (6, 7))
         first(1, (2, 3))
         first_still(1)
         first(3, (2, 3))
@@ -442,16 +455,18 @@ def tile_moe_pln_mlp_relu2_kernel(
         turn_pairs(2, 1, 0)
         turn_pairs(3, 1, 1)
         first(1, (6, 7))
-        first(3, (6, 7))
-        first(2, (6, 7))
-        for b in (4, 5):
-            square_pairs(b, "s")
-            turn_pairs(b, 4, b - 4)
+        for b in (6, 7):
+            first(3, (b,))
+            first(2, (b,))
+        square_pairs(4, "g")
+        square_pairs(5, "s")
+        turn_pairs(5, 4, 0)
+        turn_pairs(4, 4, 1)
         late[False] = hold([P, SLOTS], U32, "hw", "xw")
-        late[True] = hold([P, 2 * C], U32, "hw0", "gw2_6")
+        late[True] = hold([P, 2 * C], U32, "hw0", "gw2_7")
         weave(1, 1, "v")
-        rectify(6, "v")
-        rectify(7, "s")
+        rectify(6, "s")
+        rectify(7, "v")
         quantise_h(0, 512)
         weave(2, 4, "s")
         for b in (6, 7):

@@ -27,6 +27,7 @@ XW = 1536 + 1408
 PLANE_AT = (0, 0, 1024, 1024)
 XS = 1024 + 704
 LIFT = (0, 4, 4, 0)
+SOURCE = (0, 2, 1, 3)
 
 
 def tile_moe_pln_mlp_relu2_kernel(
@@ -68,25 +69,26 @@ def tile_moe_pln_mlp_relu2_kernel(
         gw, gs, w1w, w1s, wide = {}, {}, {}, {}, {}
 
         def load_x(s):
-            nc.sync.dma_start(out=raw[s][:], in_=xT_v[s])
+            nc.sync.dma_start(out=raw[s][:], in_=xT_v[SOURCE[s]])
 
         def load_w1(s, lo, hi):
             words1 = hold([P, (hi - lo) * 2 * H], U8, "w1w%d%d" % (s, lo))
             nc.sync.dma_start(
                 out=words1[:].bitcast(I32).rearrange("p (e b) -> p e b", e=hi - lo),
-                in_=w1w_v[lo:hi, s].rearrange("e p b -> p e b"),
+                in_=w1w_v[lo:hi, SOURCE[s]].rearrange("e p b -> p e b"),
             )
             for e in range(lo, hi):
                 w1w[s, e] = words1[:, (e - lo) * 2 * H : (e - lo + 1) * 2 * H]
 
-        def load_w1e(e, lo, hi):
-            words1 = hold([P, (hi - lo) * 2 * H], U8, "w1e%d%d" % (e, lo))
+        def load_w1e(e, lo, step):
+            passes = range(lo, PASSES, step)
+            words1 = hold([P, len(passes) * 2 * H], U8, "w1e%d%d" % (e, lo))
             nc.sync.dma_start(
-                out=words1[:].bitcast(I32).rearrange("p (s b) -> p s b", s=hi - lo),
-                in_=w1w_v[e, lo:hi].rearrange("s p b -> p s b"),
+                out=words1[:].bitcast(I32).rearrange("p (s b) -> p s b", s=len(passes)),
+                in_=w1w_v[e, lo:PASSES:step].rearrange("s p b -> p s b"),
             )
-            for s in range(lo, hi):
-                w1w[s, e] = words1[:, (s - lo) * 2 * H : (s - lo + 1) * 2 * H]
+            for i, a in enumerate(passes):
+                w1w[SOURCE.index(a), e] = words1[:, i * 2 * H : (i + 1) * 2 * H]
 
         def load_w1_scales(odd):
             plane = hold([P, 2 * E * H], U8, "w1s%d" % odd)
@@ -97,7 +99,7 @@ def tile_moe_pln_mlp_relu2_kernel(
                     in_=w1s_v[odd : E * PASSES : 2, r:16:4, :].rearrange("a q b -> q a b"),
                 )
             for a in range(2 * E):
-                w1s[2 * (a % 2) + odd, a // 2] = plane[:, a * H : (a + 1) * H]
+                w1s[SOURCE.index(2 * (a % 2) + odd), a // 2] = plane[:, a * H : (a + 1) * H]
 
         def load_w2():
             nc.sync.dma_start(
@@ -200,16 +202,17 @@ def tile_moe_pln_mlp_relu2_kernel(
                     out=idle[:],
                     lhsT=gw[0, 2].bitcast(FP8X4),
                     lhsT_scale=rows[:, 0:P],
-                    rhs=w1w[0, 0].bitcast(FP4X4),
+                    rhs=w1w[0, 1].bitcast(FP4X4),
                     rhs_scale=rows[:, 0:H],
                     start=True,
                     stop=True,
                 )
 
         still = {}
-        early = hold([P, 2 * C, 4], BF16, "early")
-        hbe = [early[:, 0:C, :], early[:, C : 2 * C, :], hold([P, C, 4], BF16, "hbe2"), hold([P, C, 4], BF16, "hbe3")]
-        for b in range(2 * E):
+        early = hold([P, 3 * P, 4], BF16, "early")
+        hbe = {1: early[:, 0:C, :], 2: hold([P, C, 4], BF16, "hbe2"), 3: hold([P, C, 4], BF16, "hbe3")}
+        hb[0] = early[:, C : 3 * P, :]
+        for b in range(2, 2 * E):
             hb[b] = hbe[b // 2][:, b % 2 * P : (b % 2 + 1) * P, :]
 
         def deal(s, tag=None):
@@ -240,12 +243,19 @@ def tile_moe_pln_mlp_relu2_kernel(
                 )
 
         def finish_still():
-            lanes = hold([P, 2, C, 2], F32, "lanes")
+            relu[0] = hold([P, 2, C, 2], F32, "lanes")
             for u in range(2):
-                nc.scalar.activation(lanes[:, u, :, :], acc[u][:].rearrange("p (d n) -> p n d", d=2), RELU)
-            for b in range(2):
-                src = lanes[:, :, b * P : (b + 1) * P, :].rearrange("p u n d -> p n u d")
-                nc.scalar.activation(hb[b].rearrange("p n (u d) -> p n u d", u=2), src, SQUARE)
+                nc.scalar.activation(relu[0][:, u, :, :], acc[u][:].rearrange("p (d n) -> p n d", d=2), RELU)
+
+        def square_still(b, engine):
+            if b == 1:
+                hb[b] = hold([P, P, 4], BF16, "hb1", "gw2_6")[:, :, :]
+            src = relu[0][:, :, b * P : (b + 1) * P, :].rearrange("p u n d -> p n u d")
+            dst = hb[b].rearrange("p n (u d) -> p n u d", u=2)
+            if engine == "s":
+                nc.scalar.activation(dst, src, SQUARE)
+            else:
+                nc.gpsimd.tensor_tensor(dst, src, src, MULT)
 
         def rectify(b, engine):
             relu[b] = hold([P, 4, P], F32, "r%d" % b)
@@ -304,13 +314,15 @@ def tile_moe_pln_mlp_relu2_kernel(
             else:
                 nc.vector.tensor_copy(dst, src)
 
-        def quantise_h(lo, hi):
-            src = early[:, lo:hi, :] if lo < 2 * C else hbe[lo // C][:, lo % C : lo % C + hi - lo, :]
-            nc.vector.quantize_mx(
-                out=late[lo < 2 * C][:, lo:hi].bitcast(FP8X4),
-                scales=hs[:, lo:hi],
-                in_=src.rearrange("p n t -> p (n t)"),
-            )
+        def column(slot):
+            return slot if slot >= 2 * C else (slot + C) % (2 * C)
+
+        def hidden(lo, hi):
+            base = lo // (2 * C) * 2 * C
+            return late[base][:, lo - base : hi - base]
+
+        def quantise_h(lo, hi, src):
+            nc.vector.quantize_mx(out=hidden(lo, hi).bitcast(FP8X4), scales=hs[:, lo:hi], in_=src.rearrange("p n t -> p (n t)"))
 
         def second(j, lo, hi, b, width=C):
             sums[j, lo] = bank(b)
@@ -320,8 +332,8 @@ def tile_moe_pln_mlp_relu2_kernel(
                     out=sums[j, lo][:, at - lo : at - lo + width],
                     lhsT=w2w[:, 2 * w : 2 * (w + P)].bitcast(FP4X4),
                     lhsT_scale=w2s[:, w : w + P],
-                    rhs=late[at < 2 * C][:, at : at + width].bitcast(FP8X4),
-                    rhs_scale=hs[:, at : at + width],
+                    rhs=hidden(column(at), column(at) + width).bitcast(FP8X4),
+                    rhs_scale=hs[:, column(at) : column(at) + width],
                     start=True,
                     stop=True,
                 )
@@ -369,12 +381,12 @@ def tile_moe_pln_mlp_relu2_kernel(
         make_identity(nc, ident[:])
         load_x(1)
         load_x(2)
-        load_w1(0, 0, 1)
+        load_w1(0, 1, 2)
         load_x(3)
-        load_w1(0, 1, 3)
         load_w1_scales(0)
-        load_w1_scales(1)
-        load_w1(0, 3, 4)
+        load_w1(0, 2, 4)
+        load_w1e(0, 0, 2)
+        load_w1(1, 1, 2)
         halves(0)
         cast(0, 0, 256, "v")
         cast(0, 256, 352, "v")
@@ -402,8 +414,8 @@ def tile_moe_pln_mlp_relu2_kernel(
         cast(3, 256, 384, "s")
         cast(3, 384, T, "g")
         scales((0, 1), 6, 8, 1536, first_rows)
-        load_w1(1, 0, 2)
         lower(1, 0, 8, one)
+        load_w1_scales(1)
         load_w1(3, 0, 2)
         load_w1(2, 0, 2)
         words(1, 0, 4, 1024)
@@ -412,12 +424,12 @@ def tile_moe_pln_mlp_relu2_kernel(
         scales((2, 3), 0, 4, 704)
         lower(2, 0, 4, three)
         load_pos()
-        load_w1e(2, 1, 4)
+        load_w1e(2, 1, 1)
         words(3, 2, 4, T)
         words(2, 0, 4, 1024)
         scales((2, 3), 4, 6, T)
         lower(2, 4, 6, one)
-        load_w1e(3, 1, 4)
+        load_w1e(3, 1, 1)
         words(3, 0, 2, T)
         scales((2, 3), 6, 8, T)
         lower(2, 6, 8, one)
@@ -434,9 +446,8 @@ def tile_moe_pln_mlp_relu2_kernel(
         deal(1)
         deal(3)
         deal(2)
-        first(0, range(2, 6))
+        first(0, range(2, 8))
         first_still(0)
-        first(0, (6, 7))
         first(1, (2, 3))
         first_still(1)
         first(3, (2, 3))
@@ -447,6 +458,7 @@ def tile_moe_pln_mlp_relu2_kernel(
         first_still(2)
         first_still(3)
         finish_still()
+        square_still(0, "s")
         first(1, (4, 5))
         first(3, (4, 5))
         for b in (4, 5):
@@ -462,27 +474,29 @@ def tile_moe_pln_mlp_relu2_kernel(
         square_pairs(5, "s")
         turn_pairs(5, 4, 0)
         turn_pairs(4, 4, 1)
-        late[False] = hold([P, SLOTS], U32, "hw", "xw")
-        late[True] = hold([P, 2 * C], U32, "hw0", "gw2_7")
+        late[2 * C] = hold([P, 2 * C], U32, "hw", "xw")
+        late[0] = hold([P, 2 * C], U32, "hw0", "gw2_7")
         weave(1, 1, "v")
         rectify(6, "s")
         rectify(7, "v")
-        quantise_h(0, 512)
+        square_still(1, "s")
+        quantise_h(0, 384, early[:])
         weave(2, 4, "s")
         for b in (6, 7):
             turn(b)
             square(b)
+        quantise_h(512, 768, hbe[2][:])
+        quantise_h(384, 512, hb[1])
         second(0, 0, 512, 0)
-        quantise_h(512, 768)
-        fetch(0, 0, 512, "v")
         second(0, 512, 768, 2)
-        quantise_h(768, 896)
+        quantise_h(768, 896, hb[6])
         second(0, 768, 896, 3, 128)
-        fetch(0, 512, 768, "s")
-        quantise_h(896, 1024)
+        quantise_h(896, 1024, hb[7])
         second(0, 896, 1024, 1, 128)
+        fetch(0, 0, 512, "s")
+        fetch(0, 512, 768, "v")
         fetch(0, 768, 896, "s")
-        fetch(0, 896, 1024, "s")
+        fetch(0, 896, 1024, "v")
         second(1, 0, 512, 5)
         fetch(1, 0, 512, "s")
         second(1, 512, 1024, 4)

@@ -396,12 +396,12 @@ def tile_moe_pln_mlp_relu2_kernel(
         words(0, 0, 8, 1408)
         halves(1)
         cast(1, 0, 256, "s")
-        cast(1, 256, 384, "s")
-        cast(1, 384, T, "g")
+        cast(1, 256, 352, "s")
+        cast(1, 352, T, "g")
         quantise(1, 0, 256)
         quantise(1, 256, T)
         first_rows = (hold([P, SLOTS], U8, "gs0_0"), 0)
-        scales((0, 1), 0, 6, 1024, first_rows)
+        scales((0, 1), 0, 4, 704, first_rows)
         warm(3)
         halves(2, "xb1_1")
         cast(2, 0, 256, "s")
@@ -411,15 +411,16 @@ def tile_moe_pln_mlp_relu2_kernel(
         quantise(2, 256, T)
         halves(3, "xb1_1")
         cast(3, 0, 256, "s")
-        cast(3, 256, 384, "s")
-        cast(3, 384, T, "g")
-        scales((0, 1), 6, 8, 1536, first_rows)
+        cast(3, 256, 320, "s")
+        cast(3, 320, T, "g")
+        scales((0, 1), 4, 8, 1280, first_rows)
+        words(1, 2, 4, 1024)
         lower(1, 0, 8, one)
         load_w1_scales(1)
         load_w1(3, 0, 2)
         load_w1(2, 0, 2)
-        words(1, 0, 4, 1024)
         quantise(3, 0, 256)
+        words(1, 0, 2, 1280)
         quantise(3, 256, T)
         scales((2, 3), 0, 4, 704)
         lower(2, 0, 4, three)

@@ -249,7 +249,7 @@ def tile_moe_pln_mlp_relu2_kernel(
 
         def square_still(b, engine):
             if b == 1:
-                hb[b] = hold([P, P, 4], BF16, "hb1", "gw2_6")[:, :, :]
+                hb[b] = hold([P, P, 4], BF16, "hb1", "r4")[:, :, :]
             src = relu[0][:, :, b * P : (b + 1) * P, :].rearrange("p u n d -> p n u d")
             dst = hb[b].rearrange("p n (u d) -> p n u d", u=2)
             if engine == "s":
@@ -381,12 +381,12 @@ def tile_moe_pln_mlp_relu2_kernel(
         make_identity(nc, ident[:])
         load_x(1)
         load_x(2)
-        load_w1(0, 1, 2)
         load_x(3)
+        load_w1(0, 1, 2)
         load_w1_scales(0)
         load_w1(0, 2, 4)
         load_w1e(0, 0, 2)
-        load_w1(1, 1, 2)
+        load_w1e(1, 1, 1)
         halves(0)
         cast(0, 0, 256, "v")
         cast(0, 256, 352, "v")
@@ -417,8 +417,7 @@ def tile_moe_pln_mlp_relu2_kernel(
         words(1, 2, 4, 1024)
         lower(1, 0, 8, one)
         load_w1_scales(1)
-        load_w1(3, 0, 2)
-        load_w1(2, 0, 2)
+        load_w1e(0, 1, 2)
         quantise(3, 0, 256)
         words(1, 0, 2, 1280)
         quantise(3, 256, T)
@@ -445,8 +444,8 @@ def tile_moe_pln_mlp_relu2_kernel(
         load_gate()
         deal(0, "xb1_1")
         deal(1)
-        deal(3)
         deal(2)
+        deal(3)
         first(0, range(2, 8))
         first_still(0)
         first(1, (2, 3))
@@ -473,6 +472,7 @@ def tile_moe_pln_mlp_relu2_kernel(
             first(2, (b,))
         square_pairs(4, "g")
         square_pairs(5, "s")
+        square_still(1, "g")
         turn_pairs(5, 4, 0)
         turn_pairs(4, 4, 1)
         late[2 * C] = hold([P, 2 * C], U32, "hw", "xw")
@@ -480,7 +480,6 @@ def tile_moe_pln_mlp_relu2_kernel(
         weave(1, 1, "v")
         rectify(6, "s")
         rectify(7, "v")
-        square_still(1, "s")
         quantise_h(0, 384, early[:])
         weave(2, 4, "s")
         for b in (6, 7):

@@ -54,7 +54,8 @@ def tile_moe_pln_mlp_relu2_kernel(
         w2w_v = w2_words.bitcast(I32)
         w2s_v = w2_scales.bitcast(I32)
 
-        raw = [hold([P, 4, T], F32, "raw%d" % s) for s in range(PASSES)]
+        raw = {s: hold([P, 4, T], F32, "raw%d" % s) for s in range(1, PASSES)}
+        pairs = [hold([P, 2, T], F32, "pair%d" % u) for u in range(2)]
         xb = {}
         xw = hold([P, XW], U32, "xw")
         xs = hold([P, XS], U8, "xs")
@@ -132,6 +133,18 @@ def tile_moe_pln_mlp_relu2_kernel(
                 return
             dst = rounded(s, lo, hi).rearrange("p (c i) t -> p c t i", i=4)
             src = src.rearrange("p t (c i) -> p c t i", i=4)
+            if engine == "s":
+                nc.scalar.copy(dst, src)
+            else:
+                nc.vector.tensor_copy(dst, src)
+
+        def load_pairs():
+            for u in range(2):
+                nc.sync.dma_start(out=pairs[u][:], in_=xT_v[SOURCE[0], :, 2 * u : 2 * u + 2, :])
+
+        def cast_pair(u, lo, hi, engine):
+            dst = rounded(0, lo, hi)[:, :, 2 * u : 2 * u + 2].rearrange("p (c i) t -> p c i t", i=4)
+            src = pairs[u][:, :, lo:hi].rearrange("p t (c i) -> p c i t", i=4)
             if engine == "s":
                 nc.scalar.copy(dst, src)
             else:
@@ -375,7 +388,7 @@ def tile_moe_pln_mlp_relu2_kernel(
             nc.vector.tensor_tensor(o[:], part(j, 1, lo, hi), part(j, 0, lo, hi), ADD)
             (queue or nc.sync).dma_start(out=out[j * P : (j + 1) * P, lo:hi], in_=o[:])
 
-        load_x(0)
+        load_pairs()
         nc.sync.dma_start(offs_t[:], offs)
         nc.gpsimd.memset(xs[:].bitcast(I32), 0)
         make_identity(nc, ident[:])
@@ -388,16 +401,18 @@ def tile_moe_pln_mlp_relu2_kernel(
         load_w1e(0, 0, 2)
         load_w1e(1, 1, 1)
         halves(0)
-        cast(0, 0, 256, "v")
-        cast(0, 256, 352, "v")
-        cast(0, 352, T, "s")
+        cast_pair(0, 0, 256, "v")
+        cast_pair(0, 256, T, "s")
+        cast_pair(1, 0, 256, "v")
+        cast_pair(1, 256, 352, "v")
+        cast_pair(1, 352, T, "s")
         quantise(0, 0, 256)
         quantise(0, 256, T)
         words(0, 0, 8, 1408)
         halves(1)
         cast(1, 0, 256, "s")
-        cast(1, 256, 352, "s")
-        cast(1, 352, T, "g")
+        cast(1, 256, 336, "s")
+        cast(1, 336, T, "g")
         quantise(1, 0, 256)
         quantise(1, 256, T)
         first_rows = (hold([P, SLOTS], U8, "gs0_0"), 0)

from contextlib import ExitStack

import concourse.mybir as mybir
from concourse.masks import make_identity

K, T, E, C, H, N = 2048, 512, 4, 256, 512, 384
P = 128
PASSES = K // 512
SLOTS = E * C
FLOPS = 2 * SLOTS * (K * H + H * N)

F32 = mybir.dt.float32
BF16 = mybir.dt.bfloat16
I32 = mybir.dt.int32
U32 = mybir.dt.uint32
U16 = mybir.dt.uint16
U8 = mybir.dt.uint8
FP8X4 = mybir.dt.float8_e4m3fn_x4
FP4X4 = mybir.dt.float4_e2m1fn_x4
RELU = mybir.ActivationFunctionType.Relu
SQUARE = mybir.ActivationFunctionType.Square
COPY = mybir.ActivationFunctionType.Copy
MULT = mybir.AluOpType.mult
ADD = mybir.AluOpType.add
WORDS_AT = (1536, 0, 512, 1024)
XW = 1536 + 1408
PLANE_AT = (0, 0, 1024, 1024)
XS = 1024 + 704
LIFT = (0, 4, 4, 0)
SOURCE = (0, 2, 1, 3)


def tile_moe_pln_mlp_relu2_kernel(
    tc, xT, w1_words, w1_scales, w2_words, w2_scales, gate, offs, pos1, pos2, out
):
    nc = tc.nc
    with ExitStack() as ctx:
        lists = ctx.enter_context(tc.tile_pool(name="lists", bufs=1))
        keep = ctx.enter_context(tc.tile_pool(name="keep", bufs=1))
        psum = ctx.enter_context(tc.psum_pool(name="psum", bufs=1))

        def hold(shape, dtype, name, tag=None):
            return keep.tile(shape, dtype, name=name, tag=tag or name, align_bytes=256)

        def bank(b):
            return psum.tile([P, H], F32, name="bank%d" % b)

        offs_t = lists.tile([P, SLOTS // 16], U16, name="offs_t")
        pos_t = [lists.tile([P, T // 16], U16, name="pos%d_t" % i) for i in range(2)]

        xT_v = xT.rearrange("(s p j) t -> s p j t", p=P, j=4)
        w1w_v = w1_words.bitcast(I32)
        w1s_v = w1_scales.bitcast(I32).rearrange("e s q b -> (e s) q b")
        w2w_v = w2_words.bitcast(I32)
        w2s_v = w2_scales.bitcast(I32)

        raw = {s: hold([P, 4, T], F32, "raw%d" % s) for s in range(1, PASSES)}
        pairs = [hold([P, 2, T], F32, "pair%d" % u) for u in range(2)]
        xb = {}
        xw = hold([P, XW], U32, "xw")
        xs = hold([P, XS], U8, "xs")
        late = {}
        hs = hold([P, SLOTS], U8, "hs")
        y = [hold([P, SLOTS], F32, "y%d" % j) for j in range(N // P)]
        ident = hold([P, P], F32, "ident")
        w2s = hold([P, E * N], U8, "w2s")
        w2w = hold([P, E * 2 * N], U8, "w2w")
        g = hold([P, 2, T], F32, "g")
        gcol = hold([P, T // P], F32, "gcol")
        gw, gs, w1w, w1s, wide = {}, {}, {}, {}, {}

        def load_x(s):
            nc.sync.dma_start(out=raw[s][:], in_=xT_v[SOURCE[s]])

        def load_w1(s, lo, hi):
            words1 = hold([P, (hi - lo) * 2 * H], U8, "w1w%d%d" % (s, lo))
            nc.sync.dma_start(
                out=words1[:].bitcast(I32).rearrange("p (e b) -> p e b", e=hi - lo),
                in_=w1w_v[lo:hi, SOURCE[s]].rearrange("e p b -> p e b"),
            )
            for e in range(lo, hi):
                w1w[s, e] = words1[:, (e - lo) * 2 * H : (e - lo + 1) * 2 * H]

        def load_w1e(e, lo, step):
            passes = range(lo, PASSES, step)
            words1 = hold([P, len(passes) * 2 * H], U8, "w1e%d%d" % (e, lo))
            nc.sync.dma_start(
                out=words1[:].bitcast(I32).rearrange("p (s b) -> p s b", s=len(passes)),
                in_=w1w_v[e, lo:PASSES:step].rearrange("s p b -> p s b"),
            )
            for i, a in enumerate(passes):
                w1w[SOURCE.index(a), e] = words1[:, i * 2 * H : (i + 1) * 2 * H]

        def load_w1_scales(odd):
            plane = hold([P, 2 * E * H], U8, "w1s%d" % odd)
            nc.vector.memset(plane[:, 0 : 2 * H].bitcast(I32), 0)
            for r in range(4):
                nc.sync.dma_start(
                    out=plane[r:P:32, :].bitcast(I32).rearrange("p (a b) -> p a b", b=H // 4),
                    in_=w1s_v[odd : E * PASSES : 2, r:16:4, :].rearrange("a q b -> q a b"),
                )
            for a in range(2 * E):
                w1s[SOURCE.index(2 * (a % 2) + odd), a // 2] = plane[:, a * H : (a + 1) * H]

        def load_w2():
            nc.sync.dma_start(
                out=w2w[:].bitcast(I32).rearrange("p (e b) -> p e b", e=E),
                in_=w2w_v[:, 0].rearrange("e p b -> p e b"),
            )
            for r in range(4):
                nc.sync.dma_start(
                    out=w2s[r:P:32, :].bitcast(I32).rearrange("p (a b) -> p a b", b=N // 4),
                    in_=w2s_v[:, 0, r:16:4, :].rearrange("e q b -> q e b"),
                )

        def load_gate():
            nc.sync.dma_start(out=g[:], in_=gate[:, 0:P, :].rearrange("g p t -> p g t"))
            with nc.allow_non_contiguous_dma(reason="one gate value a partition"):
                nc.sync.dma_start(out=gcol[:], in_=gate[1, P, :].rearrange("(c p) -> p c", p=P))

        def load_pos():
            nc.sync.dma_start(pos_t[0][:], pos1)
            nc.sync.dma_start(pos_t[1][:], pos2)

        def rounded(s, lo, hi):
            half = lo // 256
            return xb[s, half][:, lo - 256 * half : hi - 256 * half, :]

        def cast(s, lo, hi, engine):
            src = raw[s][:, :, lo:hi]
            if engine == "g":
                nc.gpsimd.tensor_copy(rounded(s, lo, hi), src.rearrange("p t c -> p c t"))
                return
            dst = rounded(s, lo, hi).rearrange("p (c i) t -> p c t i", i=4)
            src = src.rearrange("p t (c i) -> p c t i", i=4)
            if engine == "s":
                nc.scalar.copy(dst, src)
            else:
                nc.vector.tensor_copy(dst, src)

        def load_pairs():
            for u in range(2):
                nc.sync.dma_start(out=pairs[u][:], in_=xT_v[SOURCE[0], :, 2 * u : 2 * u + 2, :])

        def cast_pair(u, lo, hi, engine):
            dst = rounded(0, lo, hi)[:, :, 2 * u : 2 * u + 2].rearrange("p (c i) t -> p c i t", i=4)
            src = pairs[u][:, :, lo:hi].rearrange("p t (c i) -> p c i t", i=4)
            if engine == "s":
                nc.scalar.copy(dst, src)
            else:
                nc.vector.tensor_copy(dst, src)

        def halves(s, tag=None):
            xb[s, 0] = hold([P, 256, 4], BF16, "xb%d_0" % s)
            xb[s, 1] = hold([P, 256, 4], BF16, "xb%d_1" % s, tag)

        def quantise(s, lo, hi):
            nc.vector.quantize_mx(
                out=xw[:, WORDS_AT[s] + lo : WORDS_AT[s] + hi].bitcast(FP8X4),
                scales=xs[LIFT[s] : P, PLANE_AT[s] + lo : PLANE_AT[s] + hi],
                in_=rounded(s, lo, hi).rearrange("p c t -> p (c t)"),
            )

        def words(s, lo, hi, reach, tag=None):
            codes = hold([P, (hi - lo) * P], U32, "gw%d_%d" % (s, lo), tag)
            nc.vector.tensor_copy(codes[:], xw[:, WORDS_AT[s] : WORDS_AT[s] + reach].indirect(offs_t[:, lo * 8 : hi * 8]))
            if lo == 0:
                wide[s] = codes[:, 0:C]
            for b in range(lo, hi):
                gw[s, b] = codes[:, (b - lo) * P : (b - lo + 1) * P]

        def scales(passes, lo, hi, reach, rows=None):
            at = PLANE_AT[passes[0]]
            rows, base = rows or (hold([P, (hi - lo) * P], U8, "gs%d_%d" % (passes[0], lo)), lo)
            nc.vector.tensor_copy(rows[:, (lo - base) * P : (hi - base) * P], xs[:, at : at + reach].indirect(offs_t[:, lo * 8 : hi * 8]))
            lo = base
            for s in passes:
                for b in range(lo, hi):
                    gs[s, b] = (rows, lo)

        def lower(s, lo, hi, pieces):
            rows, base = gs[s, lo]
            low = hold([P, (hi - lo) * P], U8, "low%d_%d" % (s, lo))
            cols = slice((lo - base) * P, (hi - base) * P)
            for a, n in pieces:
                nc.sync.dma_start(out=low[a : a + n, :].bitcast(I32), in_=rows[LIFT[s] + a : LIFT[s] + a + n, cols].bitcast(I32))
            for b in range(lo, hi):
                gs[s, b] = (low, lo)

        one = ((0, 112),)
        three = ((0, 4), (32, 64), (96, 4))
        acc, done, relu, turned, hb, sums, terms = {}, {}, {}, {}, {}, {}, {}

        def first(s, blocks):
            for b in blocks:
                done[b] = done.get(b, 0) + 1
                if done[b] == 1:
                    acc[b] = bank(b)
                rows, base = gs[s, b]
                nc.tensor.matmul_mx(
                    out=acc[b][:],
                    lhsT=gw[s, b].bitcast(FP8X4),
                    lhsT_scale=rows[:, (b - base) * P : (b - base + 1) * P],
                    rhs=w1w[s, b // 2].bitcast(FP4X4),
                    rhs_scale=w1s[s, b // 2],
                    start=(done[b] == 1),
                    stop=(done[b] == PASSES),
                )

        def warm(n):
            rows, base = gs[0, 2]
            idle = bank(7)
            for i in range(n):
                nc.tensor.matmul_mx(
                    out=idle[:],
                    lhsT=gw[0, 2].bitcast(FP8X4),
                    lhsT_scale=rows[:, 0:P],
                    rhs=w1w[0, 1].bitcast(FP4X4),
                    rhs_scale=rows[:, 0:H],
                    start=True,
                    stop=True,
                )

        still = {}
        early = hold([P, 3 * P, 4], BF16, "early")
        hbe = {1: early[:, 0:C, :], 2: hold([P, C, 4], BF16, "hbe2"), 3: hold([P, C, 4], BF16, "hbe3")}
        hb[0] = early[:, C : 3 * P, :]
        for b in range(2, 2 * E):
            hb[b] = hbe[b // 2][:, b % 2 * P : (b % 2 + 1) * P, :]

        def deal(s, tag=None):
            codes = hold([P, 2 * H], U8, "dealt%d" % s)
            nc.scalar.copy(
                codes[:].bitcast(U16).rearrange("p (t c i) -> p c t i", t=4, i=8),
                w1w[s, 0].bitcast(U16).rearrange("p (c i t) -> p c t i", t=4, i=8),
            )
            rows = hold([P, H], U8, "dealt_rows%d" % s, tag)
            nc.gpsimd.tensor_copy(rows[:].rearrange("p (t m) -> p t m", t=4), w1s[s, 0].rearrange("p (m t) -> p t m", t=4))
            still[s] = (codes, rows)

        def first_still(s):
            done["still"] = done.get("still", 0) + 1
            codes, rows = still[s]
            token_rows, base = gs[s, 0]
            for t in range(4):
                if done["still"] == 1 and t % 2 == 0:
                    acc[t // 2] = bank(t // 2)
                nc.tensor.matmul_mx(
                    out=acc[t // 2][:, t % 2 * C : (t % 2 + 1) * C],
                    lhsT=codes[:, 2 * t * P : 2 * (t + 1) * P].bitcast(FP4X4),
                    lhsT_scale=rows[:, t * P : (t + 1) * P],
                    rhs=wide[s].bitcast(FP8X4),
                    rhs_scale=token_rows[:, 0:C],
                    start=(done["still"] == 1 and t % 2 == 0),
                    stop=(done["still"] == PASSES and t % 2 == 1),
                )

        def finish_still():
            relu[0] = hold([P, 2, C, 2], F32, "lanes")
            for u in range(2):
                nc.scalar.activation(relu[0][:, u, :, :], acc[u][:].rearrange("p (d n) -> p n d", d=2), RELU)

        def square_still(b, engine):
            if b == 1:
                hb[b] = hold([P, P, 4], BF16, "hb1", "r4")[:, :, :]
            src = relu[0][:, :, b * P : (b + 1) * P, :].rearrange("p u n d -> p n u d")
            dst = hb[b].rearrange("p n (u d) -> p n u d", u=2)
            if engine == "s":
                nc.scalar.activation(dst, src, SQUARE)
            else:
                nc.gpsimd.tensor_tensor(dst, src, src, MULT)

        def rectify(b, engine):
            relu[b] = hold([P, 4, P], F32, "r%d" % b)
            lanes = acc[b][:].rearrange("p (m t) -> p t m", t=4)
            if engine == "v":
                nc.vector.tensor_scalar_max(relu[b][:], lanes, 0.0)
            else:
                nc.scalar.activation(relu[b][:], lanes, RELU)

        def turn(b):
            turned[b] = bank(b)
            for t in range(4):
                nc.tensor.transpose(turned[b][:, t * P : (t + 1) * P], relu[b][:, t, :], ident[:])

        def square(b, engine="s"):
            src = turned[b][:].rearrange("p (t n) -> p n t", t=4)
            if engine == "s":
                nc.scalar.activation(hb[b], src, SQUARE)
            else:
                kept = hold([P, P, 4], F32, "kept%d" % b)
                nc.vector.tensor_copy(kept[:], src)
                nc.vector.tensor_tensor(hb[b], src, kept[:], MULT)

        squared = {}

        def rectify_pairs(b, engine):
            relu[b] = hold([P, 2, P, 2], F32, "r%d" % b)
            lanes = acc[b][:].rearrange("p (m u d) -> p u m d", u=2, d=2)
            if engine == "v":
                nc.vector.tensor_scalar_max(relu[b][:], lanes, 0.0)
            else:
                nc.scalar.activation(relu[b][:], lanes, RELU)

        def square_pairs(b, engine, tag=None):
            squared[b] = hold([P, H], BF16, "sq%d" % b, tag)
            src = relu[b][:].rearrange("p u m d -> p (u m d)")
            if engine == "s":
                nc.scalar.activation(squared[b][:], src, SQUARE)
            elif engine == "v":
                nc.vector.tensor_tensor(squared[b][:], src, src, MULT)
            else:
                nc.gpsimd.tensor_tensor(squared[b][:], src, src, MULT)

        def turn_pairs(b, into, at):
            if at == 0:
                turned["pairs", into] = bank(into)
            turned[b] = turned["pairs", into][:, b % 2 * C : (b % 2 + 1) * C]
            for u in range(2):
                nc.tensor.transpose(turned[b][:, u * P : (u + 1) * P], squared[b][:].bitcast(F32)[:, u * P : (u + 1) * P], ident[:])

        def weave(e, into, engine):
            dst = hbe[e][:, :, :].rearrange("p n t -> p (n t)").bitcast(F32).rearrange("p (b n u) -> p b n u", b=2, u=2)
            src = turned["pairs", into][:].rearrange("p (b u n) -> p b n u", b=2, u=2)
            if engine == "s":
                nc.scalar.copy(dst, src)
            else:
                nc.vector.tensor_copy(dst, src)

        def column(slot):
            return slot if slot >= 2 * C else (slot + C) % (2 * C)

        def hidden(lo, hi):
            base = lo // (2 * C) * 2 * C
            return late[base][:, lo - base : hi - base]

        def quantise_h(lo, hi, src):
            nc.vector.quantize_mx(out=hidden(lo, hi).bitcast(FP8X4), scales=hs[:, lo:hi], in_=src.rearrange("p n t -> p (n t)"))

        def second(j, lo, hi, b, width=C):
            sums[j, lo] = bank(b)
            for at in range(lo, hi, width):
                w = at // C * N + j * P
                nc.tensor.matmul_mx(
                    out=sums[j, lo][:, at - lo : at - lo + width],
                    lhsT=w2w[:, 2 * w : 2 * (w + P)].bitcast(FP4X4),
                    lhsT_scale=w2s[:, w : w + P],
                    rhs=hidden(column(at), column(at) + width).bitcast(FP8X4),
                    rhs_scale=hs[:, column(at) : column(at) + width],
                    start=True,
                    stop=True,
                )

        def fetch(j, lo, hi, engine):
            if engine == "v":
                nc.vector.tensor_copy(y[j][:, lo:hi], sums[j, lo][:, 0 : hi - lo])
            else:
                nc.scalar.copy(y[j][:, lo:hi], sums[j, lo][:, 0 : hi - lo])

        def term(j, i, lo=0, hi=T, tag=None):
            terms[j, i, lo] = hold([P, hi - lo], F32, "term%d%d_%d" % (j, i, lo), tag)
            nc.vector.tensor_tensor(terms[j, i, lo][:], y[j][:].indirect(pos_t[i][:, lo // 16 : hi // 16]), g[:, i, lo:hi], MULT)

        def part(j, i, lo, hi):
            base = max(a for r, c, a in terms if (r, c) == (j, i) and a <= lo)
            return terms[j, i, base][:, lo - base : hi - base]

        def pick(j, lo=0, hi=T, tag=None):
            terms[j, 2, lo] = hold([P, hi - lo], F32, "picked%d_%d" % (j, lo), tag)
            nc.scalar.activation(terms[j, 2, lo][:], y[j][:].indirect(pos_t[1][:, lo // 16 : hi // 16]), COPY)

        def weigh(j, lo, hi, b1, b2):
            n = hi - lo
            across = bank(b1)
            for c in range(n // P):
                nc.tensor.transpose(across[:, c * P : (c + 1) * P], part(j, 2, lo + c * P, lo + (c + 1) * P), ident[:])
            weighed = hold([P, n], F32, "weighed%d_%d" % (j, lo))
            for c in range(n // P):
                at = lo // P + c
                nc.scalar.activation(weighed[:, c * P : (c + 1) * P], across[:, c * P : (c + 1) * P], COPY, scale=gcol[:, at : at + 1])
            back = bank(b2)
            for c in range(n // P):
                nc.tensor.transpose(back[:, c * P : (c + 1) * P], weighed[:, c * P : (c + 1) * P], ident[:])
            terms[j, 1, lo] = back

        def add(j, lo=0, hi=T, queue=None):
            o = hold([P, hi - lo], F32, "o%d_%d" % (j, lo))
            nc.vector.tensor_tensor(o[:], part(j, 1, lo, hi), part(j, 0, lo, hi), ADD)
            (queue or nc.sync).dma_start(out=out[j * P : (j + 1) * P, lo:hi], in_=o[:])

        load_pairs()
        nc.sync.dma_start(offs_t[:], offs)
        nc.gpsimd.memset(xs[:].bitcast(I32), 0)
        make_identity(nc, ident[:])
        load_x(1)
        load_x(2)
        load_x(3)
        load_w1(0, 1, 2)
        load_w1_scales(0)
        load_w1(0, 2, 4)
        load_w1e(0, 0, 2)
        load_w1e(1, 1, 1)
        halves(0)
        cast_pair(0, 0, 256, "v")
        cast_pair(0, 256, T, "s")
        cast_pair(1, 0, 256, "v")
        cast_pair(1, 256, 352, "v")
        cast_pair(1, 352, T, "s")
        quantise(0, 0, 256)
        quantise(0, 256, T)
        words(0, 0, 8, 1408)
        halves(1)
        cast(1, 0, 256, "s")
        cast(1, 256, 336, "s")
        cast(1, 336, T, "g")
        quantise(1, 0, 256)
        quantise(1, 256, T)
        first_rows = (hold([P, SLOTS], U8, "gs0_0"), 0)
        scales((0, 1), 0, 4, 704, first_rows)
        warm(3)
        halves(2, "xb1_1")
        cast(2, 0, 256, "s")
        cast(2, 256, 352, "s")
        cast(2, 352, T, "g")
        quantise(2, 0, 256)
        quantise(2, 256, T)
        halves(3, "xb1_1")
        cast(3, 0, 256, "s")
        cast(3, 256, 320, "s")
        cast(3, 320, T, "g")
        scales((0, 1), 4, 8, 1280, first_rows)
        words(1, 2, 4, 1024)
        lower(1, 0, 8, one)
        load_w1_scales(1)
        load_w1e(0, 1, 2)
        quantise(3, 0, 256)
        words(1, 0, 2, 1280)
        quantise(3, 256, T)
        scales((2, 3), 0, 4, 704)
        lower(2, 0, 4, three)
        load_pos()
        load_w1e(2, 1, 1)
        words(3, 2, 4, T)
        words(2, 0, 4, 1024)
        scales((2, 3), 4, 6, T)
        lower(2, 4, 6, one)
        load_w1e(3, 1, 1)
        words(3, 0, 2, T)
        scales((2, 3), 6, 8, T)
        lower(2, 6, 8, one)
        words(1, 4, 6, 1536)
        words(3, 4, 6, T)
        words(2, 4, 6, 1024)
        words(1, 6, 8, 1536)
        for b in (6, 7):
            words(3, b, b + 1, T)
            words(2, b, b + 1, 1024)
        load_w2()
        load_gate()
        deal(0, "xb1_1")
        deal(1)
        deal(2)
        deal(3)
        first(0, range(2, 8))
        first_still(0)
        first(1, (2, 3))
        first_still(1)
        first(3, (2, 3))
        for b in (2, 3):
            first(2, (b,))
            rectify_pairs(b, "s")
            square_pairs(b, "g")
        first_still(2)
        first_still(3)
        finish_still()
        square_still(0, "s")
        first(1, (4, 5))
        first(3, (4, 5))
        for b in (4, 5):
            first(2, (b,))
            rectify_pairs(b, "s")
        turn_pairs(2, 1, 0)
        turn_pairs(3, 1, 1)
        first(1, (6, 7))
        for b in (6, 7):
            first(3, (b,))
            first(2, (b,))
        square_pairs(4, "g")
        square_pairs(5, "s")
        square_still(1, "g")
        turn_pairs(5, 4, 0)
        turn_pairs(4, 4, 1)
        late[2 * C] = hold([P, 2 * C], U32, "hw", "xw")
        late[0] = hold([P, 2 * C], U32, "hw0", "gw2_7")
        weave(1, 1, "v")
        rectify(6, "s")
        rectify(7, "v")
        quantise_h(0, 384, early[:])
        weave(2, 4, "s")
        for b in (6, 7):
            turn(b)
            square(b)
        quantise_h(512, 768, hbe[2][:])
        quantise_h(384, 512, hb[1])
        second(0, 0, 512, 0)
        second(0, 512, 768, 2)
        quantise_h(768, 896, hb[6])
        second(0, 768, 896, 3, 128)
        quantise_h(896, 1024, hb[7])
        second(0, 896, 1024, 1, 128)
        fetch(0, 0, 512, "s")
        fetch(0, 512, 768, "v")
        fetch(0, 768, 896, "s")
        fetch(0, 896, 1024, "v")
        second(1, 0, 512, 5)
        fetch(1, 0, 512, "s")
        second(1, 512, 1024, 4)
        fetch(1, 512, 1024, "s")
        second(2, 0, 512, 6)
        second(2, 512, 1024, 7)
        term(0, 0)
        fetch(2, 0, 512, "s")
        fetch(2, 512, 1024, "v")
        pick(0)
        pick(2)
        term(1, 0)
        term(1, 1)
        term(2, 0)
        add(1)
        weigh(0, 0, T, 0, 1)
        weigh(2, 0, 256, 3, 4)
        weigh(2, 256, T, 6, 5)
        add(0)
        add(2, 0, 256)
        add(2, 256, T)
